import numpy as np, ml_dtypes
CORES = [10,34,74,98]
N = 4
BF = ml_dtypes.bfloat16
def gentries(a):
    return np.ascontiguousarray(a.reshape(8, 16, -1).transpose(0, 2, 1)).reshape(8, -1)
def gtable(e):
    e = np.asarray(e); return np.ascontiguousarray(e.reshape(8, -1, 16).transpose(0, 2, 1)).reshape(128, -1).astype(np.int32)
W, CELLS, K, RO, TH1, TH2 = 4096, 1024, 256, 4, 256, 600
def world(rng, fam, uneven):
    X = np.zeros((N, 8, W, 16), np.int64)
    for g in range(8):
        P = int(fam[g]); pr = rng.integers(0, 256, (P, 16))
        if uneven: pr = np.floor(rng.random((P, 16)) * np.exp2(8 * rng.random((P, 1)))).astype(np.int64)
        w = rng.integers(0, P, (N, W)); s = rng.choice(np.array([2, 8, 24]), (N, W, 1))
        X[:, g] = np.clip(pr[w] + rng.integers(-24, 25, (N, W, 16)) * s // 24, 0, 255)
    return X
def parts(rng, fam, uneven=False):
    return (world(rng, fam, uneven), rng.integers(0, W, (N, 8, CELLS, 16)), rng.integers(0, CELLS, (N, 8, K)), rng.integers(0, 256, (N, 8, K, 16)),
            rng.integers(0, 256, (N, 8, 16, 16)), rng.integers(0, 256, (N, 8, 16)))
def half(a):
    return np.ascontiguousarray(a).astype(np.float32).astype(BF)
def pack(X, ce, v, z, kp, wv):
    return {"px": half(X.transpose(0, 1, 3, 2).reshape(N, 128, W)), "ce": np.ascontiguousarray(ce.transpose(0, 1, 3, 2).reshape(N, 128, CELLS)).astype(np.int32),
            "v0": np.stack([gtable(a) for a in v]), "z0": half(z.transpose(0, 1, 3, 2).reshape(N, 128, K)), "kap": half(kp.reshape(N, 128, 16)), "wu": half(wv.reshape(N, 128, 1))}
def cut(a):
    return a // 16 + (np.arange(16) < a % 16)
def setup_inputs(rng):
    return pack(*parts(rng, rng.choice(np.array([8, 10, 12, 16]), 8)))
def setup_inputs_spread(rng):
    X, ce, v, z, kp, wv = parts(rng, rng.permutation(np.array([2, 4, 8, 12, 16, 32, 64, 128])), True)
    e = rng.choice(np.array([1.0, 2.0, 6.0]), (N, 8, CELLS, 1)); ce = np.floor(W * rng.random(ce.shape) ** e).astype(np.int64)
    v = np.floor(CELLS * rng.random(v.shape) ** 3).astype(np.int64)
    z = np.floor(rng.random(z.shape) * np.exp2(8 * rng.random((N, 8, K, 1)))).astype(np.int64)
    kp = np.floor(256 * rng.random(kp.shape) ** rng.choice(np.array([0.5, 1.0, 4.0]), (N, 8, 1, 16))).astype(np.int64)
    wv = np.floor(256 * rng.random(wv.shape) ** 2).astype(np.int64)
    return pack(X, ce, v, z, kp, wv)
def setup_inputs_ends(rng):
    def mix(n):
        return np.where(rng.random((N, 8, n, 1)) < 0.5, 255 * rng.integers(0, 2, (N, 8, n, 16)), 255 * rng.integers(0, 2, (N, 8, n, 1)))
    i = np.arange(16); R = 255 * (i < 9)
    X = mix(W); X[:, :, W - 1] = 255; X[:, :, 0] = 0; X[:, 3, 0] = 255
    X[:, 7, W - 1] = R; X[:, 7, 0] = 255 * (i < 4); X[:, 7, W - 2] = 255
    kind = rng.integers(0, 6, (N, 8, CELLS, 1)); slot = rng.integers(0, 16, (N, 8, CELLS, 1)); coin = rng.integers(0, 2, (N, 8, CELLS, 16))
    on = np.where(kind == 0, 0, np.where(kind == 1, i == slot, np.where(kind == 2, (i == 0) | (i == 15), np.where(kind == 3, 1, coin))))
    ce = (W - 1) * on.astype(np.int64)
    ce = np.where((kind == 5) & (rng.random(ce.shape) < 0.5), rng.integers(0, W, ce.shape), ce)
    ce[:, 7, CELLS - 1] = 0; ce[:, 7, CELLS - 1, 15] = W - 1; ce[:, 7, 0] = 0; ce[:, 7, 0, 14:] = W - 2
    v = np.where(rng.random((N, 8, K)) < 0.8, (CELLS - 1) * rng.integers(0, 2, (N, 8, K)), rng.integers(0, CELLS, (N, 8, K)))
    v[:, :, 0] = 0; v[:, :, K - 1] = CELLS - 1; v[:, 7, K - 2] = 0
    z = mix(K); z[:, 6] = np.where(rng.random((N, K, 1)) < 0.8, 255, z[:, 6]); z[:, 7, K - 2:] = 255; z[:, :, K - 1] = 255
    kp = np.where(rng.random((N, 8, 16, 16)) < 0.15, rng.integers(0, 256, (N, 8, 16, 16)), 255 * rng.integers(0, 2, (N, 8, 16, 16)))
    wv = np.where(rng.random((N, 8, 16)) < 0.15, rng.integers(0, 256, (N, 8, 16)), 255 * rng.integers(0, 2, (N, 8, 16)))
    kp[:, 6] = 255; wv[:, 6] = 255
    last = np.where(i == 0, 255, np.where(i == 1, 2, 0))
    wv[:, 7] = np.where(i < 9, last, wv[:, 7]); kp[:, 7, :, 15] = np.where(i < 9, last, kp[:, 7, :, 15])
    ce[:, 4, CELLS - 1] = 0; ce[:, 4, 0] = i + 1
    X[:, 4, 1] = 255 * (i < 2); X[:, 4, 2:17] = 255 * (i >= 2)
    ce[:, 5, CELLS - 1] = (W - 1) * (i == 0); ce[:, 5, 0] = (W - 1) * (i == 0); wv[:, 5] = last
    kp[:, 5] = 255 * (kp[:, 5] > 127); X[:, 5, (65025 * np.arange(17)) & (W - 1)] = 0
    ce[:, 2, CELLS - 1] = np.where(i < 15, 1 + i % 10, W - 1); ce[:, 2, CELLS - 256] = 0; wv[:, 2] = last
    X[:, 2, 1:11] = 255; X[:, 2, 1:11, 0] = 254 - np.arange(10)
    return pack(X, ce, v, z, kp, wv)
def setup_inputs_corners(rng):
    X, ce, v, z, kp, wv = parts(rng, np.full(8, 12)); T = 64
    X = np.where(rng.random(X.shape) < 0.5, rng.integers(100, 128, X.shape), rng.integers(0, 21, X.shape))
    for g in range(8):
        ba = rng.integers(128, 224, (T, 16))
        for r in range(N):
            pl = (ba @ kp[r, g]) & (W - 1); cl = (ba @ wv[r, g]) & (CELLS - 1)
            own = rng.permutation(np.setdiff1d(np.arange(W), pl))[:5 * T].reshape(5, T)
            X[r, g, own[0]] = ba
            for i in range(1, 4): X[r, g, own[i]] = ba - cut(TH1 - 2 + i)
            st = rng.permutation(np.setdiff1d(np.arange(CELLS), cl))[:T]; ce[r, g, st, rng.integers(0, 16, T)] = own[0]
            for t in range(T):
                qs = rng.permutation(16); am = int(rng.choice(np.array([0, TH2 - 1, TH2, TH2 + 1])))
                X[r, g, pl[t, qs[1]]] = ba[t] - cut(am + int(rng.integers(0, 2))); X[r, g, pl[t, qs[0]]] = ba[t] - cut(am)
                n = int(rng.choice(np.array([0, 1, 1, 2, 2, 3, 15, 16])))
                ce[r, g, cl[t]] = rng.permutation(np.concatenate([own[rng.integers(0, 2, n), t], own[rng.integers(2, 5, 16 - n), t]]))
            tl = rng.permutation(np.arange(K) % T); v[r, g] = st[tl]; z[r, g] = ba[tl]
    return pack(X, ce, v, z, kp, wv)
def setup_inputs_crowd(rng):
    fam = np.full(8, 10); fam[4] = 1
    X, ce, v, z, kp, wv = parts(rng, fam); X[:, 5] = rng.integers(0, 256, (N, W, 16))
    for g in (0, 1, 4, 5):
        v[:, g] = v[:, g, :1].copy(); z[:, g] = z[:, g, :1].copy()
    for g in (1, 5):
        for r in range(N):
            o = int(rng.choice(np.array([0, K - 1, int(rng.integers(0, K))])))
            v[r, g, o] = (v[r, g, o] + 1 + int(rng.integers(0, CELLS - 1))) % CELLS; z[r, g, o] = rng.integers(0, 256, 16)
    wv[:, 2] = 0; kp[:, 2] = 0; kp[:, 6] = 0; v[:, 3] = v[:, 3, :1].copy()
    return pack(X, ce, v, z, kp, wv)
def setup_inputs_ties(rng):
    X, ce, v, z, kp, wv = parts(rng, np.full(8, 12)); val = np.array([0, 64, 128, 255])
    for g in range(8):
        a = rng.choice(val, (12, 16)); b = rng.choice(val, (6, 8))
        pool = np.concatenate([a, a[:, ::-1], np.concatenate([b, b[:, ::-1]], axis=1)])
        X[:, g] = pool[rng.integers(0, 30, (N, W))]
    h = rng.choice(val, (N, 8, K, 8)); z = np.concatenate([h, h[..., ::-1]], axis=3)
    return pack(X, ce, v, z, kp, wv)
def check_inputs(d):
    bad = []
    for k, hi in (("px", 255), ("ce", W - 1), ("v0", CELLS - 1), ("z0", 255), ("kap", 255), ("wu", 255)):
        a = np.asarray(d[k]).astype(np.float64)
        if not (np.min(a) >= 0 and np.max(a) <= hi): bad.append("range of " + k)
        elif not np.all(a == np.floor(a)): bad.append("whole numbers in " + k)
    return bad
def ints(a):
    return a.astype(np.float32).astype(np.int64)
def first(key):
    w = np.zeros(key.shape, bool)
    for g in range(8): w[g, np.unique(key[g], return_index=True)[1]] = True
    return w
def one(a, k):
    return np.take_along_axis(a, k.reshape(8, K, *([1] * (a.ndim - 2))), 2)[:, :, 0]
def reference(px, ce, v0, z0, kap, wu):
    X = ints(px).reshape(N, 8, 16, W).transpose(0, 1, 3, 2).copy()
    C = ce.astype(np.int64).reshape(N, 8, 16, CELLS).transpose(0, 1, 3, 2).copy()
    kp = ints(kap).reshape(N, 8, 16, 16); wv = ints(wu).reshape(N, 8, 16)
    v = [gentries(a).astype(np.int64) for a in v0]; z = [a for a in ints(z0).reshape(N, 8, 16, K).transpose(0, 1, 3, 2)]
    al = [np.zeros((8, K), np.int64) for p in range(N)]
    g2 = np.arange(8)[:, None]; g3 = g2[:, :, None]; lane = np.arange(K)[None, :] + np.zeros((8, 1), np.int64)
    for t in range(RO):
        hx = []; hn = []
        for p in range(N):
            L = C[p][g2, v[p]]; x = X[p][g3, L]
            k = np.argmax(np.add.reduce(np.minimum(x, z[p][:, :, None, :]), axis=3), axis=2)
            hx.append(one(x, k)); hn.append(one(L, k))
        nv = []; nz = []; na = []; F = []; nm = []; live = []
        for p in range(N):
            o = (p - 1) % N; x = hx[o]; zz = z[o]; a = al[o]
            b = np.add.reduce(wv[p][:, None, :] * x, axis=2) & (CELLS - 1)
            M = C[p][g2, b]; y = X[p][g3, M]
            d = np.add.reduce(np.abs(y - x[:, :, None, :]), axis=3); j = np.argmin(d, axis=2)
            ex = np.add.reduce((d < TH1).astype(np.int64), axis=2) >= 2 + (a & 1)
            s = np.add.reduce(np.minimum(y, x[:, :, None, :]), axis=3); np.put_along_axis(s, j[:, :, None], -1, 2); m = np.argmax(s, axis=2)
            yj = one(y, j); Mj = one(M, j)
            F.append(np.maximum(x, one(y, m))); nm.append(one(M, m)); live.append(~ex)
            win = first(np.where(ex, Mj, W + b)); new = (yj + x) >> 1
            g, l = np.nonzero(win & ex); X[p][g, Mj[g, l]] = new[g, l]
            g, l = np.nonzero(win & ~ex); C[p][g, b[g, l], j[g, l]] = hn[o][g, l]
            nz.append(np.where(ex[:, :, None], np.abs(zz - yj), zz)); na.append(a + ex); nv.append(b)
        for p in range(N):
            o = (p - 1) % N; f = F[o]; on = live[o]
            c = (f @ kp[p]) & (W - 1); w = X[p][g3, c]
            d = np.add.reduce(np.abs(w - f[:, :, None, :]), axis=3); q = np.argmin(d, axis=2)
            rec = one(d, q) < TH2; cq = one(c, q); wq = one(w, q); cc = cq & (CELLS - 1)
            win = first(np.where(on, np.where(rec, cq, W + cc), -1 - lane)) & on; new = (wq + f) >> 1
            g, l = np.nonzero(win & rec); X[p][g, cq[g, l]] = new[g, l]
            g, l = np.nonzero(win & ~rec); C[p][g, cc[g, l], q[g, l]] = nm[o][g, l]
            nz[o] = np.where(on[:, :, None], (nz[o] + wq) >> 1, nz[o])
        v = nv; z = nz; al = na
    return {"yx": X.transpose(0, 1, 3, 2).reshape(N, 128, W).astype(np.float32).astype(BF), "yc": C.transpose(0, 1, 3, 2).reshape(N, 128, CELLS).astype(np.float32),
            "yz": np.stack(z).transpose(0, 1, 3, 2).reshape(N, 128, K).astype(np.float32).astype(BF), "yv": np.stack([gtable(a) for a in v]).astype(np.float32), "ya": np.stack(al).astype(np.float32)}

@@ -1,0 +1,489 @@
+from concourse.mybir import AluOpType, ActivationFunctionType
+ALU = AluOpType
+AF = ActivationFunctionType
+
+N, W, CELLS, K, RO, TH1, TH2 = 4, 4096, 1024, 256, 4, 256, 600
+TBW = W + CELLS + K
+M1 = 1.5 * 2.0 ** 23
+M4096 = 1.5 * 2.0 ** 35
+HALF = 0.5 - 2.0 ** -12
+ZW, LW = 304, 272
+
+
+def _s(cols, dtype):
+    return ("sbuf", [128, cols], dtype)
+
+
+BF, F32, I32, U16 = "bfloat16", "float32", "int32", "uint16"
+SCRATCH = {
+    "TB": _s(TBW, F32), "PXB": _s(W, BF), "CE": _s(CELLS, I32), "IDT": _s(TBW, F32), "NP": _s(16, BF),
+    "OH": _s(W, BF), "Y": _s(W, BF), "MN": _s(W, BF), "E": ("sbuf", [128, 16, 272], BF),
+    "vi": _s(16, I32), "vf": _s(16, F32), "VX": _s(128, F32), "kp": _s(16, BF), "wv": _s(8, BF), "KB": _s(128, BF),
+    "pi": _s(16, I32), "pj": _s(16, I32), "col": _s(16, F32), "ioa": _s(256, F32), "iok": _s(256, F32),
+    "W1": _s(144, BF), "W4": _s(144, BF), "W8": _s(144, BF), "W4n": _s(144, BF), "Wu": _s(144, BF),
+    "GO": _s(128, BF), "GO32": _s(128, F32), "G8k": _s(128, BF), "TRI": _s(128, BF), "tri0": _s(128, BF),
+    "I1": _s(128, BF), "I2": _s(128, BF), "I2n": _s(128, BF), "I8k": _s(128, BF), "I8n": _s(128, BF), "I1n": _s(128, BF),
+    "OH32": _s(16, F32), "NM": _s(256, BF), "m0": _s(256, BF), "JH": _s(256, BF), "JL": _s(256, BF),
+    "DA": _s(256, F32), "DAn": _s(256, F32), "c15": _s(16, U16), "cl": _s(16, F32), "dm": _s(16, F32), "hc": _s(32, F32),
+    "CC": _s(512, BF), "C2k": _s(256, BF), "nu": _s(16, U16), "Lc": _s(256, F32), "ai": _s(16, I32), "aj": _s(16, I32),
+    "bl": _s(32 * (RO + 1), U16), "bi": _s(32, I32), "bj": _s(32, I32), "bb": _s(16, F32), "yvf": _s(16, F32),
+    "Lu": _s(256, U16), "Lf": _s(256, F32), "SX": _s(128, F32), "A3": _s(256, F32), "nk": _s(256, F32),
+    "SC": _s(512, F32), "ne": _s(256, BF), "ks": _s(256, F32), "sg": _s(256, BF), "cs": _s(256, F32),
+    "oi": _s(32, I32), "oj": _s(32, I32), "off": _s(32, U16), "MS": _s(256, F32), "s2": _s(256, F32),
+    "thr": _s(16, F32), "t1": _s(16, F32), "t2": _s(16, F32), "keyL": _s(16, F32), "ku": _s(16, U16), "kr": _s(256, U16),
+    "nr": _s(16, F32), "nr0": _s(16, F32), "dv": _s(16, F32), "qi": _s(16, I32), "qj": _s(16, I32),
+    "oh": _s(256, BF), "OLD": _s(256, F32), "Ob2": _s(256, BF), "Ob3": _s(256, BF), "NP3": _s(256, BF),
+    "a1": _s(256, F32), "Ap": _s(256, F32), "Q": _s(256, F32), "T2": _s(256, F32), "fo": _s(16, U16),
+    "hi": _s(256, BF), "E12": _s(512, BF), "au": _s(16, U16), "ar": _s(256, F32),
+    "zs": _s(ZW * (RO + 1), BF), "xs": _s(K * RO, BF), "ns": _s(K * RO, F32), "fs": _s(K * RO, BF),
+    "ms": _s(K * RO, F32), "ls": _s(LW * RO, BF), "ws": _s(K * RO, BF),
+    "zr": _s(ZW * RO, BF), "xr": _s(K * RO, BF), "nq": _s(K * RO, F32), "fr": _s(K * RO, BF),
+    "mr": _s(K * RO, F32), "lr": _s(LW * RO, BF), "wr": _s(K * RO, BF),
+}
+for _b in ("pX", "pK", "pA", "pS", "pT", "pR", "pZ", "pU"):
+    SCRATCH[_b] = ("psum", [128, 512], F32)
+MSGS = ("z", "x", "n", "f", "m", "l", "w")
+SEMAPHORES = (["cV", "cA", "cP", "cG", "sent", "dv0", "dce", "dz", "dpx", "dw", "outs", "outg"]
+              + ["r%s%d" % (m, t) for m in MSGS for t in range(RO)])
+
+
+def rank_program(g, core, T, topo):
+    rank = T.rank_of(core)
+    if rank is None:
+        return
+    nxt, prv = T.cores[(rank + 1) % N], T.cores[(rank - 1) % N]
+    assert topo.may_write(core, nxt) and topo.may_write(core, prv)
+    V, A, P, S = g.vector, g.scalar, g.tensor, g.sync
+    Q = {"V": V, "A": A, "P": P, "G": g, "S": S}
+    cnt = {"cV": 0, "cA": 0, "cP": 0, "cG": 0, "sent": 0, "outs": 0, "outg": 0}
+    seen = {e: {} for e in Q}
+    wrote, readers = {}, {}
+
+    def need(e, dep):
+        if seen[e].get(dep[0], 0) < dep[1]:
+            Q[e].wait_ge(T.sem[dep[0]], dep[1])
+            seen[e][dep[0]] = dep[1]
+
+    def deps(e, R, Wr):
+        own, ds = "c" + e, {}
+        for t in R:
+            c = [wrote[t]] if t in wrote else []
+            if t[0] == "p" and t[1].isupper():
+                c += [d for d in readers.get(t, []) if d[0] != own]
+            for d in c:
+                ds[d[0]] = max(ds.get(d[0], 0), d[1])
+        for t in Wr:
+            for d in ([wrote[t]] if t in wrote else []) + readers.get(t, []):
+                ds[d[0]] = max(ds.get(d[0], 0), d[1])
+        for s in sorted(ds):
+            if not (e == "P" and s == own):
+                need(e, (s, ds[s]))
+
+    def op(e, fn, R, Wr):
+        deps(e, R, Wr)
+        fn().then_inc(T.sem["c" + e], 1)
+        cnt["c" + e] += 1
+        me = ("c" + e, cnt["c" + e])
+        for t in R:
+            readers.setdefault(t, []).append(me)
+        for t in Wr:
+            wrote[t] = me
+            readers[t] = []
+
+    def tt(out, a, b, alu, R, Wr):
+        op("V", lambda: V.tensor_tensor(out, a, b, alu), R, Wr)
+
+    def ts(out, a, s1, s2, o0, o1, R, Wr):
+        if o1 is None:
+            op("V", lambda: V.tensor_scalar(out, a, s1, None, o0), R, Wr)
+        else:
+            op("V", lambda: V.tensor_scalar(out, a, s1, s2, o0, o1), R, Wr)
+
+    def cp(out, a, R, Wr):
+        op("V", lambda: V.tensor_copy(out, a), R, Wr)
+
+    def fill(ap, c, tok):
+        op("V", lambda: V.memset(ap, c), [], [tok])
+
+    def scan(out, d1, o1, R, Wr):
+        op("V", lambda: V.tensor_tensor_scan(out, T.m0[:, :], d1, 0.0, ALU.mult, o1), R + ["m0"], Wr)
+
+    def act(out, a, R, Wr, f=AF.Identity, bias=0.0, scale=1.0):
+        op("A", lambda: A.activation(out, a, f, bias=bias, scale=scale), R, Wr)
+
+    def mm(lst, R, Wr):
+        def fn():
+            for m in lst:
+                i = P.matmul(m[0], m[1], m[2], m[3], m[4])
+            return i
+        op("P", fn, R, Wr)
+
+    def group(out, terms, start=True, stop=True):
+        n = len(terms)
+        return [(out, l, r, start and i == 0, stop and i == n - 1) for i, (l, r) in enumerate(terms)]
+
+    def send(m, t, src, dst, to, R):
+        deps("G", R, [])
+        rid, pid = topo.addr(to)[0:2]
+        g.remote_dma(dst, src, T.sem["r%s%d" % (m, t)], T.sem.sent, pid, rid, topo.mask(core, to))
+        cnt["sent"] += len(topo.engines(core, to))
+
+    for t in range(RO):
+        for m in MSGS:
+            wrote["r%s%d" % (m, t)] = ("r%s%d" % (m, t), len(topo.engines(nxt if m == "w" else prv, core)))
+
+    def sl(buf, t, w=K, a=0, b=None):
+        return buf[:, t * w + a: t * w + (w if b is None else b)]
+
+    def st(buf, t, r):
+        return buf[:, t * K + r:(t + 1) * K:16]
+
+    YT = ["Y0", "Y1", "Y2", "Y3"]
+    cells = T.TB[:, W:W + CELLS]
+    whole = T.TB[:, 0:TBW]
+
+    S.dma_start(T.vi[:, :], T.v0[:, :]).then_inc(T.sem.dv0, 16)
+    S.dma_start(T.CE[:, :], T.ce[:, :]).then_inc(T.sem.dce, 16)
+    A.dma_start(T.zs[:, 0:K], T.z0[:, :]).then_inc(T.sem.dz, 16)
+    A.dma_start(T.PXB[:, 0:W // 2], T.px[:, 0:W // 2]).then_inc(T.sem.dpx, 16)
+    S.dma_start(T.PXB[:, W // 2:W], T.px[:, W // 2:W]).then_inc(T.sem.dpx, 16)
+    wrote.update({"vi": ("dv0", 16), "CE": ("dce", 16), "z0": ("dz", 16), "PXB": ("dpx", 32), "kw": ("dw", 32)})
+
+    ioc = T.IDT[:, 0:256]
+
+    def iota(out, pattern, base, tok):
+        op("G", lambda: g.iota(out, pattern, base, 0, allow_small_or_imprecise_dtypes=True), [], [tok])
+
+    op("G", lambda: g.iota(T.pi[:, :], [[0, 16]], 0, 1), [], ["pi"])
+    iota(ioc, [[1, 256]], 0, "ioc")
+    iota(T.ioa[:, :], [[1, 16], [0, 16]], 0, "ioa")
+    iota(T.iok[:, :], [[0, 16], [1, 16]], 0, "iok")
+    iota(T.JL[:, :], [[0, 16], [-1, 16]], 15, "JL")
+    g.dma_start(T.kp[:, :], T.kap[:, :]).then_inc(T.sem.dw, 16)
+    g.dma_start(T.wv[:, 0:1], T.wu[:, :], allow_slow_non_contiguous=True).then_inc(T.sem.dw, 16)
+    pc, rc, gc_, wc, jc, lc = [T.col[:, i:i + 1] for i in range(6)]
+    fill(T.zs[:, K:K + 16], -1.0, "za0")
+    fill(T.zs[:, K + 16:K + 32], 0.0, "zb0")
+    fill(T.zs[:, K + 32:K + 48], 1.0, "zc0")
+    ts(T.pj[:, 0:1], T.pi[:, 0:1], 15, None, ALU.bitwise_and, None, ["pi"], ["pj0"])
+    ts(T.pj[:, 1:2], T.pi[:, 0:1], 4, None, ALU.arith_shift_right, None, ["pi"], ["pj1"])
+    cp(pc, T.pi[:, 0:1], ["pi"], ["pc"])
+    cp(T.col[:, 1:3], T.pj[:, 0:2], ["pj0", "pj1"], ["rg"])
+    cp(T.vf[:, :], T.vi[:, :], ["vi"], ["vf"])
+    ts(wc, gc_, 16.0, 15.0, ALU.mult, ALU.add, ["rg"], ["wc"])
+    ts(jc, rc, -256.0, 4080.0, ALU.mult, ALU.add, ["rg"], ["jc"])
+    ts(lc, rc, 1024.0, None, ALU.add, None, ["rg"], ["lc"])
+    ts(T.GO32[:, :], T.ioa[:, 0:128], gc_, None, ALU.is_equal, None, ["ioa", "rg"], ["GO32"])
+    ts(T.OH32[:, :], T.iok[:, 0:16], rc, None, ALU.is_equal, None, ["iok", "rg"], ["OH32"])
+    cp(T.bl[:, 16:32], T.vi[:, :], ["vi"], ["blA0"])
+
+    def blocks(out, src):
+        for q in range(8):
+            i = V.tensor_tensor(out[:, 16 * q:16 * q + 16], src, T.GO32[:, 16 * q:16 * q + 16], ALU.mult)
+        return i
+    op("V", lambda: blocks(T.VX, T.vf[:, :]), ["vf", "GO32"], ["VX"])
+    mm(group(T.pS[:, 0:16], [(T.VX[:, :], T.OH32[:, :])]), ["VX", "OH32"], ["pS"])
+    ts(T.I1[:, :], ioc[:, 0:128], pc, None, ALU.is_equal, None, ["ioc", "pc"], ["I1"])
+    ts(T.W4[:, :], ioc[:, 0:144], wc, 4096.0, ALU.is_equal, ALU.mult, ["ioc", "wc"], ["W4"])
+    ts(T.JH[:, :], T.ioa[:, :], -16.0, jc, ALU.mult, ALU.add, ["ioa", "jc"], ["JH"])
+    ts(T.m0[:, :], T.iok[:, :], 0.0, None, ALU.is_gt, None, ["iok"], ["m0"])
+    cp(T.bl[:, 0:16], T.pS[:, 0:16], ["pS"], ["blB0"])
+    ts(T.OH[:, 0:256], T.iok[:, :], rc, None, ALU.is_equal, None, ["iok", "rg"], ["OH"])
+    for w in (256, 512, 1024):
+        cp(T.OH[:, w:2 * w], T.OH[:, 0:w], ["OH"], ["OH"])
+    cp(cells, T.CE[:, :], ["CE"], ["TB"])
+
+    def names(t):
+        for h in range(2):
+            cp(T.Lu[:, 128 * h:128 * h + 128], cells.indirect(T.bl[:, 32 * t + 8 * h:32 * t + 8 * h + 8]),
+               ["TB", "blB%d" % t], ["Lu%d" % h])
+    names(0)
+    cp(T.OH[:, 2048:W], T.OH[:, 0:2048], ["OH"], ["OH"])
+    tok = "ioc"
+    for w in (256, 512, 1024, 2048):
+        act(T.IDT[:, w:2 * w], T.IDT[:, 0:w], ["ioc", tok], ["IDT%d" % w], bias=float(w))
+        tok = "IDT%d" % w
+    act(T.IDT[:, W:TBW], T.IDT[:, 0:TBW - W], [tok], ["IDT"], bias=float(W))
+
+    def late_constants():
+        ts(T.W1[:, :], T.W4[:, :], 2.0 ** -12, None, ALU.mult, None, ["W4"], ["W1"])
+        ts(T.Wu[:, :], T.W1[:, :], T.wv[:, 0:1], None, ALU.mult, None, ["W1", "kw"], ["Wu"])
+        ts(T.DA[0:32, :], T.ioa[0:32, :], T.col[0:32, 0:1], 4096.0, ALU.is_equal, ALU.mult, ["ioa", "pc"], ["DA"])
+        ts(T.NM[:, :], T.OH[:, 0:256], -1.0, 2.0 ** 22, ALU.add, ALU.mult, ["OH"], ["NM"])
+        fill(T.hc[:, 0:16], 1.0, "hca")
+        fill(T.hc[:, 16:32], 0.5, "hcb")
+        ts(T.tri0[:, :], ioc[:, 0:128], pc, 8192.0, ALU.is_gt, ALU.mult, ["ioc", "pc"], ["tri0"])
+        ts(T.c15[:, :], ioc[:, 0:16], 16.0, 15.0, ALU.mult, ALU.add, ["ioc"], ["c15"])
+        ts(T.cl[:, :], ioc[:, 0:16], 16.0, lc, ALU.mult, ALU.add, ["ioc", "lc"], ["cl"])
+        cp(T.NP[:, :], ioc[:, 0:16], ["ioc"], ["NP"])
+        tt(T.TRI[:, :], T.tri0[:, :], T.GO32[:, :], ALU.mult, ["tri0", "GO32"], ["TRI"])
+        ts(T.dm[:, :], T.cl[:, :], 4096.0, None, ALU.add, None, ["cl"], ["dm"])
+        op("V", lambda: blocks(T.KB, T.kp[:, :]), ["kw", "GO32"], ["KB"])
+        for name, src, c in (("I2", "I1", 2.0), ("GO", "GO32", 1.0), ("W8", "W4", 2.0), ("I8n", "I1", -8192.0),
+                             ("I8k", "I1", 8192.0), ("G8k", "GO32", 8192.0), ("I2n", "I1", -2.0), ("I1n", "I1", -1.0),
+                             ("W4n", "W4", -1.0)):
+            act(T[name][:, :], T[src][:, :], [src], [name], scale=c)
+        act(T.DAn[0:32, :], T.DA[0:32, :], ["DA"], ["DAn"], scale=-1.0)
+
+    def wr_(buf, r):
+        return buf[:, 15 - r:143 - r]
+
+    def spread(src, t, w, tok):
+        mm([(T.pX[:, 16 * r:16 * r + 16], T.I1[:, :], src[:, t * w + r:t * w + K:16], True, True) for r in range(16)],
+           [tok, "I1"], ["pX"])
+
+    def sums(src, t, tok):
+        mm([(T.pT[0:16, r:128:16], st(src, t, r), T.GO[:, 0:128:16], True, True) for r in range(16)], [tok, "GO"], ["pT"])
+        act(T.SX[0:16, :], T.pT[0:16, 0:128], ["pT"], ["SX"], bias=-4080.0)
+
+    def values_start(names, ntok):
+        mm([(T.pU[:, :], T.I8n[:, :], T.CC[:, :], True, False), (T.pU[:, 0:K], T.GO32[:, :], names, False, False)],
+           [ntok, "GO32", "I8n", "CC"], ["pU"])
+
+    def big(win, wtok, ybank, yw, mw, after_y=None):
+        cp(T.Y[:, 0:1024], win.indirect(T.Lu[:, 0:64]), [wtok, "Lu0"], ["Y0"])
+        for c in (1, 2, 3):
+            act(T.Y[:, 1024 * c:1024 * c + 1024], win.indirect(T.Lu[:, 64 * c:64 * c + 64]), [wtok, "Lu%d" % (c // 2)], [YT[c]])
+
+        def mins(c):
+            def fn():
+                for k in range(16):
+                    a, b = 1024 * c + k, 1024 * c + 1024
+                    i = V.tensor_tensor(T.MN[:, a:b:16], T.Y[:, a:b:16], T.pX[:, 64 * c:64 * c + 64], ALU.min)
+                return i
+            op("V", fn, [YT[c], "pX"], ["M%d" % c])
+
+        def red(c, src, bank, wn, tok, stop):
+            mm([(T[bank][:, 0:K], wr_(T[wn], r), src[:, 256 * r:256 * r + 256], False, stop and r == 15)
+                for r in range(4 * c, 4 * c + 4)], [tok, wn], [bank])
+        for c in range(4):
+            mins(c)
+        for kind, c in (("y", 0), ("y", 1), ("m", 0), ("y", 2), ("m", 1), ("m", 2), ("y", 3), ("m", 3)):
+            if kind == "m":
+                red(c, T.MN, "pK", mw, "M%d" % c, True)
+            elif ybank is not None:
+                red(c, T.Y, ybank, yw, YT[c], ybank != "pK")
+                if c == 3 and after_y is not None:
+                    after_y()
+
+    def offsets(n, two):
+        src = T.SC[:, 15:16 * n:16]
+        if two:
+            tt(T.oi[:, 0:n], src, T.hc[:, 0:n], ALU.mult, ["SC0", "SC1", "hca", "hcb"], ["oi"])
+        else:
+            cp(T.oi[:, 0:n], src, ["SC0"], ["oi"])
+        ts(T.oj[:, 0:n], T.oi[:, 0:n], 4095, None, ALU.bitwise_and, None, ["oi"], ["oj"])
+        ts(T.off[:, 0:n], T.oj[:, 0:n], -1.0, 4095.0, ALU.mult, ALU.add, ["oj"], ["off"])
+
+    offj = T.off[:, 0:16]
+    ohw = T.OH[:, 0:W]
+
+    def name_row(names, tok):
+        mm(group(T.pR[:, 0:K], [(T.I1[:, :], T.NM[:, :])], stop=False), ["I1", "NM"], ["pR"])
+        tt(T.MS[:, :], ohw.indirect(offj), names[:, :], ALU.mult, ["OH", "off", tok], ["MS"])
+        act(T.oh[:, :], ohw.indirect(offj), ["OH", "off"], ["oh"])
+        mm(group(T.pR[:, 0:K], [(T.GO32[:, :], T.MS[:, :])], start=False), ["GO32", "MS"], ["pR"])
+
+    def kind_row(rec, rtok, npb, nptok, made):
+        if not made:
+            act(npb, T.NP[:, 0:16].indirect(T.nu[:, :]), ["NP", "nu"], [nptok])
+        mm([(T.pU[:, 0:K], T.I8k[:, :], T.oh[:, :], False, False), (T.pU[:, K:2 * K], T.I8k[:, :], T.oh[:, :], False, False),
+            (T.pU[:, 0:K], T.I8k[:, :], npb, False, False), (T.pU[:, K:2 * K], T.I8n[:, :], npb, False, True)]
+           + group(T.pA[:, 0:K], [(T.I1[:, :], rec), (T.I8n[:, :], npb)], stop=False),
+           [nptok, "oh", "I8k", "I8n", rtok], ["pU", "pA"])
+
+    def write(shift, lim, ltok, ob, otok, between):
+        ts(T.ku[:, :], T.keyL[:, :], shift, None, ALU.add, None, ["keyL"], ["ku"])
+        ku = T.ku[:, :]
+        act(ob, whole.indirect(ku), ["TB", "TBd", "ku"], [otok])
+        act(T.OLD[:, :], whole.indirect(ku), ["TB", "TBd", "ku"], ["OLD"])
+        cp(T.kr[:, :], T.IDT[:, 0:TBW].indirect(ku), ["IDT", "ku"], ["kr"])
+        mm(group(T.pR[:, 0:K], [(T.I1[:, :], T.NM[:, :])], stop=False), ["I1", "NM"], ["pR"])
+        mm(group(T.pA[:, 0:K], [(T.I1[:, :], ob)], start=False), [otok], ["pA"])
+        act(T.a1[:, :], T.pA[:, 0:K], ["pA"], ["a1"], bias=M1, scale=HALF)
+        act(T.Ap[:, :], T.a1[:, :], ["a1"], ["Ap"], bias=-M1)
+        cuts = (0, 1, 3, 5, 8, 12, 16)
+        for h in range(6):
+            def fn():
+                for a in range(cuts[h], cuts[h + 1]):
+                    i = V.tensor_scalar(T.E[:, a, 0:K - 16 * a], T.kr[:, 16 * a:K], T.keyL[:, a:a + 1], shift,
+                                        ALU.subtract, ALU.is_equal)
+                return i
+            op("V", fn, ["kr", "keyL"], ["E%d" % h])
+            lst = [(T.pR[:, 16 * a + 16:K], T.G8k[:, :], T.E[:, a, 16:K - 16 * a], False, False)
+                   for a in range(cuts[h], min(cuts[h + 1], 15))]
+            if h == 5:
+                lst.append((T.pR[:, 0:K], T.TRI[:, :], T.E[:, :, 0:16], False, True))
+            mm(lst, ["E%d" % q for q in range(h + 1)] + ["G8k", "TRI"], ["pR"])
+        tt(T.T2[:, :], T.OLD[:, :], T.pU[:, K:2 * K], ALU.subtract, ["OLD", "pU"], ["T2"])
+        tt(T.Q[:, :], T.Ap[:, :], T.pU[:, 0:K], ALU.max, ["Ap", "pU"], ["Q"])
+        scan(T.s2[:, :], T.pR[:, 0:K], ALU.max, ["pR"], ["s2"])
+        tt(T.t1[:, :], T.s2[:, 15:K:16], T.keyL[:, :], ALU.add, ["s2", "keyL"], ["t1"])
+        tt(T.t2[:, :], T.t1[:, :], lim, ALU.min, ["t1", ltok], ["t2"])
+        ts(T.fo[:, :], T.t2[:, :], shift, None, ALU.add, None, ["t2"], ["fo"])
+        between()
+        tt(whole.indirect(T.fo[:, :]), T.T2[:, :], T.Q[:, :], ALU.max, ["fo", "T2", "Q"], ["TB", "TBd"])
+
+    def key_start(terms, R, bank="pK"):
+        mm(group(T[bank][:, 0:K], terms, stop=False), R, [bank])
+
+    jterms = [(T.I1[:, :], T.JH[:, :]), (T.I1[:, :], T.JL[:, :])]
+
+    spread(T.zs, 0, ZW, "z0")
+    key_start(jterms, ["I1", "JH", "JL"])
+    send("z", 0, sl(T.zs, 0, ZW), sl(T.zr, 0, ZW), nxt, ["z0", "za0", "zb0", "zc0"])
+    iota(T.CC[:, :], [[-3, 2], [0, 256]], 2, "CC")
+    iota(T.C2k[:, :], [[0, 256]], 2048, "C2k")
+    iota(T.TB[:, W + CELLS:TBW], [[0, 256]], 0, "TBd")
+
+    for t in range(RO):
+        if t == 0:
+            big(T.PXB[:, 0:W], "PXB", None, None, "W4")
+        else:
+            names(t)
+            big(T.TB[:, 0:W], "TB", None, None, "W4")
+        act(T.Lf[:, :], cells.indirect(T.bl[:, 32 * t + 16:32 * t + 32]), ["TB", "blA%d" % t], ["Lf"])
+        scan(T.SC[:, 0:K], T.pK[:, 0:K], ALU.max, ["pK"], ["SC0"])
+        offsets(16, False)
+        yw = T.Y[:, 0:W]
+        cp(sl(T.xs, t, K, 0, 128), yw.indirect(T.off[:, 0:8]), YT + ["off"], ["xa%d" % t])
+        act(sl(T.xs, t, K, 128, K), yw.indirect(T.off[:, 8:16]), YT + ["off"], ["xb%d" % t])
+        send("x", t, sl(T.xs, t), sl(T.xr, t), nxt, ["xa%d" % t, "xb%d" % t])
+        tt(sl(T.ns, t), ohw.indirect(offj), T.Lf[:, :], ALU.mult, ["OH", "off", "Lf"], ["ns%d" % t])
+        send("n", t, sl(T.ns, t), sl(T.nq, t), nxt, ["ns%d" % t])
+        if t == 0:
+            late_constants()
+            cp(T.TB[:, 0:W // 2], T.PXB[:, 0:W // 2], ["PXB"], ["TB"])
+            act(T.TB[:, W // 2:W], T.PXB[:, W // 2:W], ["PXB"], ["TBh"])
+        rz, rx, u = "rz%d" % t, "rx%d" % t, t + 1
+        na, par, ntx = [sl(T.zs, u, ZW, K + 16 * i, K + 16 * i + 16) for i in range(3)]
+        na0, par0, ntx0 = [sl(T.zr, t, ZW, K + 16 * i, K + 16 * i + 16) for i in range(3)]
+        tt(na, na0, ntx0, ALU.add, [rz], ["za%d" % u])
+        tt(par, par0, ntx0, ALU.is_equal, [rz], ["zb%d" % u])
+        ts(T.thr[:, :], par, 2.0, -12.0, ALU.mult, ALU.add, ["zb%d" % u], ["thr"])
+        x = sl(T.xr, t)
+        key_start([(T.I2[:, :], T.JH[:, :]), (T.I2[:, :], T.JL[:, :])], ["I2", "JH", "JL"])
+        mm(group(T.pS[:, 0:16], [(wr_(T.Wu, a), sl(T.xr, t, K, 16 * a, 16 * a + 16)) for a in range(16)]), [rx, "Wu"], ["pS"])
+        cp(T.bi[:, 0:16], T.pS[:, 0:16], ["pS"], ["bi"])
+        ts(T.bj[:, 0:16], T.bi[:, 0:16], CELLS - 1, None, ALU.bitwise_and, None, ["bi"], ["bj"])
+        cp(T.bl[:, 32 * u:32 * u + 16], T.bj[:, 0:16], ["bj"], ["blB%d" % u])
+        names(u)
+        if t == 0:
+            need("V", wrote["TBh"])
+            need("A", wrote["TBh"])
+        sums(T.xr, t, rx)
+        spread(T.xr, t, K, rx)
+        key_start(jterms + [(T.SX[0:16, :], T.DA[0:16, :])], ["I1", "JH", "JL", "SX", "DA"], "pA")
+        mm(group(T.pT[:, 256:272], [(wr_(T.Wu, r), st(T.xr, t, r)) for r in range(16)]), [rx, "Wu"], ["pT"])
+        values_start(sl(T.nq, t), "rn%d" % t)
+        big(T.TB[:, 0:W], "TB", "pA", "W4", "W8", lambda: act(T.A3[:, :], T.pA[:, 0:K], ["pA"], ["A3"]))
+        cp(T.ai[:, :], T.pT[:, 256:272], ["pT"], ["ai"])
+        ts(T.aj[:, :], T.ai[:, :], CELLS - 1, None, ALU.bitwise_and, None, ["ai"], ["aj"])
+        cp(T.bl[:, 32 * u + 16:32 * u + 32], T.aj[:, :], ["aj"], ["blA%d" % u])
+        ts(T.bb[:, :], T.aj[:, :], float(W), None, ALU.add, None, ["aj"], ["bb"])
+        act(T.Lf[:, :], cells.indirect(T.bl[:, 32 * u + 16:32 * u + 32]), ["TB", "blA%d" % u], ["Lf"])
+        tt(T.nk[:, :], T.pK[:, 0:K], T.A3[:, :], ALU.subtract, ["pK", "A3"], ["nk"])
+        scan(T.SC[:, 0:K], T.nk[:, :], ALU.max, ["nk"], ["SC0"])
+        act(T.sg[:, :], T.nk[:, :], ["nk"], ["sg"], f=AF.Sign, bias=1.0 - 4096.0 * (4080 - TH1 + 1))
+        mm(group(T.pT[:, 0:16], [(T.I1[:, :], T.sg[:, k:K:16]) for k in range(16)]), ["sg"], ["pT"])
+        tt(T.ne[:, :], T.SC[:, 0:K].indirect(T.c15[:, :]), T.nk[:, :], ALU.not_equal, ["SC0", "c15", "nk"], ["ne"])
+        tt(T.ks[:, :], T.ne[:, :], T.pK[:, 0:K], ALU.mult, ["ne", "pK"], ["ks"])
+        tt(ntx, T.pT[:, 0:16], T.thr[:, :], ALU.is_lt, ["pT", "thr"], ["zc%d" % u])
+        scan(T.SC[:, K:2 * K], T.ks[:, :], ALU.max, ["ks"], ["SC1"])
+        nr2 = sl(T.ls, t, LW, K, LW)
+        live = sl(T.ls, t, LW, 0, K)
+        cp(T.nu[:, :], ntx, ["zc%d" % u], ["nu"])
+        act(live, T.NP[:, 0:16].indirect(T.nu[:, :]), ["NP", "nu"], ["la%d" % t])
+        act(nr2, ntx, ["zc%d" % u], ["lb%d" % t], scale=8192.0)
+        offsets(32, True)
+        offm = T.off[:, 16:32]
+        tt(sl(T.fs, t), yw.indirect(offm), x, ALU.max, YT + ["off", rx], ["fs%d" % t])
+        send("f", t, sl(T.fs, t), sl(T.fr, t), nxt, ["fs%d" % t])
+        name_row(T.Lf, "Lf")
+        kind_row(x, rx, live, "la%d" % t, True)
+        tt(sl(T.ms, t), ohw.indirect(offm), T.Lf[:, :], ALU.mult, ["OH", "off", "Lf"], ["ms%d" % t])
+        send("l", t, sl(T.ls, t, LW), sl(T.lr, t, LW), nxt, ["la%d" % t, "lb%d" % t])
+        send("m", t, sl(T.ms, t), sl(T.mr, t), nxt, ["ms%d" % t])
+        scan(T.s2[:, :], T.pR[:, 0:K], ALU.max, ["pR"], ["s2"])
+        tt(T.t1[:, :], T.s2[:, 15:K:16], nr2, ALU.add, ["s2", "lb%d" % t], ["t1"])
+        tt(T.keyL[:, :], T.t1[:, :], T.bb[:, :], ALU.min, ["t1", "bb"], ["keyL"])
+        rf = "rf%d" % t
+        f = sl(T.fr, t)
+
+        def high(src, tok):
+            act(T.a1[:, :], src, [tok], ["a1"], bias=M4096, scale=1.0 + 2.0 ** -21)
+            act(T.hi[:, :], T.a1[:, :], ["a1"], ["hi"], bias=-M4096 - 4096.0)
+
+        def places():
+            c2k = (T.I1[:, :], T.C2k[:, :])
+            mm(group(T.pS[:, 0:K], [c2k], stop=False) + group(T.pZ[:, 0:K], [c2k, (T.I1n[:, :], T.C2k[:, :])], stop=False),
+               ["C2k", "I1", "I1n"], ["pS", "pZ"])
+            mm([(T.pS[:, 16 * r:16 * r + 16], T.KB[:, :], st(T.fr, t, r), False, r == 15) for r in range(16)], [rf, "KB"], ["pS"])
+            high(T.pS[:, 0:K], "pS")
+            mm([(T.pZ[:, 16 * r:16 * r + 16], T.KB[:, :], st(T.fr, t, r), False, False) for r in range(16)], [rf, "KB"], ["pZ"])
+            sums(T.fr, t, rf)
+            mm(group(T.pZ[:, 0:K], [(T.I1n[:, :], T.hi[:, :])], start=False), ["hi"], ["pZ"])
+            spread(T.fr, t, K, rf)
+            key_start(jterms + [(T.SX[0:16, :], T.DAn[0:16, :])], ["I1", "JH", "JL", "SX", "DAn"])
+            mm(group(T.pS[:, 0:K], [c2k, (T.KB[:, :], f)]), [rf], ["pS"])
+        write(0.0, T.dm[:, :], "dm", T.Ob2[:, :], "Ob2", places)
+        cp(T.Lu[:, :], T.pZ[:, 0:K], ["pZ"], ["Lu0", "Lu1"])
+
+        def lane_places():
+            high(T.pS[:, 0:K], "pS")
+            mm(group(T.pT[:, 0:K], [(T.KB[:, :], f), (T.I1n[:, :], T.hi[:, :])]), [rf, "hi"], ["pT"])
+            act(T.Lc[:, :], T.pT[:, 0:K], ["pT"], ["Lc"])
+        big(T.TB[:, 0:W], "TB", "pK", "W4n", "W8", lane_places)
+        values_start(sl(T.mr, t), "rm%d" % t)
+        rl = "rl%d" % t
+        tt(T.dv[:, :], T.cl[:, :], sl(T.lr, t, LW, K, LW), ALU.subtract, ["cl", rl], ["dv"])
+        z0 = sl(T.zr, t, ZW, 0, K)
+        mm(group(T.pS[:, 0:K], [(T.I1[:, :], z0), (T.I8n[:, :], live)])
+           + group(T.pS[:, K:2 * K], [(T.I1[:, :], T.Ob2[:, :]), (T.I8n[:, :], live)]), [rz, "la%d" % t, "Ob2"], ["pS"])
+        scan(T.SC[:, 0:K], T.pK[:, 0:K], ALU.max, ["pK"], ["SC0"])
+        offsets(16, False)
+        name_row(T.Lc, "Lc")
+        far = 4096.0 * (4080 - TH2 + 1)
+        ts(T.nu[:, :], T.SC[:, 15:K:16], far, None, ALU.is_lt, None, ["SC0"], ["nu"])
+        kind_row(f, rf, T.NP3[:, :], "NP3", False)
+        act(T.E12[:, :], T.pS[:, :], ["pS"], ["E12"], f=AF.Relu)
+        tt(sl(T.ws, t), yw.indirect(offj), sl(T.lr, t, LW, 0, K), ALU.mult, YT + ["off", rl], ["ws%d" % t])
+        send("w", t, sl(T.ws, t), sl(T.wr, t), prv, ["ws%d" % t])
+        ts(T.nr[:, :], T.nu[:, :], 8192.0, -4096.0, ALU.mult, ALU.add, ["nu"], ["nr"])
+        scan(T.s2[:, :], T.pR[:, 0:K], ALU.max, ["pR"], ["s2"])
+        cp(T.qi[:, :], T.s2[:, 15:K:16], ["s2"], ["qi"])
+        tt(T.t1[:, :], T.s2[:, 15:K:16], T.nr[:, :], ALU.add, ["s2", "nr"], ["t1"])
+        ts(T.qj[:, :], T.qi[:, :], CELLS - 1, None, ALU.bitwise_and, None, ["qi"], ["qj"])
+        tt(T.t2[:, :], T.t1[:, :], T.qj[:, :], ALU.min, ["t1", "qj"], ["t2"])
+        tt(T.keyL[:, :], T.t2[:, :], T.dv[:, :], ALU.max, ["t2", "dv"], ["keyL"])
+
+        def newz():
+            mm(group(T.pZ[:, 0:K], [(T.I1[:, :], z0), (T.I1[:, :], T.E12[:, 0:K]), (T.I2n[:, :], T.E12[:, K:2 * K])],
+                     stop=False), [rz, "E12", "I2n"], ["pZ"])
+            mm(group(T.pZ[:, 0:K], [(T.I1[:, :], sl(T.wr, t))], start=False), ["rw%d" % t], ["pZ"])
+            act(T.a1[:, :], T.pZ[:, 0:K], ["pZ"], ["a1"], bias=M1, scale=HALF)
+            act(sl(T.zs, u, ZW, 0, K), T.a1[:, :], ["a1"], ["z%d" % u], f=AF.Abs, bias=-M1)
+            if u < RO:
+                send("z", u, sl(T.zs, u, ZW), sl(T.zr, u, ZW), nxt, ["z%d" % u, "za%d" % u, "zb%d" % u, "zc%d" % u])
+                spread(T.zs, u, ZW, "z%d" % u)
+                key_start(jterms, ["I1", "JH", "JL"])
+        write(4096.0, T.cl[:, :], "cl", T.Ob3[:, :], "Ob3", newz)
+
+    def out(e, dst, src, R):
+        deps(e, R, [])
+        s = "outg" if e == "G" else "outs"
+        Q[e].dma_start(dst, src).then_inc(T.sem[s], 16)
+        cnt[s] += 16
+
+    out("G", T.yx[:, :], T.TB[:, 0:W], ["TB"])
+    out("S", T.yc[:, :], cells, ["TB"])
+    cp(T.yvf[:, :], T.aj[:, :], ["aj"], ["yvf"])
+    tt(T.t1[:, :], na, ntx, ALU.add, ["za%d" % RO, "zc%d" % RO], ["t1"])
+    ts(T.au[:, :], T.t1[:, :], -1.0, float(RO), ALU.mult, ALU.add, ["t1"], ["au"])
+    cp(T.ar[:, :], T.IDT[:, 0:256].indirect(T.au[:, :]), ["au", "ioc"], ["ar"])
+    out("A", T.yz[:, :], sl(T.zs, RO, ZW, 0, K), ["z%d" % RO])
+    out("A", T.yv[:, :], T.yvf[:, :], ["yvf"])
+    for q in range(8):
+        out("A" if q % 2 else "S", T.ya[q:q + 1, :], T.ar[16 * q:16 * q + 1, :], ["ar"])
+    for s in ("cV", "cA", "cP", "cG", "sent", "outs", "outg"):
+        need("G", (s, cnt[s]))

@@ -3,48 +3,58 @@ ALU = AluOpType
 AF = ActivationFunctionType
 
 N, W, CELLS, K, RO, TH1, TH2 = 4, 4096, 1024, 256, 4, 256, 600
-TBW = W + CELLS + K
+HN, HA, PAD = 128, 8, 16
+SP = W + 2 * CELLS
+TBW = SP + K
+YW = PAD + 16 * HN
 M1 = 1.5 * 2.0 ** 23
+M1024 = 1.5 * 2.0 ** 33
 M4096 = 1.5 * 2.0 ** 35
 HALF = 0.5 - 2.0 ** -12
-ZW, LW = 304, 272
+ZW, MW = 304, 272
+TOP = 2.0 ** 24 - 1
+VSHARE = ((64, 0), (32, 0), (64, 0))
+LOOK, PASSES, MG, XV, HV = 0.25, 3, 4, (0, 0), (0, 0)
+HOP, FLIGHT, ISSUE = 130, 4500, 600
 
 
 def _s(cols, dtype):
     return ("sbuf", [128, cols], dtype)
 
 
-BF, F32, I32, U16 = "bfloat16", "float32", "int32", "uint16"
+BF, F32, I32, U16, F16 = "bfloat16", "float32", "int32", "uint16", "float16"
 SCRATCH = {
-    "TB": _s(TBW, F32), "PXB": _s(W, BF), "CE": _s(CELLS, I32), "IDT": _s(TBW, F32), "NP": _s(16, BF),
-    "OH": _s(W, BF), "Y": _s(W, BF), "MN": _s(W, BF), "E": ("sbuf", [128, 16, 272], BF),
-    "vi": _s(16, I32), "vf": _s(16, F32), "VX": _s(128, F32), "kp": _s(16, BF), "wv": _s(8, BF), "KB": _s(128, BF),
-    "pi": _s(16, I32), "pj": _s(16, I32), "col": _s(16, F32), "ioa": _s(256, F32), "iok": _s(256, F32),
+    "TB": _s(TBW, F32), "PXB": _s(W, BF), "CE": _s(CELLS, I32), "NP": _s(16, BF), "OH": _s(YW, BF),
+    "Y0": _s(YW, BF), "Y1": _s(YW, BF), "MN": _s(W, BF), "E": ("sbuf", [128, 16, 256], BF), "YC": _s(CELLS, F32),
+    "vi": _s(16, I32), "VX": _s(256, F16), "kp": _s(16, BF), "wv": _s(8, BF), "KB": _s(128, BF), "KB2": _s(128, BF),
+    "pi": _s(16, I32), "pj": _s(16, I32), "col": _s(16, F32), "ioc": _s(256, F32), "ioa": _s(128, F32), "iok": _s(128, F32),
+    "ioe": _s(128, F32), "GE": _s(128, BF), "RS": _s(8, BF), "rep": _s(16, U16), "repf": _s(16, F32),
     "W1": _s(144, BF), "W4": _s(144, BF), "W8": _s(144, BF), "W4n": _s(144, BF), "Wu": _s(144, BF),
-    "GO": _s(128, BF), "GO32": _s(128, F32), "G8k": _s(128, BF), "TRI": _s(128, BF), "tri0": _s(128, BF),
+    "GO": _s(128, BF), "GOn": _s(128, BF), "G8k": _s(128, BF), "G8n": _s(128, BF), "TRI": _s(128, BF), "tri0": _s(128, BF),
     "I1": _s(128, BF), "I2": _s(128, BF), "I2n": _s(128, BF), "I8k": _s(128, BF), "I8n": _s(128, BF), "I1n": _s(128, BF),
-    "OH32": _s(16, F32), "NM": _s(256, BF), "m0": _s(256, BF), "JH": _s(256, BF), "JL": _s(256, BF),
-    "DA": _s(256, F32), "DAn": _s(256, F32), "c15": _s(16, U16), "cl": _s(16, F32), "dm": _s(16, F32), "hc": _s(32, F32),
-    "CC": _s(512, BF), "C2k": _s(256, BF), "nu": _s(16, U16), "Lc": _s(256, F32), "ai": _s(16, I32), "aj": _s(16, I32),
-    "bl": _s(32 * (RO + 1), U16), "bi": _s(32, I32), "bj": _s(32, I32), "bb": _s(16, F32), "yvf": _s(16, F32),
-    "Lu": _s(256, U16), "Lf": _s(256, F32), "SX": _s(128, F32), "A3": _s(256, F32), "nk": _s(256, F32),
-    "SC": _s(512, F32), "ne": _s(256, BF), "ks": _s(256, F32), "sg": _s(256, BF), "cs": _s(256, F32),
-    "oi": _s(32, I32), "oj": _s(32, I32), "off": _s(32, U16), "MS": _s(256, F32), "s2": _s(256, F32),
-    "thr": _s(16, F32), "t1": _s(16, F32), "t2": _s(16, F32), "keyL": _s(16, F32), "ku": _s(16, U16), "kr": _s(256, U16),
-    "nr": _s(16, F32), "nr0": _s(16, F32), "dv": _s(16, F32), "qi": _s(16, I32), "qj": _s(16, I32),
-    "oh": _s(256, BF), "OLD": _s(256, F32), "Ob2": _s(256, BF), "Ob3": _s(256, BF), "NP3": _s(256, BF),
-    "a1": _s(256, F32), "Ap": _s(256, F32), "Q": _s(256, F32), "T2": _s(256, F32), "fo": _s(16, U16),
-    "hi": _s(256, BF), "E12": _s(512, BF), "au": _s(16, U16), "ar": _s(256, F32),
-    "zs": _s(ZW * (RO + 1), BF), "xs": _s(K * RO, BF), "ns": _s(K * RO, F32), "fs": _s(K * RO, BF),
-    "ms": _s(K * RO, F32), "ls": _s(LW * RO, BF), "ws": _s(K * RO, BF),
-    "zr": _s(ZW * RO, BF), "xr": _s(K * RO, BF), "nq": _s(K * RO, F32), "fr": _s(K * RO, BF),
-    "mr": _s(K * RO, F32), "lr": _s(LW * RO, BF), "wr": _s(K * RO, BF),
+    "I32": _s(128, F32), "J32": _s(128, F32), "one": _s(128, BF), "CK": _s(512, BF),
+    "NM": _s(128, BF), "m0": _s(128, BF), "JH": _s(128, BF), "JL": _s(128, BF), "RR": _s(256, F32),
+    "DA": _s(128, F32), "DAn": _s(128, F32), "c15": _s(8, U16), "hc": _s(16, F32),
+    "bB": _s(16 * (RO + 1), U16), "bA": _s(16 * (RO + 1), U16), "bC": _s(16, U16),
+    "bi": _s(32, I32), "bj": _s(32, I32), "yvf": _s(16, F32), "thr": _s(16, F32), "dk": _s(16, F32),
+    "Lu": _s(256, U16), "Lf": _s(256, F32), "ck": _s(256, F32), "SX": _s(256, F32), "A3": _s(256, F32), "nk": _s(256, F32),
+    "SC": _s(512, F32), "ne": _s(256, BF), "ks": _s(256, F32), "sg": _s(256, BF), "cs": _s(256, BF),
+    "oi": _s(32, I32), "oj": _s(32, I32), "off": _s(32, U16), "ofm": _s(16, U16), "nu": _s(16, U16),
+    "MS": _s(256, F16), "kr": _s(256, F16), "s1": _s(256, F32), "s2": _s(256, F32), "ku": _s(16, U16), "fo": _s(16, U16),
+    "oh": _s(256, BF), "live": _s(256, BF), "yj": _s(256, BF), "np3": _s(256, BF), "OLD": _s(256, F32), "sel": _s(256, F32),
+    "a1": _s(256, F32), "a2": _s(256, F32), "a3": _s(256, F32), "Hs": _s(256, F32), "Cs": _s(256, F32), "Q": _s(256, F32),
+    "hi": _s(256, BF), "md": _s(256, F32), "Lcc": _s(256, F32), "E12": _s(512, BF),
+    "t1": _s(16, F32), "au": _s(16, U16), "ar": _s(256, F32),
+    "zs": _s(ZW * (RO + 1), BF), "xs": _s(K * RO, BF), "ns": _s(K * RO, F16), "fs": _s(K * RO, BF),
+    "ms": _s(MW * RO, F16), "ws": _s(K * RO, BF),
+    "zr": _s(ZW * RO, BF), "xr": _s(K * RO, BF), "nr": _s(K * RO, F16), "fr": _s(K * RO, BF),
+    "mr": _s(MW * RO, F16), "wr": _s(K * RO, BF),
 }
-for _b in ("pX", "pK", "pA", "pS", "pT", "pR", "pZ", "pU"):
+for _b in ("pX0", "pX1", "pK0", "pK1", "pU0", "pU1", "pR0", "pR1"):
     SCRATCH[_b] = ("psum", [128, 512], F32)
-MSGS = ("z", "x", "n", "f", "m", "l", "w")
+MSGS = ("z", "x0", "x1", "n", "f0", "f1", "m", "w0", "w1")
 SEMAPHORES = (["cV", "cA", "cP", "cG", "sent", "dv0", "dce", "dz", "dpx", "dw", "outs", "outg"]
-              + ["r%s%d" % (m, t) for m in MSGS for t in range(RO)])
+              + ["r%s_%d" % (m, t) for m in MSGS for t in range(RO)])
 
 
 def rank_program(g, core, T, topo):
@@ -55,435 +65,537 @@ def rank_program(g, core, T, topo):
     assert topo.may_write(core, nxt) and topo.may_write(core, prv)
     V, A, P, S = g.vector, g.scalar, g.tensor, g.sync
     Q = {"V": V, "A": A, "P": P, "G": g, "S": S}
+
+    ops, wrote, readers = [], {}, {}
+
+    def record(e, fn, R, Wr, cost, kind="op", sem=None):
+        pre = set()
+        for t in R:
+            if t in wrote:
+                pre.add(wrote[t])
+            if t[0] == "p" and t[1].isupper():
+                pre.update(d for d in readers.get(t, []) if ops[d]["e"] != e)
+        for t in Wr:
+            pre.update(([wrote[t]] if t in wrote else []) + readers.get(t, []))
+        me = len(ops)
+        ops.append({"e": e, "fn": fn, "pre": sorted(pre), "cost": cost, "kind": kind, "sem": sem})
+        for t in (R if kind == "op" else []):
+            readers.setdefault(t, []).append(me)
+        for t in Wr:
+            wrote[t] = me
+            readers[t] = []
+        return me
+
+    lines = {}
+
+    def in_line(name):
+        if name in lines:
+            ops[-1]["line"] = [lines[name]]
+        lines[name] = len(ops) - 1
+
+    def gat(n):
+        return 70 + 1.56 * n
+
+    def tt(out, a, b, alu, R, Wr, c=64):
+        record("V", lambda: V.tensor_tensor(out, a, b, alu), R, Wr, c)
+
+    def ts(out, a, s1, s2, o0, o1, R, Wr, c=64):
+        if o1 is None:
+            record("V", lambda: V.tensor_scalar(out, a, s1, None, o0), R, Wr, c)
+        else:
+            record("V", lambda: V.tensor_scalar(out, a, s1, s2, o0, o1), R, Wr, c)
+
+    def cp(out, a, R, Wr, c=64):
+        record("V", lambda: V.tensor_copy(out, a), R, Wr, c)
+
+    def fill(ap, c, tok):
+        record("V", lambda: V.memset(ap, c), [], [tok], 64)
+
+    def scan(out, d0, d1, o0, o1, R, Wr, c=HN):
+        record("V", lambda: V.tensor_tensor_scan(out, d0, d1, 0.0, o0, o1), R, Wr, c)
+
+    def act(out, a, R, Wr, f=AF.Identity, bias=0.0, scale=1.0, c=HN):
+        record("A", lambda: A.activation(out, a, f, bias=bias, scale=scale), R, Wr, c)
+
+    def mm(lst, R, Wr, c=None):
+        def fn():
+            for m in lst:
+                i = P.matmul(m[0], m[1], m[2], m[3], m[4])
+            return i
+        record("P", fn, R, Wr, 64 * len(lst) if c is None else c)
+
+    def group(out, terms, start=True, stop=True):
+        n = len(terms)
+        return [(out, l, r, start and i == 0, stop and i == n - 1) for i, (l, r) in enumerate(terms)]
+
+    def iota(out, pattern, base, tok, n):
+        record("G", lambda: g.iota(out, pattern, base, 0, allow_small_or_imprecise_dtypes=True), [], [tok], 160 + 2 * n)
+
+    def send(m, t, src, dst, R):
+        to, name = (prv if m[0] == "w" else nxt), "r%s_%d" % (m, t)
+        rid, pid = topo.addr(to)[0:2]
+        i = record("G", lambda: g.remote_dma(dst, src, T.sem[name], T.sem.sent, pid, rid, topo.mask(core, to)), R, [],
+                   ISSUE, "send", len(topo.engines(core, to)))
+        record(None, None, [], [name], FLIGHT, "land", (name, len(topo.engines(nxt if m[0] == "w" else prv, core))))
+        ops[-1]["pre"] = [i]
+
+    def load(e, dst, src, sem, total, tok, cost, **kw):
+        i = record(e, lambda: Q[e].dma_start(dst, src, **kw).then_inc(T.sem[sem], 16), [], [], 60, "dma")
+        if tok is not None:
+            record(None, None, [], [tok], cost, "land", (sem, total))
+            ops[-1]["pre"] = list(range(i + 1 - total // 16, i + 1))
+
+    def store(e, dst, src, R):
+        record(e, lambda: Q[e].dma_start(dst, src).then_inc(T.sem["outg" if e == "G" else "outs"], 16), R, [], 60, "out")
+
+    def sl(buf, t, w=K, a=0, b=None):
+        return buf[:, t * w + a: t * w + (w if b is None else b)]
+
+    def hf(buf, h, t=0, w=K):
+        return buf[:, t * w + HN * h:t * w + HN * h + HN]
+
+    def hl(buf, h, t=0):
+        return buf[:, 16 * t + HA * h:16 * t + HA * h + HA]
+
+    def dg(buf, h, a=0):
+        return buf[:, a + HN * h + 15:a + HN * h + HN:16]
+
+    cells = T.TB[:, W:SP]
+    Y = (T.Y0, T.Y1)
+    ohw = T.OH[:, 0:YW]
+
+    load("S", T.vi[:, :], T.v0[:, :], "dv0", 16, "vi", 2400)
+    load("S", T.CE[:, :], T.ce[:, :], "dce", 16, "CE", 5000)
+    load("A", T.zs[:, 0:K], T.z0[:, :], "dz", 16, "z0", 2600)
+    load("A", T.PXB[:, 0:W // 2], T.px[:, 0:W // 2], "dpx", 32, None, 0)
+    load("S", T.PXB[:, W // 2:W], T.px[:, W // 2:W], "dpx", 32, "PXB", 9000)
+    load("G", T.kp[:, :], T.kap[:, :], "dw", 32, None, 0)
+    load("G", T.wv[:, 0:1], T.wu[:, :], "dw", 32, "kw", 4000, allow_slow_non_contiguous=True)
+    wrote["z0_0"] = wrote["z1_0"] = wrote["z0"]
+
+    record("G", lambda: g.iota(T.pi[:, :], [[0, 16]], 0, 1), [], ["pi"], 200)
+    iota(T.ioc[:, :], [[1, 256]], 0, "ioc", 256)
+    iota(T.ioe[:, :], [[1, 16], [0, 8]], 0, "ioe", 128)
+    iota(T.ioa[:, :], [[1, 8], [0, 16]], 0, "ioa", 128)
+    iota(T.iok[:, :], [[0, 8], [1, 16]], 0, "iok", 128)
+    iota(T.JL[:, :], [[0, 8], [-1, 16]], 15, "JL", 128)
+    iota(T.TB[:, W + 1:SP:2], [[2, CELLS]], 2048, "TBo", CELLS)
+    iota(T.TB[:, SP:TBW], [[0, K]], 0, "TBd", K)
+    pc, rc, gc_, ec, sc_, qc, wc, jc, uc, nc = [T.col[:, i:i + 1] for i in range(10)]
+    fill(T.zs[:, K:K + 16], -1.0, "za0")
+    fill(T.zs[:, K + 16:K + 32], 0.0, "zb0")
+    fill(T.zs[:, K + 32:K + 48], 1.0, "zc0_0")
+    wrote["zc1_0"] = wrote["zc0_0"]
+    pi = T.pi[:, 0:1]
+    cp(T.pj[:, 0:1], pi, ["pi"], ["pj0"])
+    ts(T.pj[:, 1:2], pi, 15, None, ALU.bitwise_and, None, ["pi"], ["pj1"])
+    ts(T.pj[:, 2:3], pi, 4, None, ALU.arith_shift_right, None, ["pi"], ["pj2"])
+    ts(T.pj[:, 3:4], pi, 1, None, ALU.bitwise_and, None, ["pi"], ["pj3"])
+    ts(T.pj[:, 4:5], pi, 15, 1, ALU.bitwise_and, ALU.arith_shift_right, ["pi"], ["pj4"])
+    ts(T.pj[:, 5:6], pi, 7, None, ALU.bitwise_and, None, ["pi"], ["pj5"])
+    cp(T.col[:, 0:6], T.pj[:, 0:6], ["pj%d" % i for i in range(6)], ["col"])
+    ts(wc, gc_, 16.0, 15.0, ALU.mult, ALU.add, ["col"], ["wc"])
+    ts(jc, rc, -128.0, 4080.0 - PAD, ALU.mult, ALU.add, ["col"], ["jc"])
+    ts(uc, gc_, 2.0, ec, ALU.mult, ALU.add, ["col"], ["uc"])
+    ts(nc, rc, -1.0, -4096.0, ALU.mult, ALU.add, ["col"], ["nc"])
+    ts(T.GE[:, :], T.ioe[:, :], uc, None, ALU.is_equal, None, ["ioe", "uc"], ["GE"], 128)
+    ts(T.RS[:, :], T.ioc[:, 0:8], sc_, None, ALU.is_equal, None, ["ioc", "col"], ["RS"])
+    ts(T.rep[:, :], T.ioe[:, 0:16], 8.0, qc, ALU.mult, ALU.add, ["ioe", "col"], ["rep"])
+    for h in range(2):
+        tt(hf(T.VX, h), T.vi[:, 0:16].indirect(hl(T.rep, h)), T.GE[:, :], ALU.mult, ["vi", "rep", "GE"], ["VX%d" % h], gat(HN))
+        mm(group(T["pU%d" % h][:, 0:HA], [(hf(T.VX, h), T.RS[:, :])]), ["VX%d" % h, "RS"], ["pU%d" % h], 32)
+        cp(hl(T.bB, h), T["pU%d" % h][:, 0:HA], ["pU%d" % h], ["bB%d_0" % h])
+    ts(T.bA[:, 0:16], T.vi[:, :], 2.0, None, ALU.mult, None, ["vi"], ["bA0"])
+    cp(T.TB[:, W:SP:2], T.CE[:, :], ["CE"], ["TBc"], 1024)
+    ts(T.I1[:, :], T.ioc[:, 0:128], pc, None, ALU.is_equal, None, ["ioc", "col"], ["I1"], 128)
+    ts(T.W4[:, :], T.ioc[:, 0:144], wc, 4096.0, ALU.is_equal, ALU.mult, ["ioc", "wc"], ["W4"], 144)
+    ts(T.JH[:, :], T.ioa[:, :], -16.0, jc, ALU.mult, ALU.add, ["ioa", "jc"], ["JH"], 128)
+    ts(T.m0[:, :], T.iok[:, :], 0.0, None, ALU.is_gt, None, ["iok"], ["m0"], 128)
+    ts(T.OH[:, PAD:PAD + 128], T.iok[:, :], rc, None, ALU.is_equal, None, ["iok", "col"], ["OH"], 128)
+    ts(T.NM[:, :], T.OH[:, PAD:PAD + 128], -1.0, 2.0 ** 22, ALU.add, ALU.mult, ["OH"], ["NM"])
+    for w in (128, 256, 512, 1024):
+        cp(T.OH[:, PAD + w:PAD + 2 * w], T.OH[:, PAD:PAD + w], ["OH"], ["OH"], w // 2)
+    for buf, tok in ((T.OH, "OHz"), (T.Y0, "Yz0"), (T.Y1, "Yz1")):
+        fill(buf[:, 0:PAD], 0.0, tok)
+    ts(T.GO[:, :], T.ioa[:, :], gc_, None, ALU.is_equal, None, ["ioa", "col"], ["GO"], 128)
+    ts(T.W1[:, :], T.W4[:, :], 2.0 ** -12, None, ALU.mult, None, ["W4"], ["W1"])
+    ts(T.Wu[:, :], T.W1[:, :], T.wv[:, 0:1], None, ALU.mult, None, ["W1", "kw"], ["Wu"])
+    ts(T.DA[0:32, :], T.ioa[0:32, :], T.col[0:32, 0:1], 4096.0, ALU.is_equal, ALU.mult, ["ioa", "col"], ["DA"], 128)
+    fill(T.hc[:, 0:HA], 1.0, "hca")
+    fill(T.hc[:, HA:16], 0.5, "hcb")
+    ts(T.tri0[:, :], T.ioc[:, 0:128], pc, -8192.0, ALU.is_gt, ALU.mult, ["ioc", "col"], ["tri0"], 128)
+    tt(T.TRI[:, :], T.tri0[:, :], T.GO[:, :], ALU.mult, ["tri0", "GO"], ["TRI"], 256)
+    ts(T.c15[:, :], T.ioc[:, 0:HA], 16.0, 15.0, ALU.mult, ALU.add, ["ioc"], ["c15"])
+    cp(T.NP[:, :], T.ioc[:, 0:16], ["ioc"], ["NP"])
+    record("V", lambda: V.memset(T.RR[:, :], 2.0 ** 26), [], ["RR"], 256)
+    ts(T.RR[:, 0:K:16], T.ioc[:, 0:16], -16.0, nc, ALU.mult, ALU.add, ["ioc", "nc"], ["RR"])
+    fill(T.one[0:2, :], 1.0, "one")
+    fill(T.CK[0:2, 0:256], 0.5, "CK")
+    for i, c in enumerate((-2048.0, -512.0, 2048.0 - 16384.0, -8192.0)):
+        fill(T.CK[0:1, 128 * i:128 * i + 128], c, "CK")
+
+    def blocks():
+        for q in range(8):
+            i = V.tensor_tensor(T.KB[:, 16 * q:16 * q + 16], T.kp[:, :], T.GO[:, 16 * q:16 * q + 16], ALU.mult)
+        return i
+    record("V", blocks, ["kw", "GO"], ["KB"], 512)
+    for name, src, c in (("I2", "I1", 2.0), ("W8", "W4", 2.0), ("I8n", "I1", -8192.0), ("I8k", "I1", 8192.0),
+                         ("G8k", "GO", 8192.0), ("G8n", "GO", -8192.0), ("GOn", "GO", -1.0), ("I2n", "I1", -2.0),
+                         ("I1n", "I1", -1.0), ("W4n", "W4", -1.0), ("I32", "I1", 1.0), ("J32", "I1", -2.0), ("KB2", "KB", 2.0)):
+        act(T[name][:, :], T[src][:, :], [src], [name], scale=c)
+    act(T.DAn[0:32, :], T.DA[0:32, :], ["DA"], ["DAn"], scale=-1.0)
+
+    def const(i, rows=1):
+        return (T.one[0:rows, :], T.CK[0:rows, 128 * i:128 * i + 128])
+
+    def full(name):
+        return T[name][:, :]
+
+    def wr_(buf, r):
+        return buf[:, 15 - r:143 - r]
+
+    def reorder(out, lhs, src, c0, start, stop):
+        return [(out[:, a:HN:HA], lhs, src[:, c0 + 16 * a:c0 + 16 * a + 16], start, stop and (start or a == HA - 1))
+                for a in range(HA)]
+
+    def spread(h, src, c0, tok):
+        mm(reorder(T["pX%d" % h], full("I1"), src, c0, True, True), [tok, "I1"], ["pX%d" % h], 256)
+
+    def sums(h, src, c0, tok):
+        u = T["pU%d" % h]
+        mm([(u[0:HA, 128 + r:256:16], src[:, c0 + r:c0 + HN:16], T.GO[:, 0:128:16], True, True) for r in range(16)],
+           [tok, "GO"], ["pU%d" % h], 128)
+        act(T.SX[0:HA, HN * h:HN * h + HN], u[0:HA, 128:256], ["pU%d" % h], ["SX%d" % h], bias=-4080.0)
+
+    def key_start(bank, one):
+        mm(group(T[bank][:, 0:HN], [(full(one), full("JH")), (full(one), full("JL"))], stop=False), [one, "JH", "JL"], [bank])
+
+    def names(h, win, wtok, t):
+        cp(hf(T.Lu, h), win.indirect(hl(T.bB, h, t)), wtok + ["bB%d_%d" % (h, t)], ["Lu%d" % h], gat(HN))
+
+    def ytoks(h):
+        return ["Y%d_%d" % (h, q) for q in range(4)] + ["Yz%d" % h]
+
+    def big(step, h, win, wtok, ybank, yw, mw, sw=None):
+        for q in range(4):
+            o, i = Y[h][:, PAD + 512 * q:PAD + 512 * q + 512], win.indirect(T.Lu[:, HN * h + 32 * q:HN * h + 32 * q + 32])
+            if 32 * q < VSHARE[step][h]:
+                cp(o, i, wtok + ["Lu%d" % h], ["Y%d_%d" % (h, q)], gat(512))
+            else:
+                act(o, i, wtok + ["Lu%d" % h], ["Y%d_%d" % (h, q)], c=gat(512))
+                in_line("gathers")
+        px_, kb = "pX%d" % h, "pK%d" % h
+        for c in range(2):
+            yt = ["Y%d_%d" % (h, 2 * c), "Y%d_%d" % (h, 2 * c + 1)]
+            if ybank is not None:
+                if c == 1:
+                    mm([(T[ybank][:, 0:HN], T.SX[0:HA, HN * h:HN * h + HN], T[sw][0:HA, :], False, False)], ["SX%d" % h, sw], [ybank], 256)
+                for q in (2 * c, 2 * c + 1):
+                    mm([(T[ybank][:, 0:HN], wr_(T[yw], r), Y[h][:, PAD + 128 * r:PAD + 128 * r + 128], False,
+                         ybank != kb and r == 15) for r in range(4 * q, 4 * q + 4)], ["Y%d_%d" % (h, q), yw], [ybank], 256)
+            for j in range(16 // MG):
+                def fn(c=c, j=j):
+                    for k in range(MG * j, MG * j + MG):
+                        a = 1024 * c + k
+                        i = V.tensor_tensor(T.MN[:, 2048 * h + a:2048 * h + 1024 * c + 1024:16],
+                                            Y[h][:, PAD + a:PAD + 1024 * c + 1024:16], T[px_][:, 64 * c:64 * c + 64], ALU.min)
+                    return i
+                record("V", fn, yt + [px_], ["M%d_%d_%d" % (h, c, j)], 64 * MG)
+                in_line("mins")
+            mm([(T[kb][:, 0:HN], wr_(T[mw], r), T.MN[:, 2048 * h + 128 * r:2048 * h + 128 * r + 128], False, r == 15)
+                for r in range(8 * c, 8 * c + 8)], ["M%d_%d_%d" % (h, c, j) for j in range(16 // MG)] + [mw], [kb], 512)
+
+    def best(h, src, R, a=0):
+        scan(T.SC[:, a + HN * h:a + HN * h + HN], full("m0"), src, ALU.mult, ALU.max, R + ["m0"], ["SC%d_%d" % (h, a)])
+
+    def offsets(out, c0, n, tok):
+        ts(T.oj[:, c0:c0 + n], T.oi[:, c0:c0 + n], 4095, None, ALU.bitwise_and, None, ["oi" + tok], ["oj" + tok])
+        ts(out, T.oj[:, c0:c0 + n], -1.0, 4095.0, ALU.mult, ALU.add, ["oj" + tok], ["off" + tok])
+
+    def write(h, rec, old, rtok, oldf, oftok, obias, newname, ntok, npb, nptok):
+        x_, r_, hh = T["pX%d" % h], T["pR%d" % h], "%d" % h
+        oh = hf(T.oh, h)
+        mm(group(x_[:, 0:128], [(full("I1"), rec), (full("I1"), old), (full("I8n"), npb)])
+           + group(x_[:, 128:256], [const(2), (full("GO"), newname), (full("I8k"), oh), (full("I8k"), npb)]),
+           rtok + [nptok, ntok, "oh" + hh, "I8n", "I8k", "GO", "one", "CK"], ["pX" + hh], 448)
+        act(hf(T.a1, h), x_[:, 0:128], ["pX" + hh], ["a1" + hh], bias=M1, scale=HALF)
+        act(hf(T.Hs, h), hf(T.a1, h), ["a1" + hh], ["Hs" + hh], bias=-M1)
+        tt(hf(T.Q, h), hf(T.Hs, h), x_[:, 128:256], ALU.max, ["Hs" + hh, "pX" + hh], ["Q" + hh], HN)
+        u_ = T["pU" + hh][:, 256:384]
+        mm(group(u_, [(full("I8n"), oh), (full("I8k"), npb)], stop=False), [nptok, "oh" + hh], ["pU" + hh])
+        mm(group(u_, [(full("I32"), oldf)], start=False), [oftok, "I32"], ["pU" + hh], 256)
+        act(hf(T.Cs, h), u_, ["pU" + hh], ["Cs" + hh], bias=obias)
+        mm(group(r_[:, 128:256], [(full("I1"), full("NM")), (full("I1n"), hf(T.kr, h))], stop=False),
+           ["NM", "I1n", "kr" + hh], ["pR" + hh], 128)
+        top = HN * h + HN
+        cuts = (0, 4, 8) if h == 0 else (0, 4, 8, 12, 16)
+        for j in range(len(cuts) - 1):
+            cols = range(cuts[j], cuts[j + 1])
+
+            def fn(cols=cols):
+                for a in cols:
+                    lo = max(16 * a, HN * h)
+                    i = V.tensor_scalar(T.E[:, a, lo - 16 * a:top - 16 * a], T.kr[:, lo:top], T.s1[:, 16 * a + 15:16 * a + 16], 0.0,
+                                        ALU.add, ALU.is_equal)
+                return i
+            record("V", fn, ["kr" + hh, "s1%d" % (cols[0] // HA)], ["E%d_%d" % (h, j)], 256)
+            lst = []
+            for a in cols:
+                lo = max(16 * a + 16, HN * h)
+                if lo < top:
+                    lst.append((r_[:, 128 + lo - HN * h:256], full("G8n"), T.E[:, a, lo - 16 * a:top - 16 * a], False, False))
+            a = cols[0]
+            if a >= HA * h:
+                lst.append((r_[:, 128 + 16 * a - HN * h:192 + 16 * a - HN * h], full("TRI"), T.E[:, a:a + 4, 0:16],
+                            False, j == len(cuts) - 2))
+            mm(lst, ["E%d_%d" % (h, j), "G8n", "TRI"], ["pR" + hh], 256)
+        scan(hf(T.s2, h), hf(T.RR, h), r_[:, 128:256], ALU.min, ALU.max, ["RR", "pR" + hh], ["s2" + hh])
+        ts(hl(T.fo, h), dg(T.s2, h), -1.0, 2048.0, ALU.mult, ALU.add, ["s2" + hh], ["fo" + hh])
+        tt(T.TB[:, 0:TBW].indirect(hl(T.fo, h)), hf(T.Cs, h), hf(T.Q, h), ALU.max, ["fo" + hh, "Cs" + hh, "Q" + hh],
+           ["TB", "TBc", "TBo", "TBd"], 60 + 3.8 * HN)
+
+    send("z", 0, sl(T.zs, 0, ZW), sl(T.zr, 0, ZW), ["z0", "za0", "zb0", "zc0_0"])
+    TBC = ["TBc", "TBo"]
+
+    for t in range(RO):
+        u = t + 1
+        cwin, ctok = (T.CE[:, :], ["CE"]) if t == 0 else (cells, TBC)
+        pwin, ptok = (T.PXB[:, 0:W], ["PXB"]) if t == 0 else (T.TB[:, 0:W], ["TB"])
+        for h in range(2):
+            hh = "%d" % h
+            spread(h, T.zs, t * ZW + HN * h, "z%d_%d" % (h, t))
+            key_start("pK" + hh, "I1")
+            names(h, cwin, ctok, t)
+            big(0, h, pwin, ptok, None, None, "W4")
+            best(h, T["pK" + hh][:, 0:HN], ["pK" + hh])
+            cp(hl(T.oi, h), dg(T.SC, h), ["SC%d_0" % h], ["oi" + hh])
+            offsets(hl(T.off, h), HA * h, HA, hh)
+            (cp if XV[h] else act)(hf(T.xs, h, t), Y[h][:, 0:YW].indirect(hl(T.off, h)), ytoks(h) + ["off" + hh], ["xs" + hh], c=gat(HN))
+            send("x" + hh, t, hf(T.xs, h, t), hf(T.xr, h, t), ["xs" + hh])
+        act(full("Lf"), cells.indirect(sl(T.bA, t, 16)), TBC + ["bA%d" % t], ["Lf"], bias=-2048.0, c=gat(K))
+        tt(sl(T.ns, t), ohw.indirect(T.off[:, 0:16]), full("Lf"), ALU.mult, ["OH", "OHz", "off0", "off1", "Lf"], ["ns"], gat(K))
+        send("n", t, sl(T.ns, t), sl(T.nr, t), ["ns"])
+        if t == 0:
+            for q in range(4):
+                o, i = T.TB[:, 1024 * q:1024 * q + 1024], T.PXB[:, 1024 * q:1024 * q + 1024]
+                if q % 2:
+                    cp(o, i, ["PXB"], ["TB%d" % q], 1024)
+                else:
+                    act(o, i, ["PXB"], ["TB%d" % q], c=1024)
+        ptok = ["TB"] + (["TB%d" % q for q in range(4)] if t == 0 else [])
+        rz = "rz_%d" % t
+        na, par, ntx = [sl(T.zs, u, ZW, K + 16 * i, K + 16 * i + 16) for i in range(3)]
+        na0, par0, ntx0 = [sl(T.zr, t, ZW, K + 16 * i, K + 16 * i + 16) for i in range(3)]
+        tt(na, na0, ntx0, ALU.add, [rz], ["za%d" % u])
+        tt(par, par0, ntx0, ALU.is_equal, [rz], ["zb%d" % u])
+        ts(full("thr"), par, 2.0, -12.0, ALU.mult, ALU.add, ["zb%d" % u], ["thr"])
+        for h in range(2):
+            hh, c0 = "%d" % h, t * K + HN * h
+            rx, pu = "rx%d_%d" % (h, t), T["pU" + hh]
+            mm(group(pu[:, 0:HA], [(wr_(T.Wu, q), T.xr[:, c0 + 16 * (q % 8) + q // 8:c0 + 16 * (q % 8) + 16:2]) for q in range(16)]),
+               [rx, "Wu"], ["pU" + hh], 512)
+            cp(hl(T.bi, h), pu[:, 0:HA], ["pU" + hh], ["bi" + hh])
+            ts(hl(T.bj, h), hl(T.bi, h), CELLS - 1, None, ALU.bitwise_and, None, ["bi" + hh], ["bj" + hh])
+            ts(hl(T.bB, h, u), hl(T.bj, h), 2.0, None, ALU.mult, None, ["bj" + hh], ["bB%d_%d" % (h, u)])
+            names(h, cells, TBC, u)
+            spread(h, T.xr, c0, rx)
+            key_start("pK" + hh, "I2")
+            sums(h, T.xr, c0, rx)
+            key_start("pR" + hh, "I1")
+            if h == 1:
+                mm(group(pu[:, 16:32], [(wr_(T.Wu, r), T.xr[:, t * K + r:t * K + K:16]) for r in range(16)]),
+                   ["rx0_%d" % t, rx, "Wu"], ["pU1"], 512)
+                cp(T.bi[:, 16:32], pu[:, 16:32], ["pU1"], ["biA"])
+                ts(T.bj[:, 16:32], T.bi[:, 16:32], CELLS - 1, None, ALU.bitwise_and, None, ["biA"], ["bjA"])
+                ts(sl(T.bA, u, 16), T.bj[:, 16:32], 2.0, None, ALU.mult, None, ["bjA"], ["bA%d" % u])
+                ts(full("bC"), T.bj[:, 16:32], 2.0, 1.0, ALU.mult, ALU.add, ["bjA"], ["bC"])
+                act(full("Lf"), cells.indirect(sl(T.bA, u, 16)), TBC + ["bA%d" % u], ["Lf"], bias=-2048.0, c=gat(K))
+                act(full("ck"), cells.indirect(full("bC")), TBC + ["bC"], ["ck"], c=gat(K))
+            big(1, h, T.TB[:, 0:W], ptok, "pR" + hh, "W4", "W8", "DA")
+            act(hf(T.A3, h), T["pR" + hh][:, 0:HN], ["pR" + hh], ["A3" + hh])
+        for h in range(2):
+            hh = "%d" % h
+            rx, pu, pk = "rx%d_%d" % (h, t), T["pU" + hh], T["pK" + hh]
+            x, yw, live = hf(T.xr, h, t), Y[h][:, 0:YW], hf(T.live, h)
+            tt(hf(T.nk, h), pk[:, 0:HN], hf(T.A3, h), ALU.subtract, ["pK" + hh, "A3" + hh], ["nk" + hh], HN)
+            best(h, hf(T.nk, h), ["nk" + hh])
+            act(hf(T.sg, h), hf(T.nk, h), ["nk" + hh], ["sg" + hh], f=AF.Sign, bias=1.0 - 4096.0 * (4080 - TH1 + 1))
+            scan(hf(T.cs, h), full("m0"), hf(T.sg, h), ALU.mult, ALU.add, ["m0", "sg" + hh], ["cs" + hh], 64)
+            zc = "zc%d_%d" % (h, u)
+            tt(hl(ntx, h), dg(T.cs, h), hl(T.thr, h), ALU.is_lt, ["cs" + hh, "thr"], [zc])
+            cp(hl(T.nu, h), hl(ntx, h), [zc], ["nu" + hh])
+            act(live, T.NP[:, 0:16].indirect(hl(T.nu, h)), ["NP", "nu" + hh], ["live" + hh], c=gat(HN))
+            tt(hf(T.ne, h), hf(T.SC, h).indirect(full("c15")), hf(T.nk, h), ALU.not_equal, ["SC%d_0" % h, "c15", "nk" + hh],
+               ["ne" + hh], gat(HN))
+            tt(hf(T.ks, h), hf(T.ne, h), pk[:, 0:HN], ALU.mult, ["ne" + hh, "pK" + hh], ["ks" + hh], HN)
+            best(h, hf(T.ks, h), ["ks" + hh], K)
+            cp(hl(T.oi, h), dg(T.SC, h), ["SC%d_0" % h], ["oi" + hh])
+            offsets(hl(T.off, h), HA * h, HA, hh)
+            ts(hl(T.oi, h, 1), dg(T.SC, h, K), 0.5, None, ALU.mult, None, ["SC%d_%d" % (h, K)], ["oim" + hh])
+            offsets(hl(T.ofm, h), 16 + HA * h, HA, "m" + hh)
+            offj = hl(T.off, h)
+            tt(hf(T.fs, h, t), yw.indirect(hl(T.ofm, h)), x, ALU.max, ytoks(h) + ["offm" + hh, rx], ["fs" + hh], gat(HN))
+            send("f" + hh, t, hf(T.fs, h, t), hf(T.fr, h, t), ["fs" + hh])
+            tt(hf(T.MS, h), ohw.indirect(offj), hf(T.Lf, h), ALU.mult, ["OH", "OHz", "off" + hh, "Lf"], ["MS" + hh], gat(HN))
+            act(hf(T.oh, h), ohw.indirect(offj), ["OH", "OHz", "off" + hh], ["oh" + hh], c=gat(HN))
+            act(hf(T.yj, h), yw.indirect(offj), ytoks(h) + ["off" + hh], ["yj" + hh], c=gat(HN))
+            mm(group(pu[:, 0:128], [(full("I8k"), live), (full("GO"), hf(T.MS, h))]), ["I8k", "GO", "live" + hh, "MS" + hh],
+               ["pU" + hh])
+            tt(hf(T.kr, h), pu[:, 0:128], hf(T.ck, h), ALU.min, ["pU" + hh, "ck"], ["kr" + hh], HN)
+            pr = T["pR" + hh][:, 256:384]
+            mm(group(pr, [(full("I1"), full("NM"))], stop=False), ["NM"], ["pR" + hh])
+            mm(group(pr, [(full("I1n"), hf(T.kr, h))], start=False), ["I1n", "kr" + hh], ["pR" + hh])
+            scan(hf(T.s1, h), hf(T.RR, h), pr, ALU.min, ALU.max, ["RR", "pR" + hh], ["s1" + hh])
+            if h == 1:
+                tt(sl(T.ms, t, MW, 0, K), ohw.indirect(full("ofm")), full("Lf"), ALU.mult,
+                   ["OH", "OHz", "offm0", "offm1", "Lf"], ["ms"], gat(K))
+                cp(sl(T.ms, t, MW, K, MW), ntx, ["zc0_%d" % u, zc], ["ml"])
+                send("m", t, sl(T.ms, t, MW), sl(T.mr, t, MW), ["ms", "ml"])
+            z0 = hf(T.zr, h, t, ZW)
+            mm(group(pk[:, 256:384], [(full("I1"), z0), (full("I8n"), live)])
+               + group(pk[:, 384:512], [(full("I1"), hf(T.yj, h)), (full("I8n"), live)]),
+               [rz, "live" + hh, "yj" + hh, "I8n"], ["pK" + hh])
+            act(T.E12[:, K * h:K * h + K], pk[:, 256:512], ["pK" + hh], ["E12" + hh], f=AF.Relu, c=K)
+            write(h, x, hf(T.yj, h), [rx, "yj" + hh], hf(T.Lf, h), "Lf", 2048.0 - 8192.0, hf(T.nr, h, t), "rn_%d" % t,
+                  live, "live" + hh)
+        rm = "rm_%d" % t
+        for h in range(2):
+            hh, c0 = "%d" % h, t * K + HN * h
+            rf, f = "rf%d_%d" % (h, t), hf(T.fr, h, t)
+            pu, pk, pr = T["pU" + hh], T["pK" + hh], T["pR" + hh]
+            mm(group(pu[:, 256:384], [const(0, 2), (full("KB"), f)]) + group(pk[:, 128:256], [const(0)], stop=False)
+               + reorder(pk[:, 128:256], full("KB"), T.fr, c0, False, False), [rf, "KB", "one", "CK"], ["pU" + hh, "pK" + hh], 448)
+            if HV[h]:
+                ts(hf(T.hi, h), pu[:, 256:384], M4096, M4096, ALU.add, ALU.subtract, ["pU" + hh], ["hi" + hh], HN)
+            else:
+                act(hf(T.a2, h), pu[:, 256:384], ["pU" + hh], ["a2" + hh], bias=M4096)
+                act(hf(T.hi, h), hf(T.a2, h), ["a2" + hh], ["hi" + hh], bias=-M4096)
+            mm(reorder(pk[:, 128:256], full("I1n"), T.hi, HN * h, False, True), ["hi" + hh, "I1n"], ["pK" + hh], 256)
+            ts(hf(T.Lu, h), pk[:, 128:256], 2048.0, None, ALU.add, None, ["pK" + hh], ["Lu" + hh], HN)
+            spread(h, T.fr, c0, rf)
+            sums(h, T.fr, c0, rf)
+            key_start("pK" + hh, "I1")
+            mm(group(pu[:, 384:512], [const(1, 2), (full("KB"), f)]), [rf, "KB"], ["pU" + hh])
+            act(hf(T.a3, h), pu[:, 384:512], ["pU" + hh], ["a3" + hh], bias=M1024)
+            act(hf(T.md, h), hf(T.a3, h), ["a3" + hh], ["md" + hh], bias=-M1024)
+            mm(group(pr[:, 256:384], [(full("KB2"), f), (full("J32"), hf(T.md, h))]), [rf, "KB2", "J32", "md" + hh], ["pR" + hh], 320)
+            act(hf(T.Lcc, h), pr[:, 256:384], ["pR" + hh], ["Lcc" + hh], bias=2048.0)
+            big(2, h, T.TB[:, 0:W], ["TB"], "pK" + hh, "W4n", "W8", "DAn")
+        ts(full("dk"), sl(T.mr, t, MW, K, MW), -TOP, TOP, ALU.mult, ALU.add, [rm], ["dk"])
+        for h in range(2):
+            hh = "%d" % h
+            rf, f = "rf%d_%d" % (h, t), hf(T.fr, h, t)
+            pu, pk = T["pU" + hh], T["pK" + hh]
+            offj, npb, oh, w_ = hl(T.off, h), hf(T.np3, h), hf(T.oh, h), hf(T.ws, h, t)
+            best(h, pk[:, 0:HN], ["pK" + hh])
+            ts(hl(T.nu, h), dg(T.SC, h), 4096.0 * (4080 - TH2 + 1), None, ALU.is_lt, None, ["SC%d_0" % h], ["nu" + hh])
+            tt(hl(T.oi, h), dg(T.SC, h), hl(T.dk, h), ALU.max, ["SC%d_0" % h, "dk"], ["oi" + hh])
+            offsets(offj, HA * h, HA, hh)
+            act(npb, T.NP[:, 0:16].indirect(hl(T.nu, h)), ["NP", "nu" + hh], ["np" + hh], c=gat(HN))
+            act(w_, Y[h][:, 0:YW].indirect(offj), ytoks(h) + ["off" + hh], ["ws" + hh], c=gat(HN))
+            send("w" + hh, t, w_, hf(T.wr, h, t), ["ws" + hh])
+            act(oh, ohw.indirect(offj), ["OH", "OHz", "off" + hh], ["oh" + hh], c=gat(HN))
+            mm(group(pu[:, 0:128], [const(0), (full("KB"), f), (full("I1n"), hf(T.hi, h))], stop=False), [rf, "hi" + hh], ["pU" + hh])
+            mm(group(pu[:, 0:128], [(full("I8k"), npb)], start=False), ["np" + hh], ["pU" + hh])
+            tt(hf(T.sel, h), pu[:, 0:128], hf(T.Lcc, h), ALU.min, ["pU" + hh, "Lcc" + hh], ["sel" + hh], HN)
+            tt(hf(T.MS, h), ohw.indirect(offj), hf(T.sel, h), ALU.mult, ["OH", "OHz", "off" + hh, "sel" + hh], ["MS" + hh], gat(HN))
+            pr = T["pR" + hh][:, 0:128]
+            mm(group(pr, [(full("I1"), full("NM")), const(3), (full("G8k"), oh)], stop=False), ["oh" + hh, "G8k", "NM"], ["pR" + hh])
+            mm(group(pu[:, 128:256], [(full("G8n"), oh)], stop=False), ["oh" + hh, "G8n"], ["pU" + hh])
+            mm(group(pu[:, 128:256], [(full("GO"), hf(T.MS, h))], start=False), ["MS" + hh], ["pU" + hh])
+            mm(group(pr, [(full("GOn"), hf(T.MS, h))], start=False), ["MS" + hh, "GOn"], ["pR" + hh])
+            ts(hf(T.kr, h), pu[:, 128:256], 8192.0, None, ALU.add, None, ["pU" + hh], ["kr" + hh], HN)
+            scan(hf(T.s1, h), hf(T.RR, h), pr, ALU.min, ALU.max, ["RR", "pR" + hh], ["s1" + hh])
+            ts(hl(T.ku, h), dg(T.s1, h), -1.0, 2048.0, ALU.mult, ALU.add, ["s1" + hh], ["ku" + hh])
+            act(hf(T.OLD, h), T.TB[:, 0:TBW].indirect(hl(T.ku, h)), ["TB", "TBc", "TBo", "TBd", "ku" + hh], ["OLD" + hh], c=gat(HN))
+            write(h, f, w_, [rf, "ws" + hh], hf(T.OLD, h), "OLD" + hh, -8192.0, hf(T.mr, h, t, MW), rm, npb, "np" + hh)
+            e = T.E12[:, K * h:K * h + HN], T.E12[:, K * h + HN:K * h + K]
+            mm(group(pk[:, 128:256], [(full("I1"), hf(T.zr, h, t, ZW)), (full("I1"), e[0]), (full("I2n"), e[1])], stop=False),
+               [rz, "E12" + hh, "I2n"], ["pK" + hh])
+            mm(group(pk[:, 128:256], [(full("I1"), hf(T.wr, h, t))], start=False), ["rw%d_%d" % (h, t)], ["pK" + hh])
+            act(hf(T.a2, h), pk[:, 128:256], ["pK" + hh], ["a2" + hh], bias=M1, scale=HALF)
+            act(hf(T.zs, h, u, ZW), hf(T.a2, h), ["a2" + hh], ["z%d_%d" % (h, u)], f=AF.Abs, bias=-M1)
+        if u < RO:
+            send("z", u, sl(T.zs, u, ZW), sl(T.zr, u, ZW),
+                 ["z0_%d" % u, "z1_%d" % u, "za%d" % u, "zb%d" % u, "zc0_%d" % u, "zc1_%d" % u])
+
+    store("G", T.yx[:, :], T.TB[:, 0:W], ["TB"])
+    record("A", lambda: A.activation(full("YC"), T.TB[:, W:SP:2], AF.Identity), ["TBc"], ["YC"], CELLS)
+    store("S", T.yc[:, :], full("YC"), ["YC"])
+    cp(full("yvf"), T.bj[:, 16:32], ["bjA"], ["yvf"])
+    tt(full("t1"), na, ntx, ALU.add, ["za%d" % RO, "zc0_%d" % RO, "zc1_%d" % RO], ["t1"])
+    ts(full("au"), full("t1"), -1.0, float(RO), ALU.mult, ALU.add, ["t1"], ["au"])
+    cp(full("ar"), full("ioc").indirect(full("au")), ["au", "ioc"], ["ar"], gat(K))
+    store("S", T.yz[:, :], sl(T.zs, RO, ZW, 0, K), ["z0_%d" % RO, "z1_%d" % RO])
+    store("S", T.yv[:, :], full("yvf"), ["yvf"])
+    for q in range(8):
+        store("S", T.ya[q:q + 1, :], T.ar[16 * q:16 * q + 1, :], ["ar"])
+
+    n = len(ops)
+    after, before, rest = [[] for _ in ops], [[] for _ in ops], [0.0] * n
+    for i, o in enumerate(ops):
+        for d, hop in [(d, 0 if o["e"] == ops[d]["e"] == "P" else HOP) for d in o["pre"]] + [(d, 0) for d in o.get("line", [])]:
+            after[d].append((i, hop))
+            before[i].append((d, hop))
+    for i in range(n - 1, -1, -1):
+        rest[i] = ops[i]["cost"] + max([hop + rest[j] for j, hop in after[i]] + [0.0])
+
+    def plan(after, before, rest):
+        missing = [len(b) for b in before]
+        ready, ends, free, order = [0.0] * n, [0.0] * n, {e: 0.0 for e in Q}, []
+        pool = [i for i in range(n) if not missing[i]]
+        while pool:
+            def begin(i):
+                return max(ready[i], free.get(ops[i]["e"], 0.0))
+            i = min(pool, key=lambda j: (begin(j), -rest[j]))
+            soon = begin(i) + ops[i]["cost"] * LOOK
+            i = max([j for j in pool if ops[j]["e"] == ops[i]["e"] and begin(j) <= soon], key=lambda j: rest[j])
+            ends[i] = begin(i) + ops[i]["cost"]
+            if ops[i]["e"] is not None:
+                free[ops[i]["e"]] = ends[i]
+            pool.remove(i)
+            order.append(i)
+            for j, hop in after[i]:
+                ready[j] = max(ready[j], ends[i] + hop)
+                missing[j] -= 1
+                if not missing[j]:
+                    pool.append(j)
+        return max(ends), order, ends
+
+    plans = [plan(after, before, rest)]
+    for _ in range(PASSES):
+        plans.append(plan(after, before, plan(before, after, plans[-1][2])[2]))
+    order = min(plans, key=lambda p: p[0])[1]
+
     cnt = {"cV": 0, "cA": 0, "cP": 0, "cG": 0, "sent": 0, "outs": 0, "outg": 0}
     seen = {e: {} for e in Q}
-    wrote, readers = {}, {}
 
     def need(e, dep):
         if seen[e].get(dep[0], 0) < dep[1]:
             Q[e].wait_ge(T.sem[dep[0]], dep[1])
             seen[e][dep[0]] = dep[1]
 
-    def deps(e, R, Wr):
-        own, ds = "c" + e, {}
-        for t in R:
-            c = [wrote[t]] if t in wrote else []
-            if t[0] == "p" and t[1].isupper():
-                c += [d for d in readers.get(t, []) if d[0] != own]
-            for d in c:
-                ds[d[0]] = max(ds.get(d[0], 0), d[1])
-        for t in Wr:
-            for d in ([wrote[t]] if t in wrote else []) + readers.get(t, []):
-                ds[d[0]] = max(ds.get(d[0], 0), d[1])
+    for i in order:
+        o = ops[i]
+        e = o["e"]
+        if e is None:
+            continue
+        ds = {}
+        for d in o["pre"]:
+            s, v = ops[d]["sem"]
+            ds[s] = max(ds.get(s, 0), v)
         for s in sorted(ds):
-            if not (e == "P" and s == own):
+            if not (e == "P" and s == "cP"):
                 need(e, (s, ds[s]))
-
-    def op(e, fn, R, Wr):
-        deps(e, R, Wr)
-        fn().then_inc(T.sem["c" + e], 1)
-        cnt["c" + e] += 1
-        me = ("c" + e, cnt["c" + e])
-        for t in R:
-            readers.setdefault(t, []).append(me)
-        for t in Wr:
-            wrote[t] = me
-            readers[t] = []
-
-    def tt(out, a, b, alu, R, Wr):
-        op("V", lambda: V.tensor_tensor(out, a, b, alu), R, Wr)
-
-    def ts(out, a, s1, s2, o0, o1, R, Wr):
-        if o1 is None:
-            op("V", lambda: V.tensor_scalar(out, a, s1, None, o0), R, Wr)
+        if o["kind"] == "op":
+            o["fn"]().then_inc(T.sem["c" + e], 1)
+            cnt["c" + e] += 1
+            o["sem"] = ("c" + e, cnt["c" + e])
         else:
-            op("V", lambda: V.tensor_scalar(out, a, s1, s2, o0, o1), R, Wr)
-
-    def cp(out, a, R, Wr):
-        op("V", lambda: V.tensor_copy(out, a), R, Wr)
-
-    def fill(ap, c, tok):
-        op("V", lambda: V.memset(ap, c), [], [tok])
-
-    def scan(out, d1, o1, R, Wr):
-        op("V", lambda: V.tensor_tensor_scan(out, T.m0[:, :], d1, 0.0, ALU.mult, o1), R + ["m0"], Wr)
-
-    def act(out, a, R, Wr, f=AF.Identity, bias=0.0, scale=1.0):
-        op("A", lambda: A.activation(out, a, f, bias=bias, scale=scale), R, Wr)
-
-    def mm(lst, R, Wr):
-        def fn():
-            for m in lst:
-                i = P.matmul(m[0], m[1], m[2], m[3], m[4])
-            return i
-        op("P", fn, R, Wr)
-
-    def group(out, terms, start=True, stop=True):
-        n = len(terms)
-        return [(out, l, r, start and i == 0, stop and i == n - 1) for i, (l, r) in enumerate(terms)]
-
-    def send(m, t, src, dst, to, R):
-        deps("G", R, [])
-        rid, pid = topo.addr(to)[0:2]
-        g.remote_dma(dst, src, T.sem["r%s%d" % (m, t)], T.sem.sent, pid, rid, topo.mask(core, to))
-        cnt["sent"] += len(topo.engines(core, to))
-
-    for t in range(RO):
-        for m in MSGS:
-            wrote["r%s%d" % (m, t)] = ("r%s%d" % (m, t), len(topo.engines(nxt if m == "w" else prv, core)))
-
-    def sl(buf, t, w=K, a=0, b=None):
-        return buf[:, t * w + a: t * w + (w if b is None else b)]
-
-    def st(buf, t, r):
-        return buf[:, t * K + r:(t + 1) * K:16]
-
-    YT = ["Y0", "Y1", "Y2", "Y3"]
-    cells = T.TB[:, W:W + CELLS]
-    whole = T.TB[:, 0:TBW]
-
-    S.dma_start(T.vi[:, :], T.v0[:, :]).then_inc(T.sem.dv0, 16)
-    S.dma_start(T.CE[:, :], T.ce[:, :]).then_inc(T.sem.dce, 16)
-    A.dma_start(T.zs[:, 0:K], T.z0[:, :]).then_inc(T.sem.dz, 16)
-    A.dma_start(T.PXB[:, 0:W // 2], T.px[:, 0:W // 2]).then_inc(T.sem.dpx, 16)
-    S.dma_start(T.PXB[:, W // 2:W], T.px[:, W // 2:W]).then_inc(T.sem.dpx, 16)
-    wrote.update({"vi": ("dv0", 16), "CE": ("dce", 16), "z0": ("dz", 16), "PXB": ("dpx", 32), "kw": ("dw", 32)})
-
-    ioc = T.IDT[:, 0:256]
-
-    def iota(out, pattern, base, tok):
-        op("G", lambda: g.iota(out, pattern, base, 0, allow_small_or_imprecise_dtypes=True), [], [tok])
-
-    op("G", lambda: g.iota(T.pi[:, :], [[0, 16]], 0, 1), [], ["pi"])
-    iota(ioc, [[1, 256]], 0, "ioc")
-    iota(T.ioa[:, :], [[1, 16], [0, 16]], 0, "ioa")
-    iota(T.iok[:, :], [[0, 16], [1, 16]], 0, "iok")
-    iota(T.JL[:, :], [[0, 16], [-1, 16]], 15, "JL")
-    g.dma_start(T.kp[:, :], T.kap[:, :]).then_inc(T.sem.dw, 16)
-    g.dma_start(T.wv[:, 0:1], T.wu[:, :], allow_slow_non_contiguous=True).then_inc(T.sem.dw, 16)
-    pc, rc, gc_, wc, jc, lc = [T.col[:, i:i + 1] for i in range(6)]
-    fill(T.zs[:, K:K + 16], -1.0, "za0")
-    fill(T.zs[:, K + 16:K + 32], 0.0, "zb0")
-    fill(T.zs[:, K + 32:K + 48], 1.0, "zc0")
-    ts(T.pj[:, 0:1], T.pi[:, 0:1], 15, None, ALU.bitwise_and, None, ["pi"], ["pj0"])
-    ts(T.pj[:, 1:2], T.pi[:, 0:1], 4, None, ALU.arith_shift_right, None, ["pi"], ["pj1"])
-    cp(pc, T.pi[:, 0:1], ["pi"], ["pc"])
-    cp(T.col[:, 1:3], T.pj[:, 0:2], ["pj0", "pj1"], ["rg"])
-    cp(T.vf[:, :], T.vi[:, :], ["vi"], ["vf"])
-    ts(wc, gc_, 16.0, 15.0, ALU.mult, ALU.add, ["rg"], ["wc"])
-    ts(jc, rc, -256.0, 4080.0, ALU.mult, ALU.add, ["rg"], ["jc"])
-    ts(lc, rc, 1024.0, None, ALU.add, None, ["rg"], ["lc"])
-    ts(T.GO32[:, :], T.ioa[:, 0:128], gc_, None, ALU.is_equal, None, ["ioa", "rg"], ["GO32"])
-    ts(T.OH32[:, :], T.iok[:, 0:16], rc, None, ALU.is_equal, None, ["iok", "rg"], ["OH32"])
-    cp(T.bl[:, 16:32], T.vi[:, :], ["vi"], ["blA0"])
-
-    def blocks(out, src):
-        for q in range(8):
-            i = V.tensor_tensor(out[:, 16 * q:16 * q + 16], src, T.GO32[:, 16 * q:16 * q + 16], ALU.mult)
-        return i
-    op("V", lambda: blocks(T.VX, T.vf[:, :]), ["vf", "GO32"], ["VX"])
-    mm(group(T.pS[:, 0:16], [(T.VX[:, :], T.OH32[:, :])]), ["VX", "OH32"], ["pS"])
-    ts(T.I1[:, :], ioc[:, 0:128], pc, None, ALU.is_equal, None, ["ioc", "pc"], ["I1"])
-    ts(T.W4[:, :], ioc[:, 0:144], wc, 4096.0, ALU.is_equal, ALU.mult, ["ioc", "wc"], ["W4"])
-    ts(T.JH[:, :], T.ioa[:, :], -16.0, jc, ALU.mult, ALU.add, ["ioa", "jc"], ["JH"])
-    ts(T.m0[:, :], T.iok[:, :], 0.0, None, ALU.is_gt, None, ["iok"], ["m0"])
-    cp(T.bl[:, 0:16], T.pS[:, 0:16], ["pS"], ["blB0"])
-    ts(T.OH[:, 0:256], T.iok[:, :], rc, None, ALU.is_equal, None, ["iok", "rg"], ["OH"])
-    for w in (256, 512, 1024):
-        cp(T.OH[:, w:2 * w], T.OH[:, 0:w], ["OH"], ["OH"])
-    cp(cells, T.CE[:, :], ["CE"], ["TB"])
-
-    def names(t):
-        for h in range(2):
-            cp(T.Lu[:, 128 * h:128 * h + 128], cells.indirect(T.bl[:, 32 * t + 8 * h:32 * t + 8 * h + 8]),
-               ["TB", "blB%d" % t], ["Lu%d" % h])
-    names(0)
-    cp(T.OH[:, 2048:W], T.OH[:, 0:2048], ["OH"], ["OH"])
-    tok = "ioc"
-    for w in (256, 512, 1024, 2048):
-        act(T.IDT[:, w:2 * w], T.IDT[:, 0:w], ["ioc", tok], ["IDT%d" % w], bias=float(w))
-        tok = "IDT%d" % w
-    act(T.IDT[:, W:TBW], T.IDT[:, 0:TBW - W], [tok], ["IDT"], bias=float(W))
-
-    def late_constants():
-        ts(T.W1[:, :], T.W4[:, :], 2.0 ** -12, None, ALU.mult, None, ["W4"], ["W1"])
-        ts(T.Wu[:, :], T.W1[:, :], T.wv[:, 0:1], None, ALU.mult, None, ["W1", "kw"], ["Wu"])
-        ts(T.DA[0:32, :], T.ioa[0:32, :], T.col[0:32, 0:1], 4096.0, ALU.is_equal, ALU.mult, ["ioa", "pc"], ["DA"])
-        ts(T.NM[:, :], T.OH[:, 0:256], -1.0, 2.0 ** 22, ALU.add, ALU.mult, ["OH"], ["NM"])
-        fill(T.hc[:, 0:16], 1.0, "hca")
-        fill(T.hc[:, 16:32], 0.5, "hcb")
-        ts(T.tri0[:, :], ioc[:, 0:128], pc, 8192.0, ALU.is_gt, ALU.mult, ["ioc", "pc"], ["tri0"])
-        ts(T.c15[:, :], ioc[:, 0:16], 16.0, 15.0, ALU.mult, ALU.add, ["ioc"], ["c15"])
-        ts(T.cl[:, :], ioc[:, 0:16], 16.0, lc, ALU.mult, ALU.add, ["ioc", "lc"], ["cl"])
-        cp(T.NP[:, :], ioc[:, 0:16], ["ioc"], ["NP"])
-        tt(T.TRI[:, :], T.tri0[:, :], T.GO32[:, :], ALU.mult, ["tri0", "GO32"], ["TRI"])
-        ts(T.dm[:, :], T.cl[:, :], 4096.0, None, ALU.add, None, ["cl"], ["dm"])
-        op("V", lambda: blocks(T.KB, T.kp[:, :]), ["kw", "GO32"], ["KB"])
-        for name, src, c in (("I2", "I1", 2.0), ("GO", "GO32", 1.0), ("W8", "W4", 2.0), ("I8n", "I1", -8192.0),
-                             ("I8k", "I1", 8192.0), ("G8k", "GO32", 8192.0), ("I2n", "I1", -2.0), ("I1n", "I1", -1.0),
-                             ("W4n", "W4", -1.0)):
-            act(T[name][:, :], T[src][:, :], [src], [name], scale=c)
-        act(T.DAn[0:32, :], T.DA[0:32, :], ["DA"], ["DAn"], scale=-1.0)
-
-    def wr_(buf, r):
-        return buf[:, 15 - r:143 - r]
-
-    def spread(src, t, w, tok):
-        mm([(T.pX[:, 16 * r:16 * r + 16], T.I1[:, :], src[:, t * w + r:t * w + K:16], True, True) for r in range(16)],
-           [tok, "I1"], ["pX"])
-
-    def sums(src, t, tok):
-        mm([(T.pT[0:16, r:128:16], st(src, t, r), T.GO[:, 0:128:16], True, True) for r in range(16)], [tok, "GO"], ["pT"])
-        act(T.SX[0:16, :], T.pT[0:16, 0:128], ["pT"], ["SX"], bias=-4080.0)
-
-    def values_start(names, ntok):
-        mm([(T.pU[:, :], T.I8n[:, :], T.CC[:, :], True, False), (T.pU[:, 0:K], T.GO32[:, :], names, False, False)],
-           [ntok, "GO32", "I8n", "CC"], ["pU"])
-
-    def big(win, wtok, ybank, yw, mw, after_y=None):
-        cp(T.Y[:, 0:1024], win.indirect(T.Lu[:, 0:64]), [wtok, "Lu0"], ["Y0"])
-        for c in (1, 2, 3):
-            act(T.Y[:, 1024 * c:1024 * c + 1024], win.indirect(T.Lu[:, 64 * c:64 * c + 64]), [wtok, "Lu%d" % (c // 2)], [YT[c]])
-
-        def mins(c):
-            def fn():
-                for k in range(16):
-                    a, b = 1024 * c + k, 1024 * c + 1024
-                    i = V.tensor_tensor(T.MN[:, a:b:16], T.Y[:, a:b:16], T.pX[:, 64 * c:64 * c + 64], ALU.min)
-                return i
-            op("V", fn, [YT[c], "pX"], ["M%d" % c])
-
-        def red(c, src, bank, wn, tok, stop):
-            mm([(T[bank][:, 0:K], wr_(T[wn], r), src[:, 256 * r:256 * r + 256], False, stop and r == 15)
-                for r in range(4 * c, 4 * c + 4)], [tok, wn], [bank])
-        for c in range(4):
-            mins(c)
-        for kind, c in (("y", 0), ("y", 1), ("m", 0), ("y", 2), ("m", 1), ("m", 2), ("y", 3), ("m", 3)):
-            if kind == "m":
-                red(c, T.MN, "pK", mw, "M%d" % c, True)
-            elif ybank is not None:
-                red(c, T.Y, ybank, yw, YT[c], ybank != "pK")
-                if c == 3 and after_y is not None:
-                    after_y()
-
-    def offsets(n, two):
-        src = T.SC[:, 15:16 * n:16]
-        if two:
-            tt(T.oi[:, 0:n], src, T.hc[:, 0:n], ALU.mult, ["SC0", "SC1", "hca", "hcb"], ["oi"])
-        else:
-            cp(T.oi[:, 0:n], src, ["SC0"], ["oi"])
-        ts(T.oj[:, 0:n], T.oi[:, 0:n], 4095, None, ALU.bitwise_and, None, ["oi"], ["oj"])
-        ts(T.off[:, 0:n], T.oj[:, 0:n], -1.0, 4095.0, ALU.mult, ALU.add, ["oj"], ["off"])
-
-    offj = T.off[:, 0:16]
-    ohw = T.OH[:, 0:W]
-
-    def name_row(names, tok):
-        mm(group(T.pR[:, 0:K], [(T.I1[:, :], T.NM[:, :])], stop=False), ["I1", "NM"], ["pR"])
-        tt(T.MS[:, :], ohw.indirect(offj), names[:, :], ALU.mult, ["OH", "off", tok], ["MS"])
-        act(T.oh[:, :], ohw.indirect(offj), ["OH", "off"], ["oh"])
-        mm(group(T.pR[:, 0:K], [(T.GO32[:, :], T.MS[:, :])], start=False), ["GO32", "MS"], ["pR"])
-
-    def kind_row(rec, rtok, npb, nptok, made):
-        if not made:
-            act(npb, T.NP[:, 0:16].indirect(T.nu[:, :]), ["NP", "nu"], [nptok])
-        mm([(T.pU[:, 0:K], T.I8k[:, :], T.oh[:, :], False, False), (T.pU[:, K:2 * K], T.I8k[:, :], T.oh[:, :], False, False),
-            (T.pU[:, 0:K], T.I8k[:, :], npb, False, False), (T.pU[:, K:2 * K], T.I8n[:, :], npb, False, True)]
-           + group(T.pA[:, 0:K], [(T.I1[:, :], rec), (T.I8n[:, :], npb)], stop=False),
-           [nptok, "oh", "I8k", "I8n", rtok], ["pU", "pA"])
-
-    def write(shift, lim, ltok, ob, otok, between):
-        ts(T.ku[:, :], T.keyL[:, :], shift, None, ALU.add, None, ["keyL"], ["ku"])
-        ku = T.ku[:, :]
-        act(ob, whole.indirect(ku), ["TB", "TBd", "ku"], [otok])
-        act(T.OLD[:, :], whole.indirect(ku), ["TB", "TBd", "ku"], ["OLD"])
-        cp(T.kr[:, :], T.IDT[:, 0:TBW].indirect(ku), ["IDT", "ku"], ["kr"])
-        mm(group(T.pR[:, 0:K], [(T.I1[:, :], T.NM[:, :])], stop=False), ["I1", "NM"], ["pR"])
-        mm(group(T.pA[:, 0:K], [(T.I1[:, :], ob)], start=False), [otok], ["pA"])
-        act(T.a1[:, :], T.pA[:, 0:K], ["pA"], ["a1"], bias=M1, scale=HALF)
-        act(T.Ap[:, :], T.a1[:, :], ["a1"], ["Ap"], bias=-M1)
-        cuts = (0, 1, 3, 5, 8, 12, 16)
-        for h in range(6):
-            def fn():
-                for a in range(cuts[h], cuts[h + 1]):
-                    i = V.tensor_scalar(T.E[:, a, 0:K - 16 * a], T.kr[:, 16 * a:K], T.keyL[:, a:a + 1], shift,
-                                        ALU.subtract, ALU.is_equal)
-                return i
-            op("V", fn, ["kr", "keyL"], ["E%d" % h])
-            lst = [(T.pR[:, 16 * a + 16:K], T.G8k[:, :], T.E[:, a, 16:K - 16 * a], False, False)
-                   for a in range(cuts[h], min(cuts[h + 1], 15))]
-            if h == 5:
-                lst.append((T.pR[:, 0:K], T.TRI[:, :], T.E[:, :, 0:16], False, True))
-            mm(lst, ["E%d" % q for q in range(h + 1)] + ["G8k", "TRI"], ["pR"])
-        tt(T.T2[:, :], T.OLD[:, :], T.pU[:, K:2 * K], ALU.subtract, ["OLD", "pU"], ["T2"])
-        tt(T.Q[:, :], T.Ap[:, :], T.pU[:, 0:K], ALU.max, ["Ap", "pU"], ["Q"])
-        scan(T.s2[:, :], T.pR[:, 0:K], ALU.max, ["pR"], ["s2"])
-        tt(T.t1[:, :], T.s2[:, 15:K:16], T.keyL[:, :], ALU.add, ["s2", "keyL"], ["t1"])
-        tt(T.t2[:, :], T.t1[:, :], lim, ALU.min, ["t1", ltok], ["t2"])
-        ts(T.fo[:, :], T.t2[:, :], shift, None, ALU.add, None, ["t2"], ["fo"])
-        between()
-        tt(whole.indirect(T.fo[:, :]), T.T2[:, :], T.Q[:, :], ALU.max, ["fo", "T2", "Q"], ["TB", "TBd"])
-
-    def key_start(terms, R, bank="pK"):
-        mm(group(T[bank][:, 0:K], terms, stop=False), R, [bank])
-
-    jterms = [(T.I1[:, :], T.JH[:, :]), (T.I1[:, :], T.JL[:, :])]
-
-    spread(T.zs, 0, ZW, "z0")
-    key_start(jterms, ["I1", "JH", "JL"])
-    send("z", 0, sl(T.zs, 0, ZW), sl(T.zr, 0, ZW), nxt, ["z0", "za0", "zb0", "zc0"])
-    iota(T.CC[:, :], [[-3, 2], [0, 256]], 2, "CC")
-    iota(T.C2k[:, :], [[0, 256]], 2048, "C2k")
-    iota(T.TB[:, W + CELLS:TBW], [[0, 256]], 0, "TBd")
-
-    for t in range(RO):
-        if t == 0:
-            big(T.PXB[:, 0:W], "PXB", None, None, "W4")
-        else:
-            names(t)
-            big(T.TB[:, 0:W], "TB", None, None, "W4")
-        act(T.Lf[:, :], cells.indirect(T.bl[:, 32 * t + 16:32 * t + 32]), ["TB", "blA%d" % t], ["Lf"])
-        scan(T.SC[:, 0:K], T.pK[:, 0:K], ALU.max, ["pK"], ["SC0"])
-        offsets(16, False)
-        yw = T.Y[:, 0:W]
-        cp(sl(T.xs, t, K, 0, 128), yw.indirect(T.off[:, 0:8]), YT + ["off"], ["xa%d" % t])
-        act(sl(T.xs, t, K, 128, K), yw.indirect(T.off[:, 8:16]), YT + ["off"], ["xb%d" % t])
-        send("x", t, sl(T.xs, t), sl(T.xr, t), nxt, ["xa%d" % t, "xb%d" % t])
-        tt(sl(T.ns, t), ohw.indirect(offj), T.Lf[:, :], ALU.mult, ["OH", "off", "Lf"], ["ns%d" % t])
-        send("n", t, sl(T.ns, t), sl(T.nq, t), nxt, ["ns%d" % t])
-        if t == 0:
-            late_constants()
-            cp(T.TB[:, 0:W // 2], T.PXB[:, 0:W // 2], ["PXB"], ["TB"])
-            act(T.TB[:, W // 2:W], T.PXB[:, W // 2:W], ["PXB"], ["TBh"])
-        rz, rx, u = "rz%d" % t, "rx%d" % t, t + 1
-        na, par, ntx = [sl(T.zs, u, ZW, K + 16 * i, K + 16 * i + 16) for i in range(3)]
-        na0, par0, ntx0 = [sl(T.zr, t, ZW, K + 16 * i, K + 16 * i + 16) for i in range(3)]
-        tt(na, na0, ntx0, ALU.add, [rz], ["za%d" % u])
-        tt(par, par0, ntx0, ALU.is_equal, [rz], ["zb%d" % u])
-        ts(T.thr[:, :], par, 2.0, -12.0, ALU.mult, ALU.add, ["zb%d" % u], ["thr"])
-        x = sl(T.xr, t)
-        key_start([(T.I2[:, :], T.JH[:, :]), (T.I2[:, :], T.JL[:, :])], ["I2", "JH", "JL"])
-        mm(group(T.pS[:, 0:16], [(wr_(T.Wu, a), sl(T.xr, t, K, 16 * a, 16 * a + 16)) for a in range(16)]), [rx, "Wu"], ["pS"])
-        cp(T.bi[:, 0:16], T.pS[:, 0:16], ["pS"], ["bi"])
-        ts(T.bj[:, 0:16], T.bi[:, 0:16], CELLS - 1, None, ALU.bitwise_and, None, ["bi"], ["bj"])
-        cp(T.bl[:, 32 * u:32 * u + 16], T.bj[:, 0:16], ["bj"], ["blB%d" % u])
-        names(u)
-        if t == 0:
-            need("V", wrote["TBh"])
-            need("A", wrote["TBh"])
-        sums(T.xr, t, rx)
-        spread(T.xr, t, K, rx)
-        key_start(jterms + [(T.SX[0:16, :], T.DA[0:16, :])], ["I1", "JH", "JL", "SX", "DA"], "pA")
-        mm(group(T.pT[:, 256:272], [(wr_(T.Wu, r), st(T.xr, t, r)) for r in range(16)]), [rx, "Wu"], ["pT"])
-        values_start(sl(T.nq, t), "rn%d" % t)
-        big(T.TB[:, 0:W], "TB", "pA", "W4", "W8", lambda: act(T.A3[:, :], T.pA[:, 0:K], ["pA"], ["A3"]))
-        cp(T.ai[:, :], T.pT[:, 256:272], ["pT"], ["ai"])
-        ts(T.aj[:, :], T.ai[:, :], CELLS - 1, None, ALU.bitwise_and, None, ["ai"], ["aj"])
-        cp(T.bl[:, 32 * u + 16:32 * u + 32], T.aj[:, :], ["aj"], ["blA%d" % u])
-        ts(T.bb[:, :], T.aj[:, :], float(W), None, ALU.add, None, ["aj"], ["bb"])
-        act(T.Lf[:, :], cells.indirect(T.bl[:, 32 * u + 16:32 * u + 32]), ["TB", "blA%d" % u], ["Lf"])
-        tt(T.nk[:, :], T.pK[:, 0:K], T.A3[:, :], ALU.subtract, ["pK", "A3"], ["nk"])
-        scan(T.SC[:, 0:K], T.nk[:, :], ALU.max, ["nk"], ["SC0"])
-        act(T.sg[:, :], T.nk[:, :], ["nk"], ["sg"], f=AF.Sign, bias=1.0 - 4096.0 * (4080 - TH1 + 1))
-        mm(group(T.pT[:, 0:16], [(T.I1[:, :], T.sg[:, k:K:16]) for k in range(16)]), ["sg"], ["pT"])
-        tt(T.ne[:, :], T.SC[:, 0:K].indirect(T.c15[:, :]), T.nk[:, :], ALU.not_equal, ["SC0", "c15", "nk"], ["ne"])
-        tt(T.ks[:, :], T.ne[:, :], T.pK[:, 0:K], ALU.mult, ["ne", "pK"], ["ks"])
-        tt(ntx, T.pT[:, 0:16], T.thr[:, :], ALU.is_lt, ["pT", "thr"], ["zc%d" % u])
-        scan(T.SC[:, K:2 * K], T.ks[:, :], ALU.max, ["ks"], ["SC1"])
-        nr2 = sl(T.ls, t, LW, K, LW)
-        live = sl(T.ls, t, LW, 0, K)
-        cp(T.nu[:, :], ntx, ["zc%d" % u], ["nu"])
-        act(live, T.NP[:, 0:16].indirect(T.nu[:, :]), ["NP", "nu"], ["la%d" % t])
-        act(nr2, ntx, ["zc%d" % u], ["lb%d" % t], scale=8192.0)
-        offsets(32, True)
-        offm = T.off[:, 16:32]
-        tt(sl(T.fs, t), yw.indirect(offm), x, ALU.max, YT + ["off", rx], ["fs%d" % t])
-        send("f", t, sl(T.fs, t), sl(T.fr, t), nxt, ["fs%d" % t])
-        name_row(T.Lf, "Lf")
-        kind_row(x, rx, live, "la%d" % t, True)
-        tt(sl(T.ms, t), ohw.indirect(offm), T.Lf[:, :], ALU.mult, ["OH", "off", "Lf"], ["ms%d" % t])
-        send("l", t, sl(T.ls, t, LW), sl(T.lr, t, LW), nxt, ["la%d" % t, "lb%d" % t])
-        send("m", t, sl(T.ms, t), sl(T.mr, t), nxt, ["ms%d" % t])
-        scan(T.s2[:, :], T.pR[:, 0:K], ALU.max, ["pR"], ["s2"])
-        tt(T.t1[:, :], T.s2[:, 15:K:16], nr2, ALU.add, ["s2", "lb%d" % t], ["t1"])
-        tt(T.keyL[:, :], T.t1[:, :], T.bb[:, :], ALU.min, ["t1", "bb"], ["keyL"])
-        rf = "rf%d" % t
-        f = sl(T.fr, t)
-
-        def high(src, tok):
-            act(T.a1[:, :], src, [tok], ["a1"], bias=M4096, scale=1.0 + 2.0 ** -21)
-            act(T.hi[:, :], T.a1[:, :], ["a1"], ["hi"], bias=-M4096 - 4096.0)
-
-        def places():
-            c2k = (T.I1[:, :], T.C2k[:, :])
-            mm(group(T.pS[:, 0:K], [c2k], stop=False) + group(T.pZ[:, 0:K], [c2k, (T.I1n[:, :], T.C2k[:, :])], stop=False),
-               ["C2k", "I1", "I1n"], ["pS", "pZ"])
-            mm([(T.pS[:, 16 * r:16 * r + 16], T.KB[:, :], st(T.fr, t, r), False, r == 15) for r in range(16)], [rf, "KB"], ["pS"])
-            high(T.pS[:, 0:K], "pS")
-            mm([(T.pZ[:, 16 * r:16 * r + 16], T.KB[:, :], st(T.fr, t, r), False, False) for r in range(16)], [rf, "KB"], ["pZ"])
-            sums(T.fr, t, rf)
-            mm(group(T.pZ[:, 0:K], [(T.I1n[:, :], T.hi[:, :])], start=False), ["hi"], ["pZ"])
-            spread(T.fr, t, K, rf)
-            key_start(jterms + [(T.SX[0:16, :], T.DAn[0:16, :])], ["I1", "JH", "JL", "SX", "DAn"])
-            mm(group(T.pS[:, 0:K], [c2k, (T.KB[:, :], f)]), [rf], ["pS"])
-        write(0.0, T.dm[:, :], "dm", T.Ob2[:, :], "Ob2", places)
-        cp(T.Lu[:, :], T.pZ[:, 0:K], ["pZ"], ["Lu0", "Lu1"])
-
-        def lane_places():
-            high(T.pS[:, 0:K], "pS")
-            mm(group(T.pT[:, 0:K], [(T.KB[:, :], f), (T.I1n[:, :], T.hi[:, :])]), [rf, "hi"], ["pT"])
-            act(T.Lc[:, :], T.pT[:, 0:K], ["pT"], ["Lc"])
-        big(T.TB[:, 0:W], "TB", "pK", "W4n", "W8", lane_places)
-        values_start(sl(T.mr, t), "rm%d" % t)
-        rl = "rl%d" % t
-        tt(T.dv[:, :], T.cl[:, :], sl(T.lr, t, LW, K, LW), ALU.subtract, ["cl", rl], ["dv"])
-        z0 = sl(T.zr, t, ZW, 0, K)
-        mm(group(T.pS[:, 0:K], [(T.I1[:, :], z0), (T.I8n[:, :], live)])
-           + group(T.pS[:, K:2 * K], [(T.I1[:, :], T.Ob2[:, :]), (T.I8n[:, :], live)]), [rz, "la%d" % t, "Ob2"], ["pS"])
-        scan(T.SC[:, 0:K], T.pK[:, 0:K], ALU.max, ["pK"], ["SC0"])
-        offsets(16, False)
-        name_row(T.Lc, "Lc")
-        far = 4096.0 * (4080 - TH2 + 1)
-        ts(T.nu[:, :], T.SC[:, 15:K:16], far, None, ALU.is_lt, None, ["SC0"], ["nu"])
-        kind_row(f, rf, T.NP3[:, :], "NP3", False)
-        act(T.E12[:, :], T.pS[:, :], ["pS"], ["E12"], f=AF.Relu)
-        tt(sl(T.ws, t), yw.indirect(offj), sl(T.lr, t, LW, 0, K), ALU.mult, YT + ["off", rl], ["ws%d" % t])
-        send("w", t, sl(T.ws, t), sl(T.wr, t), prv, ["ws%d" % t])
-        ts(T.nr[:, :], T.nu[:, :], 8192.0, -4096.0, ALU.mult, ALU.add, ["nu"], ["nr"])
-        scan(T.s2[:, :], T.pR[:, 0:K], ALU.max, ["pR"], ["s2"])
-        cp(T.qi[:, :], T.s2[:, 15:K:16], ["s2"], ["qi"])
-        tt(T.t1[:, :], T.s2[:, 15:K:16], T.nr[:, :], ALU.add, ["s2", "nr"], ["t1"])
-        ts(T.qj[:, :], T.qi[:, :], CELLS - 1, None, ALU.bitwise_and, None, ["qi"], ["qj"])
-        tt(T.t2[:, :], T.t1[:, :], T.qj[:, :], ALU.min, ["t1", "qj"], ["t2"])
-        tt(T.keyL[:, :], T.t2[:, :], T.dv[:, :], ALU.max, ["t2", "dv"], ["keyL"])
-
-        def newz():
-            mm(group(T.pZ[:, 0:K], [(T.I1[:, :], z0), (T.I1[:, :], T.E12[:, 0:K]), (T.I2n[:, :], T.E12[:, K:2 * K])],
-                     stop=False), [rz, "E12", "I2n"], ["pZ"])
-            mm(group(T.pZ[:, 0:K], [(T.I1[:, :], sl(T.wr, t))], start=False), ["rw%d" % t], ["pZ"])
-            act(T.a1[:, :], T.pZ[:, 0:K], ["pZ"], ["a1"], bias=M1, scale=HALF)
-            act(sl(T.zs, u, ZW, 0, K), T.a1[:, :], ["a1"], ["z%d" % u], f=AF.Abs, bias=-M1)
-            if u < RO:
-                send("z", u, sl(T.zs, u, ZW), sl(T.zr, u, ZW), nxt, ["z%d" % u, "za%d" % u, "zb%d" % u, "zc%d" % u])
-                spread(T.zs, u, ZW, "z%d" % u)
-                key_start(jterms, ["I1", "JH", "JL"])
-        write(4096.0, T.cl[:, :], "cl", T.Ob3[:, :], "Ob3", newz)
-
-    def out(e, dst, src, R):
-        deps(e, R, [])
-        s = "outg" if e == "G" else "outs"
-        Q[e].dma_start(dst, src).then_inc(T.sem[s], 16)
-        cnt[s] += 16
-
-    out("G", T.yx[:, :], T.TB[:, 0:W], ["TB"])
-    out("S", T.yc[:, :], cells, ["TB"])
-    cp(T.yvf[:, :], T.aj[:, :], ["aj"], ["yvf"])
-    tt(T.t1[:, :], na, ntx, ALU.add, ["za%d" % RO, "zc%d" % RO], ["t1"])
-    ts(T.au[:, :], T.t1[:, :], -1.0, float(RO), ALU.mult, ALU.add, ["t1"], ["au"])
-    cp(T.ar[:, :], T.IDT[:, 0:256].indirect(T.au[:, :]), ["au", "ioc"], ["ar"])
-    out("A", T.yz[:, :], sl(T.zs, RO, ZW, 0, K), ["z%d" % RO])
-    out("A", T.yv[:, :], T.yvf[:, :], ["yvf"])
-    for q in range(8):
-        out("A" if q % 2 else "S", T.ya[q:q + 1, :], T.ar[16 * q:16 * q + 1, :], ["ar"])
+            o["fn"]()
+            if o["kind"] == "send":
+                cnt["sent"] += o["sem"]
+            elif o["kind"] == "out":
+                cnt["outg" if e == "G" else "outs"] += 16
     for s in ("cV", "cA", "cP", "cG", "sent", "outs", "outg"):
         need("G", (s, cnt[s]))

@@ -11,11 +11,18 @@ M1 = 1.5 * 2.0 ** 23
 M1024 = 1.5 * 2.0 ** 33
 M4096 = 1.5 * 2.0 ** 35
 HALF = 0.5 - 2.0 ** -12
-ZW, MW = 304, 272
+XW, MW = 512, 304
 TOP = 2.0 ** 24 - 1
-VSHARE = ((64, 0), (32, 0), (64, 0))
-LOOK, PASSES, MG, XV, HV = 0.25, 3, 4, (0, 0), (0, 0)
-HOP, FLIGHT, ISSUE = 130, 4500, 600
+XPARTS = ((0, 2), (2, 4))
+VSHARE = ((1, 0, 1, 0), (1, 0, 1, 0), (1, 1, 1, 0))
+WIDE = ((1, 3), (1, 3), (1,))
+JOIN, MG, XV, HV, ZJOIN, LIST, GUARD, WV = 1, 4, (0, 0), (0, 0), 0, 0, 1, 2
+MERGE = ()
+RELAYED, HAND = ("z", "n"), 3500
+BON = {"x": 1000, "b": 0, "f": 0, "p": 0, "w": 0, "t0": 0, "lf": 0, "z": -3000}
+LOOKS, PASSES = (0.25,), 3
+HOP, FLIGHT, ISSUE = 230, 5000, 800
+LOADS = (2200, 4000, 2400, 6000, 3500)
 
 
 def _s(cols, dtype):
@@ -25,48 +32,65 @@ def _s(cols, dtype):
 BF, F32, I32, U16, F16 = "bfloat16", "float32", "int32", "uint16", "float16"
 SCRATCH = {
     "TB": _s(TBW, F32), "PXB": _s(W, BF), "CE": _s(CELLS, I32), "NP": _s(16, BF), "OH": _s(YW, BF),
-    "Y0": _s(YW, BF), "Y1": _s(YW, BF), "MN": _s(W, BF), "E": ("sbuf", [128, 16, 256], BF), "YC": _s(CELLS, F32),
-    "vi": _s(16, I32), "VX": _s(256, F16), "kp": _s(16, BF), "wv": _s(8, BF), "KB": _s(128, BF), "KB2": _s(128, BF),
+    "Y0": _s(YW, BF), "Y1": _s(YW, BF), "MN": _s(W, BF), "E": ("sbuf", [128, 16, 256], BF),
+    "YC": _s(CELLS, F32), "xT": _s(128, BF), "SEL": _s(1024, BF),
+    "vi": _s(16, I32), "VX": _s(512, F16), "kp": _s(16, BF), "wv": _s(8, BF), "KB": _s(128, BF), "KB2": _s(128, BF),
     "pi": _s(16, I32), "pj": _s(16, I32), "col": _s(16, F32), "ioc": _s(256, F32), "ioa": _s(128, F32), "iok": _s(128, F32),
-    "ioe": _s(128, F32), "GE": _s(128, BF), "RS": _s(8, BF), "rep": _s(16, U16), "repf": _s(16, F32),
+    "ioe": _s(128, F32), "GE": _s(128, BF), "RS": _s(8, BF), "rep": _s(8, U16),
     "W1": _s(144, BF), "W4": _s(144, BF), "W8": _s(144, BF), "W4n": _s(144, BF), "Wu": _s(144, BF),
-    "GO": _s(128, BF), "GOn": _s(128, BF), "G8k": _s(128, BF), "G8n": _s(128, BF), "TRI": _s(128, BF), "tri0": _s(128, BF),
-    "I1": _s(128, BF), "I2": _s(128, BF), "I2n": _s(128, BF), "I8k": _s(128, BF), "I8n": _s(128, BF), "I1n": _s(128, BF),
+    "GO": _s(128, BF), "GOn": _s(128, BF), "G8n": _s(128, BF), "TRI": _s(128, BF),
+    "I1": _s(128, BF), "I2": _s(128, BF), "I2n": _s(128, BF), "I1n": _s(128, BF),
     "I32": _s(128, F32), "J32": _s(128, F32), "one": _s(128, BF), "CK": _s(512, BF),
-    "NM": _s(128, BF), "m0": _s(128, BF), "JH": _s(128, BF), "JL": _s(128, BF), "RR": _s(256, F32),
+    "NM": _s(256, BF), "m0": _s(128, BF), "JH": _s(128, BF), "JL": _s(128, BF), "RR": _s(256, F32),
     "DA": _s(128, F32), "DAn": _s(128, F32), "c15": _s(8, U16), "hc": _s(16, F32),
     "bB": _s(16 * (RO + 1), U16), "bA": _s(16 * (RO + 1), U16), "bC": _s(16, U16),
     "bi": _s(32, I32), "bj": _s(32, I32), "yvf": _s(16, F32), "thr": _s(16, F32), "dk": _s(16, F32),
     "Lu": _s(256, U16), "Lf": _s(256, F32), "ck": _s(256, F32), "SX": _s(256, F32), "A3": _s(256, F32), "nk": _s(256, F32),
-    "SC": _s(512, F32), "ne": _s(256, BF), "ks": _s(256, F32), "sg": _s(256, BF), "cs": _s(256, BF),
-    "oi": _s(32, I32), "oj": _s(32, I32), "off": _s(32, U16), "ofm": _s(16, U16), "nu": _s(16, U16),
+    "SC": _s(768, F32), "ne": _s(256, BF), "ks": _s(256, F32), "sg": _s(256, BF), "cs": _s(256, BF),
+    "oi": _s(48, I32), "oj": _s(48, I32), "off": _s(16, U16), "of2": _s(32, U16), "nu": _s(16, U16),
     "MS": _s(256, F16), "kr": _s(256, F16), "s1": _s(256, F32), "s2": _s(256, F32), "ku": _s(16, U16), "fo": _s(16, U16),
     "oh": _s(256, BF), "live": _s(256, BF), "yj": _s(256, BF), "np3": _s(256, BF), "OLD": _s(256, F32), "sel": _s(256, F32),
-    "a1": _s(256, F32), "a2": _s(256, F32), "a3": _s(256, F32), "Hs": _s(256, F32), "Cs": _s(256, F32), "Q": _s(256, F32),
+    "a1": _s(256, F32), "a2": _s(256, F32), "Hs": _s(256, F32), "Cs": _s(256, F32), "Q": _s(256, F32),
     "hi": _s(256, BF), "md": _s(256, F32), "Lcc": _s(256, F32), "E12": _s(512, BF),
-    "t1": _s(16, F32), "au": _s(16, U16), "ar": _s(256, F32),
-    "zs": _s(ZW * (RO + 1), BF), "xs": _s(K * RO, BF), "ns": _s(K * RO, F16), "fs": _s(K * RO, BF),
-    "ms": _s(MW * RO, F16), "ws": _s(K * RO, BF),
-    "zr": _s(ZW * RO, BF), "xr": _s(K * RO, BF), "nr": _s(K * RO, F16), "fr": _s(K * RO, BF),
-    "mr": _s(MW * RO, F16), "wr": _s(K * RO, BF),
+    "t1": _s(16, F32), "au": _s(16, U16), "ar": _s(256, F32), "ckl": _s(16, F32), "kl": _s(16, F32),
+    "xs": _s(XW * (RO + 1), BF), "ns": _s(K * RO, F16), "fs": _s(K * RO, BF), "ms": _s(MW * RO, F16), "ws": _s(K * RO, BF),
+    "xr": _s(XW * RO, BF), "nr": _s(K * RO, F16), "fr": _s(K * RO, BF), "mr": _s(MW * (RO + 1), F16), "wr": _s(K * RO, BF),
 }
 for _b in ("pX0", "pX1", "pK0", "pK1", "pU0", "pU1", "pR0", "pR1"):
     SCRATCH[_b] = ("psum", [128, 512], F32)
-MSGS = ("z", "x0", "x1", "n", "f0", "f1", "m", "w0", "w1")
+MSGS = ("z", "x0", "x1", "x2", "x3", "n", "f0", "f1", "m", "w0", "w1")
 SEMAPHORES = (["cV", "cA", "cP", "cG", "sent", "dv0", "dce", "dz", "dpx", "dw", "outs", "outg"]
-              + ["r%s_%d" % (m, t) for m in MSGS for t in range(RO)])
+              + ["r%s_%d" % (m, t) for m in MSGS for t in range(RO)] + ["h%s_%d" % (m, t) for m in "znm" for t in range(RO)])
 
 
 def rank_program(g, core, T, topo):
+    def relay(r):
+        own, to = T.cores[r], T.cores[(r + 1) % N]
+        return [c for c in topo.cores_of(own) if c not in T.cores and topo.die(c) != topo.die(own) and topo.may_write(c, to)][0]
+
+    def inner(r):
+        own = T.cores[r]
+        return [e for e in topo.engines(own, relay(r)) if e not in topo.engines(own, T.cores[(r + 1) % N])]
+
     rank = T.rank_of(core)
     if rank is None:
+        for r in range(N):
+            if RELAYED and core == relay(r):
+                to = T.cores[(r + 1) % N]
+                rid, pid = topo.addr(to)[0:2]
+                for t in range(RO):
+                    for m in RELAYED:
+                        ap = {"z": T.xr[:, XW * t + K:XW * t + XW], "n": T.nr[:, K * t:K * t + K], "m": T.mr[:, MW * t:MW * t + MW]}[m]
+                        g.wait_ge(T.sem["h%s_%d" % (m, t)], len(inner(r)))
+                        g.remote_dma(ap, ap, T.sem["r%s_%d" % (m, t)], T.sem.sent, pid, rid, topo.mask(core, to))
+                g.wait_ge(T.sem.sent, RO * len(RELAYED) * len(topo.engines(core, to)))
         return
     nxt, prv = T.cores[(rank + 1) % N], T.cores[(rank - 1) % N]
     assert topo.may_write(core, nxt) and topo.may_write(core, prv)
     V, A, P, S = g.vector, g.scalar, g.tensor, g.sync
     Q = {"V": V, "A": A, "P": P, "G": g, "S": S}
 
-    ops, wrote, readers = [], {}, {}
+    ops, wrote, readers, lines, plus = [], {}, {}, {}, [0]
 
     def record(e, fn, R, Wr, cost, kind="op", sem=None):
         pre = set()
@@ -78,7 +102,8 @@ def rank_program(g, core, T, topo):
         for t in Wr:
             pre.update(([wrote[t]] if t in wrote else []) + readers.get(t, []))
         me = len(ops)
-        ops.append({"e": e, "fn": fn, "pre": sorted(pre), "cost": cost, "kind": kind, "sem": sem})
+        ops.append({"e": e, "fn": fn, "pre": sorted(pre), "cost": cost, "kind": kind, "sem": sem, "plus": plus[0],
+                    "tag": (Wr or R or ["-"])[0]})
         for t in (R if kind == "op" else []):
             readers.setdefault(t, []).append(me)
         for t in Wr:
@@ -86,15 +111,17 @@ def rank_program(g, core, T, topo):
             readers[t] = []
         return me
 
-    lines = {}
-
     def in_line(name):
         if name in lines:
             ops[-1]["line"] = [lines[name]]
         lines[name] = len(ops) - 1
 
+    def behind(tok):
+        if GUARD:
+            ops[-1]["line"] = ops[-1].get("line", []) + [wrote[tok]]
+
     def gat(n):
-        return 70 + 1.56 * n
+        return 70 + 1.5 * n
 
     def tt(out, a, b, alu, R, Wr, c=64):
         record("V", lambda: V.tensor_tensor(out, a, b, alu), R, Wr, c)
@@ -108,19 +135,19 @@ def rank_program(g, core, T, topo):
     def cp(out, a, R, Wr, c=64):
         record("V", lambda: V.tensor_copy(out, a), R, Wr, c)
 
-    def fill(ap, c, tok):
-        record("V", lambda: V.memset(ap, c), [], [tok], 64)
+    def fill(ap, c, tok, cost=64):
+        record("V", lambda: V.memset(ap, c), [], [tok], cost)
 
     def scan(out, d0, d1, o0, o1, R, Wr, c=HN):
         record("V", lambda: V.tensor_tensor_scan(out, d0, d1, 0.0, o0, o1), R, Wr, c)
 
-    def act(out, a, R, Wr, f=AF.Identity, bias=0.0, scale=1.0, c=HN):
-        record("A", lambda: A.activation(out, a, f, bias=bias, scale=scale), R, Wr, c)
+    def act(out, a, R, Wr, f=AF.Identity, c=HN, **kw):
+        record("A", lambda: A.activation(out, a, f, **kw), R, Wr, c)
 
     def mm(lst, R, Wr, c=None):
         def fn():
             for m in lst:
-                i = P.matmul(m[0], m[1], m[2], m[3], m[4])
+                i = P.matmul(m[0], m[1], m[2], bool(m[3]), bool(m[4]))
             return i
         record("P", fn, R, Wr, 64 * len(lst) if c is None else c)
 
@@ -132,21 +159,31 @@ def rank_program(g, core, T, topo):
         record("G", lambda: g.iota(out, pattern, base, 0, allow_small_or_imprecise_dtypes=True), [], [tok], 160 + 2 * n)
 
     def send(m, t, src, dst, R):
-        to, name = (prv if m[0] == "w" else nxt), "r%s_%d" % (m, t)
+        name = "r%s_%d" % (m, t)
+        if m in RELAYED:
+            to, first, engines, last = relay(rank), "h%s_%d" % (m, t), inner(rank), relay((rank - 1) % N)
+        else:
+            to, first, last = (prv, name, nxt) if m[0] == "w" else (nxt, name, prv)
+            engines = topo.engines(core, to)
         rid, pid = topo.addr(to)[0:2]
-        i = record("G", lambda: g.remote_dma(dst, src, T.sem[name], T.sem.sent, pid, rid, topo.mask(core, to)), R, [],
-                   ISSUE, "send", len(topo.engines(core, to)))
-        record(None, None, [], [name], FLIGHT, "land", (name, len(topo.engines(nxt if m[0] == "w" else prv, core))))
+        i = record("G", lambda: g.remote_dma(dst, src, T.sem[first], T.sem.sent, pid, rid, sum(1 << e for e in engines)), R, [],
+                   ISSUE, "send", len(engines))
+        if m in RELAYED:
+            in_line("relayed")
+        record(None, None, [], [name], FLIGHT + HAND * (m in RELAYED), "land", (name, len(topo.engines(last, core))))
         ops[-1]["pre"] = [i]
 
     def load(e, dst, src, sem, total, tok, cost, **kw):
         i = record(e, lambda: Q[e].dma_start(dst, src, **kw).then_inc(T.sem[sem], 16), [], [], 60, "dma")
+        in_line("loads" + e)
         if tok is not None:
             record(None, None, [], [tok], cost, "land", (sem, total))
             ops[-1]["pre"] = list(range(i + 1 - total // 16, i + 1))
 
-    def store(e, dst, src, R):
-        record(e, lambda: Q[e].dma_start(dst, src).then_inc(T.sem["outg" if e == "G" else "outs"], 16), R, [], 60, "out")
+    def store(e, dst, src, R, cost=2000):
+        i = record(e, lambda: Q[e].dma_start(dst, src).then_inc(T.sem["outg" if e == "G" else "outs"], 16), R, [], 60, "out")
+        record(None, None, [], [], cost, "land")
+        ops[-1]["pre"] = [i]
 
     def sl(buf, t, w=K, a=0, b=None):
         return buf[:, t * w + a: t * w + (w if b is None else b)]
@@ -154,45 +191,48 @@ def rank_program(g, core, T, topo):
     def hf(buf, h, t=0, w=K):
         return buf[:, t * w + HN * h:t * w + HN * h + HN]
 
-    def hl(buf, h, t=0):
-        return buf[:, 16 * t + HA * h:16 * t + HA * h + HA]
+    def hl(buf, h):
+        return buf[:, HA * h:HA * h + HA]
 
     def dg(buf, h, a=0):
         return buf[:, a + HN * h + 15:a + HN * h + HN:16]
+
+    def full(name):
+        return T[name][:, :]
+
+    def counts(buf, t):
+        return [sl(buf, t, MW, K + 16 * i, K + 16 * i + 16) for i in range(3)]
 
     cells = T.TB[:, W:SP]
     Y = (T.Y0, T.Y1)
     ohw = T.OH[:, 0:YW]
 
-    load("S", T.vi[:, :], T.v0[:, :], "dv0", 16, "vi", 2400)
-    load("S", T.CE[:, :], T.ce[:, :], "dce", 16, "CE", 5000)
-    load("A", T.zs[:, 0:K], T.z0[:, :], "dz", 16, "z0", 2600)
+    load("S", T.vi[:, :], T.v0[:, :], "dv0", 16, "vi", LOADS[0])
+    load("S", T.CE[:, :], T.ce[:, :], "dce", 16, "CE", LOADS[1])
+    load("A", T.xs[:, K:XW], T.z0[:, :], "dz", 16, "z0", LOADS[2])
     load("A", T.PXB[:, 0:W // 2], T.px[:, 0:W // 2], "dpx", 32, None, 0)
-    load("S", T.PXB[:, W // 2:W], T.px[:, W // 2:W], "dpx", 32, "PXB", 9000)
+    load("S", T.PXB[:, W // 2:W], T.px[:, W // 2:W], "dpx", 32, "PXB", LOADS[3])
     load("G", T.kp[:, :], T.kap[:, :], "dw", 32, None, 0)
-    load("G", T.wv[:, 0:1], T.wu[:, :], "dw", 32, "kw", 4000, allow_slow_non_contiguous=True)
+    load("G", T.wv[:, 0:1], T.wu[:, :], "dw", 32, "kw", LOADS[4], allow_slow_non_contiguous=True)
     wrote["z0_0"] = wrote["z1_0"] = wrote["z0"]
 
     record("G", lambda: g.iota(T.pi[:, :], [[0, 16]], 0, 1), [], ["pi"], 200)
     iota(T.ioc[:, :], [[1, 256]], 0, "ioc", 256)
     iota(T.ioe[:, :], [[1, 16], [0, 8]], 0, "ioe", 128)
+    iota(T.JH[:, :], [[-16, 8], [0, 16]], 0, "JH", 128)
     iota(T.ioa[:, :], [[1, 8], [0, 16]], 0, "ioa", 128)
     iota(T.iok[:, :], [[0, 8], [1, 16]], 0, "iok", 128)
     iota(T.JL[:, :], [[0, 8], [-1, 16]], 15, "JL", 128)
     iota(T.TB[:, W + 1:SP:2], [[2, CELLS]], 2048, "TBo", CELLS)
     iota(T.TB[:, SP:TBW], [[0, K]], 0, "TBd", K)
+    iota(T.SEL[:, :], [[1, 8], [16, 8], [0, 16]], 8, "SEL", 1024)
     pc, rc, gc_, ec, sc_, qc, wc, jc, uc, nc = [T.col[:, i:i + 1] for i in range(10)]
-    fill(T.zs[:, K:K + 16], -1.0, "za0")
-    fill(T.zs[:, K + 16:K + 32], 0.0, "zb0")
-    fill(T.zs[:, K + 32:K + 48], 1.0, "zc0_0")
-    wrote["zc1_0"] = wrote["zc0_0"]
+    for i, (ap, c) in enumerate(zip(counts(T.mr, RO), (-1.0, 0.0, 1.0))):
+        fill(ap, c, "first%d" % i)
     pi = T.pi[:, 0:1]
     cp(T.pj[:, 0:1], pi, ["pi"], ["pj0"])
-    ts(T.pj[:, 1:2], pi, 15, None, ALU.bitwise_and, None, ["pi"], ["pj1"])
-    ts(T.pj[:, 2:3], pi, 4, None, ALU.arith_shift_right, None, ["pi"], ["pj2"])
-    ts(T.pj[:, 3:4], pi, 1, None, ALU.bitwise_and, None, ["pi"], ["pj3"])
-    ts(T.pj[:, 4:5], pi, 15, 1, ALU.bitwise_and, ALU.arith_shift_right, ["pi"], ["pj4"])
-    ts(T.pj[:, 5:6], pi, 7, None, ALU.bitwise_and, None, ["pi"], ["pj5"])
+    for i, (mask, shift) in enumerate(((15, 0), (127, 4), (1, 0), (15, 1), (7, 0))):
+        ts(T.pj[:, i + 1:i + 2], pi, mask, shift, ALU.bitwise_and, ALU.arith_shift_right, ["pi"], ["pj%d" % (i + 1)])
     cp(T.col[:, 0:6], T.pj[:, 0:6], ["pj%d" % i for i in range(6)], ["col"])
     ts(wc, gc_, 16.0, 15.0, ALU.mult, ALU.add, ["col"], ["wc"])
     ts(jc, rc, -128.0, 4080.0 - PAD, ALU.mult, ALU.add, ["col"], ["jc"])
@@ -200,34 +240,37 @@ def rank_program(g, core, T, topo):
     ts(nc, rc, -1.0, -4096.0, ALU.mult, ALU.add, ["col"], ["nc"])
     ts(T.GE[:, :], T.ioe[:, :], uc, None, ALU.is_equal, None, ["ioe", "uc"], ["GE"], 128)
     ts(T.RS[:, :], T.ioc[:, 0:8], sc_, None, ALU.is_equal, None, ["ioc", "col"], ["RS"])
-    ts(T.rep[:, :], T.ioe[:, 0:16], 8.0, qc, ALU.mult, ALU.add, ["ioe", "col"], ["rep"])
+    ts(T.rep[:, 0:8], T.ioe[:, 0:8], qc, None, ALU.add, None, ["ioe", "col"], ["rep"])
     for h in range(2):
-        tt(hf(T.VX, h), T.vi[:, 0:16].indirect(hl(T.rep, h)), T.GE[:, :], ALU.mult, ["vi", "rep", "GE"], ["VX%d" % h], gat(HN))
-        mm(group(T["pU%d" % h][:, 0:HA], [(hf(T.VX, h), T.RS[:, :])]), ["VX%d" % h, "RS"], ["pU%d" % h], 32)
-        cp(hl(T.bB, h), T["pU%d" % h][:, 0:HA], ["pU%d" % h], ["bB%d_0" % h])
+        bank = "pU%d" % h
+        tt(hf(T.VX, h), hl(T.vi, h).indirect(T.rep[:, 0:8]), T.GE[:, :], ALU.mult, ["vi", "rep", "GE"], ["VX%d" % h], gat(HN))
+        mm(group(T[bank][:, 0:HA], [(hf(T.VX, h), T.RS[:, :])]), ["VX%d" % h, "RS"], [bank], 32)
+        cp(hl(T.bB, h), T[bank][:, 0:HA], [bank], ["bB%d_0" % (2 * h), "bB%d_0" % (2 * h + 1)])
     ts(T.bA[:, 0:16], T.vi[:, :], 2.0, None, ALU.mult, None, ["vi"], ["bA0"])
     cp(T.TB[:, W:SP:2], T.CE[:, :], ["CE"], ["TBc"], 1024)
     ts(T.I1[:, :], T.ioc[:, 0:128], pc, None, ALU.is_equal, None, ["ioc", "col"], ["I1"], 128)
     ts(T.W4[:, :], T.ioc[:, 0:144], wc, 4096.0, ALU.is_equal, ALU.mult, ["ioc", "wc"], ["W4"], 144)
-    ts(T.JH[:, :], T.ioa[:, :], -16.0, jc, ALU.mult, ALU.add, ["ioa", "jc"], ["JH"], 128)
+    ts(T.JH[:, :], T.JH[:, :], jc, None, ALU.add, None, ["JH", "jc"], ["JH"])
     ts(T.m0[:, :], T.iok[:, :], 0.0, None, ALU.is_gt, None, ["iok"], ["m0"], 128)
     ts(T.OH[:, PAD:PAD + 128], T.iok[:, :], rc, None, ALU.is_equal, None, ["iok", "col"], ["OH"], 128)
-    ts(T.NM[:, :], T.OH[:, PAD:PAD + 128], -1.0, 2.0 ** 22, ALU.add, ALU.mult, ["OH"], ["NM"])
     for w in (128, 256, 512, 1024):
         cp(T.OH[:, PAD + w:PAD + 2 * w], T.OH[:, PAD:PAD + w], ["OH"], ["OH"], w // 2)
+    ts(T.NM[:, :], T.OH[:, PAD:PAD + K], -1.0, 2.0 ** 22, ALU.add, ALU.mult, ["OH"], ["NM"], 128)
+    NM1 = T.NM[:, 0:HN]
     for buf, tok in ((T.OH, "OHz"), (T.Y0, "Yz0"), (T.Y1, "Yz1")):
         fill(buf[:, 0:PAD], 0.0, tok)
     ts(T.GO[:, :], T.ioa[:, :], gc_, None, ALU.is_equal, None, ["ioa", "col"], ["GO"], 128)
     ts(T.W1[:, :], T.W4[:, :], 2.0 ** -12, None, ALU.mult, None, ["W4"], ["W1"])
     ts(T.Wu[:, :], T.W1[:, :], T.wv[:, 0:1], None, ALU.mult, None, ["W1", "kw"], ["Wu"])
     ts(T.DA[0:32, :], T.ioa[0:32, :], T.col[0:32, 0:1], 4096.0, ALU.is_equal, ALU.mult, ["ioa", "col"], ["DA"], 128)
+    ts(T.SEL[:, :], T.SEL[:, :], pc, None, ALU.is_equal, None, ["SEL", "col"], ["SEL"], 512)
     fill(T.hc[:, 0:HA], 1.0, "hca")
     fill(T.hc[:, HA:16], 0.5, "hcb")
-    ts(T.tri0[:, :], T.ioc[:, 0:128], pc, -8192.0, ALU.is_gt, ALU.mult, ["ioc", "col"], ["tri0"], 128)
-    tt(T.TRI[:, :], T.tri0[:, :], T.GO[:, :], ALU.mult, ["tri0", "GO"], ["TRI"], 256)
+    ts(T.TRI[:, :], T.ioc[:, 0:128], pc, -8192.0, ALU.is_gt, ALU.mult, ["ioc", "col"], ["TRI"], 128)
+    tt(T.TRI[:, :], T.TRI[:, :], T.GO[:, :], ALU.mult, ["TRI", "GO"], ["TRI"], 256)
     ts(T.c15[:, :], T.ioc[:, 0:HA], 16.0, 15.0, ALU.mult, ALU.add, ["ioc"], ["c15"])
-    cp(T.NP[:, :], T.ioc[:, 0:16], ["ioc"], ["NP"])
-    record("V", lambda: V.memset(T.RR[:, :], 2.0 ** 26), [], ["RR"], 256)
+    ts(T.NP[:, :], T.ioc[:, 0:16], 8192.0, None, ALU.mult, None, ["ioc"], ["NP"])
+    fill(T.RR[:, :], 2.0 ** 26, "RR", 256)
     ts(T.RR[:, 0:K:16], T.ioc[:, 0:16], -16.0, nc, ALU.mult, ALU.add, ["ioc", "nc"], ["RR"])
     fill(T.one[0:2, :], 1.0, "one")
     fill(T.CK[0:2, 0:256], 0.5, "CK")
@@ -239,294 +282,388 @@ def rank_program(g, core, T, topo):
             i = V.tensor_tensor(T.KB[:, 16 * q:16 * q + 16], T.kp[:, :], T.GO[:, 16 * q:16 * q + 16], ALU.mult)
         return i
     record("V", blocks, ["kw", "GO"], ["KB"], 512)
-    for name, src, c in (("I2", "I1", 2.0), ("W8", "W4", 2.0), ("I8n", "I1", -8192.0), ("I8k", "I1", 8192.0),
-                         ("G8k", "GO", 8192.0), ("G8n", "GO", -8192.0), ("GOn", "GO", -1.0), ("I2n", "I1", -2.0),
+    for name, src, c in (("I2", "I1", 2.0), ("W8", "W4", 2.0), ("G8n", "GO", -8192.0), ("GOn", "GO", -1.0), ("I2n", "I1", -2.0),
                          ("I1n", "I1", -1.0), ("W4n", "W4", -1.0), ("I32", "I1", 1.0), ("J32", "I1", -2.0), ("KB2", "KB", 2.0)):
         act(T[name][:, :], T[src][:, :], [src], [name], scale=c)
     act(T.DAn[0:32, :], T.DA[0:32, :], ["DA"], ["DAn"], scale=-1.0)
+    I1, I1n, GO, GOn = full("I1"), full("I1n"), full("GO"), full("GOn")
 
     def const(i, rows=1):
         return (T.one[0:rows, :], T.CK[0:rows, 128 * i:128 * i + 128])
 
-    def full(name):
-        return T[name][:, :]
-
     def wr_(buf, r):
         return buf[:, 15 - r:143 - r]
 
-    def reorder(out, lhs, src, c0, start, stop):
-        return [(out[:, a:HN:HA], lhs, src[:, c0 + 16 * a:c0 + 16 * a + 16], start, stop and (start or a == HA - 1))
-                for a in range(HA)]
+    def reorder2(out, lhs, src, stop):
+        return [(out[:, a:HN:HA], lhs, src[:, 16 * a:16 * a + 16], False, stop and a == HA - 1) for a in range(HA)]
 
-    def spread(h, src, c0, tok):
-        mm(reorder(T["pX%d" % h], full("I1"), src, c0, True, True), [tok, "I1"], ["pX%d" % h], 256)
+    def spread(step, q, src, tok):
+        c = q % 2
+        bank = "pX%d" % c
+        if q in WIDE[step]:
+            mm([(T[bank][:, 0:128], src, I1, True, True)], [tok, "I1"], [bank])
+            act(full("xT"), T[bank][:, 0:128], [bank], ["xT"])
+            for i, bk in enumerate(("pU%d" % (q // 2), bank)):
+                mm([(T[bk][:, :], full("xT"), T.SEL[:, 512 * i:512 * i + 512], True, True)], ["xT", "SEL"], [bk], 256)
+        else:
+            mm([(T[bank][:, a:64:HA], I1, src[:, 16 * a + 8 * c:16 * a + 8 * c + 8], True, True) for a in range(HA)],
+               [tok, "I1"], [bank], 256)
 
-    def sums(h, src, c0, tok):
+    def sums(h, src, toks):
         u = T["pU%d" % h]
-        mm([(u[0:HA, 128 + r:256:16], src[:, c0 + r:c0 + HN:16], T.GO[:, 0:128:16], True, True) for r in range(16)],
-           [tok, "GO"], ["pU%d" % h], 128)
+        mm([(u[0:HA, 128 + r:256:16], src[:, r:HN:16], T.GO[:, 0:128:16], True, True) for r in range(16)],
+           toks + ["GO"], ["pU%d" % h], 128)
         act(T.SX[0:HA, HN * h:HN * h + HN], u[0:HA, 128:256], ["pU%d" % h], ["SX%d" % h], bias=-4080.0)
 
-    def key_start(bank, one):
-        mm(group(T[bank][:, 0:HN], [(full(one), full("JH")), (full(one), full("JL"))], stop=False), [one, "JH", "JL"], [bank])
+    def key_start(bank, one, a=0, b=HN):
+        mm(group(T[bank][:, a:b], [(full(one), T.JH[:, a:b]), (full(one), T.JL[:, a:b])], stop=False), [one, "JH", "JL"], [bank],
+           b - a)
 
-    def names(h, win, wtok, t):
-        cp(hf(T.Lu, h), win.indirect(hl(T.bB, h, t)), wtok + ["bB%d_%d" % (h, t)], ["Lu%d" % h], gat(HN))
+    def names(q0, q1, win, wtok, t):
+        cp(T.Lu[:, 64 * q0:64 * q1], win.indirect(T.bB[:, 16 * t + 4 * q0:16 * t + 4 * q1]),
+           wtok + ["bB%d_%d" % (q, t) for q in range(q0, q1)], ["Lu%d" % q for q in range(q0, q1)], gat(64 * (q1 - q0)))
 
-    def ytoks(h):
-        return ["Y%d_%d" % (h, q) for q in range(4)] + ["Yz%d" % h]
+    def ytoks(h, q1=2):
+        return ["Y%d_%d" % (h, i) for i in range(2 * q1)] + ["Yz%d" % h]
 
-    def big(step, h, win, wtok, ybank, yw, mw, sw=None):
-        for q in range(4):
-            o, i = Y[h][:, PAD + 512 * q:PAD + 512 * q + 512], win.indirect(T.Lu[:, HN * h + 32 * q:HN * h + 32 * q + 32])
-            if 32 * q < VSHARE[step][h]:
-                cp(o, i, wtok + ["Lu%d" % h], ["Y%d_%d" % (h, q)], gat(512))
+    def big(step, q, last, win, wtok, ybank, yw, mw, sw=None):
+        h, c = q // 2, q % 2
+        px_, kb, y0, m0_ = "pX%d" % c, "pK%d" % h, PAD + 1024 * c, 1024 * q
+        yt = ["Y%d_%d" % (h, 2 * c + i) for i in range(2)]
+        for i in range(2):
+            o, src = Y[h][:, y0 + 512 * i:y0 + 512 * i + 512], win.indirect(T.Lu[:, 64 * q + 32 * i:64 * q + 32 * i + 32])
+            if i < VSHARE[step][q]:
+                cp(o, src, wtok + ["Lu%d" % q], [yt[i]], gat(512))
             else:
-                act(o, i, wtok + ["Lu%d" % h], ["Y%d_%d" % (h, q)], c=gat(512))
+                act(o, src, wtok + ["Lu%d" % q], [yt[i]], c=gat(512))
                 in_line("gathers")
-        px_, kb = "pX%d" % h, "pK%d" % h
-        for c in range(2):
-            yt = ["Y%d_%d" % (h, 2 * c), "Y%d_%d" % (h, 2 * c + 1)]
-            if ybank is not None:
-                if c == 1:
-                    mm([(T[ybank][:, 0:HN], T.SX[0:HA, HN * h:HN * h + HN], T[sw][0:HA, :], False, False)], ["SX%d" % h, sw], [ybank], 256)
-                for q in (2 * c, 2 * c + 1):
-                    mm([(T[ybank][:, 0:HN], wr_(T[yw], r), Y[h][:, PAD + 128 * r:PAD + 128 * r + 128], False,
-                         ybank != kb and r == 15) for r in range(4 * q, 4 * q + 4)], ["Y%d_%d" % (h, q), yw], [ybank], 256)
-            for j in range(16 // MG):
-                def fn(c=c, j=j):
-                    for k in range(MG * j, MG * j + MG):
-                        a = 1024 * c + k
-                        i = V.tensor_tensor(T.MN[:, 2048 * h + a:2048 * h + 1024 * c + 1024:16],
-                                            Y[h][:, PAD + a:PAD + 1024 * c + 1024:16], T[px_][:, 64 * c:64 * c + 64], ALU.min)
-                    return i
-                record("V", fn, yt + [px_], ["M%d_%d_%d" % (h, c, j)], 64 * MG)
-                in_line("mins")
+        if ybank is not None:
+            if c == 1:
+                mm([(T[ybank][:, 0:HN], T.SX[0:HA, HN * h:HN * h + HN], T[sw][0:HA, :], False, False)], ["SX%d" % h, sw], [ybank], 256)
+            for i in range(2):
+                mm([(T[ybank][:, 0:HN], wr_(T[yw], r), Y[h][:, PAD + 128 * r:PAD + 128 * r + 128], False, ybank != kb and r == 15)
+                    for r in range(8 * c + 4 * i, 8 * c + 4 * i + 4)], [yt[i], yw], [ybank], 256)
+
+        def add(r0, r1, toks):
             mm([(T[kb][:, 0:HN], wr_(T[mw], r), T.MN[:, 2048 * h + 128 * r:2048 * h + 128 * r + 128], False, r == 15)
-                for r in range(8 * c, 8 * c + 8)], ["M%d_%d_%d" % (h, c, j) for j in range(16 // MG)] + [mw], [kb], 512)
+                for r in range(8 * c + r0, 8 * c + r1)], toks + [mw], [kb], 64 * (r1 - r0))
+        if q in WIDE[step]:
+            for j in range(4):
+                bk, a = ("pU%d" % h, px_)[j // 2], 256 * j
+                tt(T.MN[:, m0_ + a:m0_ + a + 256], Y[h][:, y0 + a:y0 + a + 256], T[bk][:, a % 512:a % 512 + 256], ALU.min,
+                   [yt[j // 2], bk], ["M%d_%d" % (q, j)], 256)
+                in_line("mins")
+                add(2 * j, 2 * j + 2, ["M%d_%d" % (q, j)])
+            return
+        for j in range(16 // MG):
+            def fn(j=j):
+                for k in range(MG * j, MG * j + MG):
+                    i = V.tensor_tensor(T.MN[:, m0_ + k:m0_ + 1024:16], Y[h][:, y0 + k:y0 + 1024:16], T[px_][:, 0:64], ALU.min)
+                return i
+            record("V", fn, yt + [px_], ["M%d_%d" % (q, j)], 64 * MG)
+            in_line("mins")
+        add(0, 8, ["M%d_%d" % (q, j) for j in range(16 // MG)])
 
     def best(h, src, R, a=0):
         scan(T.SC[:, a + HN * h:a + HN * h + HN], full("m0"), src, ALU.mult, ALU.max, R + ["m0"], ["SC%d_%d" % (h, a)])
 
-    def offsets(out, c0, n, tok):
-        ts(T.oj[:, c0:c0 + n], T.oi[:, c0:c0 + n], 4095, None, ALU.bitwise_and, None, ["oi" + tok], ["oj" + tok])
-        ts(out, T.oj[:, c0:c0 + n], -1.0, 4095.0, ALU.mult, ALU.add, ["oj" + tok], ["off" + tok])
+    def offsets(out, c0, n, tok, w1=[], w2=[]):
+        ts(T.oj[:, c0:c0 + n], T.oi[:, c0:c0 + n], 4095, None, ALU.bitwise_and, None, ["oi" + tok], ["oj" + tok] + w1)
+        ts(out, T.oj[:, c0:c0 + n], -1.0, 4095.0, ALU.mult, ALU.add, ["oj" + tok], ["off" + tok] + w2)
 
-    def write(h, rec, old, rtok, oldf, oftok, obias, newname, ntok, npb, nptok):
-        x_, r_, hh = T["pX%d" % h], T["pR%d" % h], "%d" % h
-        oh = hf(T.oh, h)
-        mm(group(x_[:, 0:128], [(full("I1"), rec), (full("I1"), old), (full("I8n"), npb)])
-           + group(x_[:, 128:256], [const(2), (full("GO"), newname), (full("I8k"), oh), (full("I8k"), npb)]),
-           rtok + [nptok, ntok, "oh" + hh, "I8n", "I8k", "GO", "one", "CK"], ["pX" + hh], 448)
-        act(hf(T.a1, h), x_[:, 0:128], ["pX" + hh], ["a1" + hh], bias=M1, scale=HALF)
+    def settle(key):
+        r_ = T.pR1[:, 128:128 + K]
+        mm(group(r_, [(I1, full("NM")), (I1n, full("kr"))], stop=False), ["NM", "I1n", "kr0", "kr1"], ["pR1"], 256)
+        for j in range(4):
+            cols = range(4 * j, 4 * j + 4)
+
+            def fn(cols=cols):
+                for a in cols:
+                    i = V.tensor_scalar(T.E[:, a, 0:K - 16 * a], T.kr[:, 16 * a:K], key(a), 0.0, ALU.add, ALU.is_equal)
+                return i
+            etok = ["E0_%d" % j, "E1_%d" % j]
+            record("V", fn, ["kr0", "kr1", "s1%d" % (j // 2)], etok, sum(max(64, 128 - 8 * a) for a in cols))
+            mm([(r_[:, 16 * a + 16:K], full("G8n"), T.E[:, a, 16:K - 16 * a], False, False) for a in cols if a < 15]
+               + [(r_[:, 64 * j:64 * j + 64], full("TRI"), T.E[:, 4 * j:4 * j + 4, 0:16], False, j == 3)],
+               etok + ["G8n", "TRI"], ["pR1"], 32 + sum(max(32, 120 - 8 * a) for a in cols))
+        scan(full("s2"), full("RR"), r_, ALU.min, ALU.max, ["RR", "pR1"], ["s20", "s21"], K)
+        ts(full("fo"), T.s2[:, 15:K:16], -1.0, 2048.0, ALU.mult, ALU.add, ["s20", "s21"], ["fo0", "fo1"])
+        tt(T.TB[:, 0:TBW].indirect(full("fo")), full("Cs"), full("Q"), ALU.max, ["fo0", "Cs0", "Cs1", "Q0", "Q1"],
+           ["TB", "TBc", "TBo", "TBd"], 60 + 3.5 * K)
+
+    def write(h, rec, old, rtok, oldf, oftok, obias, newname, ntok, npb, nptok, c0, key, step):
+        r_, hh = T["pR%d" % h], "%d" % h
+        xb, cb = ("pU0", "pU0") if h == 0 else ("pX0", "pX1")
+        x_, u_, oh = T[xb], T[cb][:, 256:384], hf(T.oh, h)
+        mm(group(x_[:, c0:c0 + 128], [(I1, rec), (I1, old), (I1n, npb)])
+           + group(x_[:, 384:512], [const(2), (GO, newname), (I1, oh), (I1, npb)]),
+           rtok + [nptok, ntok, "oh" + hh, "I1n", "GO", "one", "CK"], [xb], 448)
+        act(hf(T.a1, h), x_[:, c0:c0 + 128], [xb], ["a1" + hh], bias=M1, scale=HALF)
         act(hf(T.Hs, h), hf(T.a1, h), ["a1" + hh], ["Hs" + hh], bias=-M1)
-        tt(hf(T.Q, h), hf(T.Hs, h), x_[:, 128:256], ALU.max, ["Hs" + hh, "pX" + hh], ["Q" + hh], HN)
-        u_ = T["pU" + hh][:, 256:384]
-        mm(group(u_, [(full("I8n"), oh), (full("I8k"), npb)], stop=False), [nptok, "oh" + hh], ["pU" + hh])
-        mm(group(u_, [(full("I32"), oldf)], start=False), [oftok, "I32"], ["pU" + hh], 256)
-        act(hf(T.Cs, h), u_, ["pU" + hh], ["Cs" + hh], bias=obias)
-        mm(group(r_[:, 128:256], [(full("I1"), full("NM")), (full("I1n"), hf(T.kr, h))], stop=False),
-           ["NM", "I1n", "kr" + hh], ["pR" + hh], 128)
+        tt(hf(T.Q, h), hf(T.Hs, h), x_[:, 384:512], ALU.max, ["Hs" + hh, xb], ["Q" + hh], HN)
+        mm(group(u_, [(I1n, oh), (I1, npb)], stop=False), [nptok, "oh" + hh], [cb])
+        mm(group(u_, [(full("I32"), oldf)], start=False), [oftok, "I32"], [cb], 256)
+        act(hf(T.Cs, h), u_, [cb], ["Cs" + hh], bias=obias)
+        if step in MERGE:
+            if h == 1:
+                settle(key)
+            return
+        mm(group(r_[:, 128:256], [(I1, NM1), (I1n, hf(T.kr, h))], stop=False), ["NM", "I1n", "kr" + hh], ["pR" + hh], 128)
         top = HN * h + HN
         cuts = (0, 4, 8) if h == 0 else (0, 4, 8, 12, 16)
         for j in range(len(cuts) - 1):
             cols = range(cuts[j], cuts[j + 1])
+            own = cols[0] >= HA * h
+            e0, etok = 128 * (not own), "E%d_%d" % (h, j)
 
-            def fn(cols=cols):
+            def fn(cols=cols, e0=e0):
                 for a in cols:
                     lo = max(16 * a, HN * h)
-                    i = V.tensor_scalar(T.E[:, a, lo - 16 * a:top - 16 * a], T.kr[:, lo:top], T.s1[:, 16 * a + 15:16 * a + 16], 0.0,
-                                        ALU.add, ALU.is_equal)
+                    i = V.tensor_scalar(T.E[:, a, e0:e0 + top - lo], T.kr[:, lo:top], key(a), 0.0, ALU.add, ALU.is_equal)
                 return i
-            record("V", fn, ["kr" + hh, "s1%d" % (cols[0] // HA)], ["E%d_%d" % (h, j)], 256)
+            record("V", fn, ["kr" + hh, "s1%d" % (cols[0] // HA)], [etok], 256)
             lst = []
             for a in cols:
                 lo = max(16 * a + 16, HN * h)
                 if lo < top:
-                    lst.append((r_[:, 128 + lo - HN * h:256], full("G8n"), T.E[:, a, lo - 16 * a:top - 16 * a], False, False))
+                    lst.append((r_[:, 128 + lo - HN * h:256], full("G8n"), T.E[:, a, e0 + 16 * own:e0 + 16 * own + top - lo], False, False))
             a = cols[0]
-            if a >= HA * h:
+            if own:
                 lst.append((r_[:, 128 + 16 * a - HN * h:192 + 16 * a - HN * h], full("TRI"), T.E[:, a:a + 4, 0:16],
                             False, j == len(cuts) - 2))
-            mm(lst, ["E%d_%d" % (h, j), "G8n", "TRI"], ["pR" + hh], 256)
+            mm(lst, [etok, "G8n", "TRI"], ["pR" + hh], 200)
         scan(hf(T.s2, h), hf(T.RR, h), r_[:, 128:256], ALU.min, ALU.max, ["RR", "pR" + hh], ["s2" + hh])
         ts(hl(T.fo, h), dg(T.s2, h), -1.0, 2048.0, ALU.mult, ALU.add, ["s2" + hh], ["fo" + hh])
         tt(T.TB[:, 0:TBW].indirect(hl(T.fo, h)), hf(T.Cs, h), hf(T.Q, h), ALU.max, ["fo" + hh, "Cs" + hh, "Q" + hh],
-           ["TB", "TBc", "TBo", "TBd"], 60 + 3.8 * HN)
+           ["TB", "TBc", "TBo", "TBd"], 60 + 3.5 * HN)
 
-    send("z", 0, sl(T.zs, 0, ZW), sl(T.zr, 0, ZW), ["z0", "za0", "zb0", "zc0_0"])
-    TBC = ["TBc", "TBo"]
+    def key_scan(a):
+        return T.s1[:, 16 * a + 15:16 * a + 16]
+
+    def key_list(a):
+        return T.kl[:, a:a + 1]
+
+    TBC, late = ["TBc", "TBo"], []
 
     for t in range(RO):
         u = t + 1
         cwin, ctok = (T.CE[:, :], ["CE"]) if t == 0 else (cells, TBC)
         pwin, ptok = (T.PXB[:, 0:W], ["PXB"]) if t == 0 else (T.TB[:, 0:W], ["TB"])
-        for h in range(2):
-            hh = "%d" % h
-            spread(h, T.zs, t * ZW + HN * h, "z%d_%d" % (h, t))
-            key_start("pK" + hh, "I1")
-            names(h, cwin, ctok, t)
-            big(0, h, pwin, ptok, None, None, "W4")
-            best(h, T["pK" + hh][:, 0:HN], ["pK" + hh])
-            cp(hl(T.oi, h), dg(T.SC, h), ["SC%d_0" % h], ["oi" + hh])
-            offsets(hl(T.off, h), HA * h, HA, hh)
-            (cp if XV[h] else act)(hf(T.xs, h, t), Y[h][:, 0:YW].indirect(hl(T.off, h)), ytoks(h) + ["off" + hh], ["xs" + hh], c=gat(HN))
-            send("x" + hh, t, hf(T.xs, h, t), hf(T.xr, h, t), ["xs" + hh])
+        zt = ["z0_%d" % t, "z1_%d" % t]
+        if not ZJOIN:
+            plus[0] = BON["z"]
+            send("z", t, sl(T.xs, t, XW, K, XW), sl(T.xr, t, XW, K, XW), zt)
+            plus[0] = 0
+        for q0, q1 in XPARTS:
+            h, qq, a, b = q0 // 2, "q%d" % q0, 64 * q0, 64 * q1
+            kb, c0, c1 = "pK%d" % h, a - HN * h, b - HN * h
+            key_start(kb, "I1", c0, c1)
+            names(q0, q1, cwin, ctok, t)
+            for q in range(q0, q1):
+                spread(0, q, sl(T.xs, t, XW, K + a, K + b), zt[h])
+                big(0, q, q == q1 - 1, pwin, ptok, None, None, "W4")
+            plus[0] = BON["x"]
+            scan(T.SC[:, a:b], T.m0[:, 0:b - a], T[kb][:, c0:c1], ALU.mult, ALU.max, [kb, "m0"], ["SC%d_0" % h], b - a)
+            cp(T.oi[:, 4 * q0:4 * q1], T.SC[:, a + 15:b:16], ["SC%d_0" % h], ["oi" + qq, "oi%d" % h])
+            offsets(T.off[:, 4 * q0:4 * q1], 4 * q0, 4 * (q1 - q0), qq, ["oj%d" % h], ["off%d" % h])
+            (cp if XV[h] else act)(sl(T.xs, t, XW, a, b), Y[h][:, 0:PAD + 16 * c1].indirect(T.off[:, 4 * q0:4 * q1]),
+                                   ytoks(h, q1 - 2 * h) + ["off" + qq], ["xs" + qq], c=gat(b - a))
+            if ZJOIN and q1 == 4:
+                send("x%d" % q0, t, sl(T.xs, t, XW, a, XW), sl(T.xr, t, XW, a, XW), ["xs" + qq] + zt)
+                wrote["rz_%d" % t] = wrote["rx%d_%d" % (q0, t)]
+            else:
+                send("x%d" % q0, t, sl(T.xs, t, XW, a, b), sl(T.xr, t, XW, a, b), ["xs" + qq])
+            plus[0] = 0
+            for q in range(q0, q1):
+                wrote["rx%d_%d" % (q, t)] = wrote["rx%d_%d" % (q0, t)]
+        plus[0] = BON["lf"]
         act(full("Lf"), cells.indirect(sl(T.bA, t, 16)), TBC + ["bA%d" % t], ["Lf"], bias=-2048.0, c=gat(K))
-        tt(sl(T.ns, t), ohw.indirect(T.off[:, 0:16]), full("Lf"), ALU.mult, ["OH", "OHz", "off0", "off1", "Lf"], ["ns"], gat(K))
+        plus[0] = 0
+        tt(sl(T.ns, t), ohw.indirect(full("off")), full("Lf"), ALU.mult,
+           ["OH", "OHz", "Lf"] + ["offq%d" % q0 for q0, q1 in XPARTS] + ["off0", "off1"], ["ns"], gat(K))
         send("n", t, sl(T.ns, t), sl(T.nr, t), ["ns"])
         if t == 0:
-            for q in range(4):
-                o, i = T.TB[:, 1024 * q:1024 * q + 1024], T.PXB[:, 1024 * q:1024 * q + 1024]
-                if q % 2:
-                    cp(o, i, ["PXB"], ["TB%d" % q], 1024)
-                else:
-                    act(o, i, ["PXB"], ["TB%d" % q], c=1024)
-        ptok = ["TB"] + (["TB%d" % q for q in range(4)] if t == 0 else [])
+            for q in range(8):
+                o, i = T.TB[:, 512 * q:512 * q + 512], T.PXB[:, 512 * q:512 * q + 512]
+                (cp if q < WV else act)(o, i, ["PXB"], ["TB%d" % q], c=512)
+        ptok = ["TB"] + (["TB%d" % q for q in range(8)] if t == 0 else [])
         rz = "rz_%d" % t
-        na, par, ntx = [sl(T.zs, u, ZW, K + 16 * i, K + 16 * i + 16) for i in range(3)]
-        na0, par0, ntx0 = [sl(T.zr, t, ZW, K + 16 * i, K + 16 * i + 16) for i in range(3)]
-        tt(na, na0, ntx0, ALU.add, [rz], ["za%d" % u])
-        tt(par, par0, ntx0, ALU.is_equal, [rz], ["zb%d" % u])
-        ts(full("thr"), par, 2.0, -12.0, ALU.mult, ALU.add, ["zb%d" % u], ["thr"])
-        for h in range(2):
-            hh, c0 = "%d" % h, t * K + HN * h
-            rx, pu = "rx%d_%d" % (h, t), T["pU" + hh]
-            mm(group(pu[:, 0:HA], [(wr_(T.Wu, q), T.xr[:, c0 + 16 * (q % 8) + q // 8:c0 + 16 * (q % 8) + 16:2]) for q in range(16)]),
-               [rx, "Wu"], ["pU" + hh], 512)
-            cp(hl(T.bi, h), pu[:, 0:HA], ["pU" + hh], ["bi" + hh])
-            ts(hl(T.bj, h), hl(T.bi, h), CELLS - 1, None, ALU.bitwise_and, None, ["bi" + hh], ["bj" + hh])
-            ts(hl(T.bB, h, u), hl(T.bj, h), 2.0, None, ALU.mult, None, ["bj" + hh], ["bB%d_%d" % (h, u)])
-            names(h, cells, TBC, u)
-            spread(h, T.xr, c0, rx)
-            key_start("pK" + hh, "I2")
-            sums(h, T.xr, c0, rx)
-            key_start("pR" + hh, "I1")
-            if h == 1:
-                mm(group(pu[:, 16:32], [(wr_(T.Wu, r), T.xr[:, t * K + r:t * K + K:16]) for r in range(16)]),
-                   ["rx0_%d" % t, rx, "Wu"], ["pU1"], 512)
+        na, par, ntx = counts(T.ms, t)
+        na0, par0, ntx0 = counts(T.mr, t - 1 if t else RO)
+        was = ["rm_%d" % (t - 1)] if t else ["first0", "first1", "first2"]
+        tt(na, na0, ntx0, ALU.add, was, ["za%d" % t])
+        tt(par, par0, ntx0, ALU.is_equal, was, ["zb%d" % t])
+        ts(full("thr"), par, 2.0, -12.0, ALU.mult, ALU.add, ["zb%d" % t], ["thr"])
+        rxs = ["rx%d_%d" % (q, t) for q in range(4)]
+        for q0, q1 in XPARTS:
+            h, qq, a, b = q0 // 2, "q%d" % q0, 4 * q0, 4 * q1
+            hh = "%d" % h
+            pu = T["pU" + hh]
+            plus[0] = BON["b"]
+            xq = hf(T.xr, h, t, XW)
+            mm(group(pu[:, a:b], [(wr_(T.Wu, i), xq[:, 16 * (i % 8) + i // 8:16 * (i % 8) + 16:2]) for i in range(16)]),
+               [rxs[q0], "Wu"], ["pU" + hh], 512)
+            behind("offq%d" % XPARTS[-1][0])
+            cp(T.bi[:, a:b], pu[:, a:b], ["pU" + hh], ["bi" + qq])
+            ts(T.bj[:, a:b], T.bi[:, a:b], CELLS - 1, None, ALU.bitwise_and, None, ["bi" + qq], ["bj" + qq])
+            ts(T.bB[:, 16 * u + a:16 * u + b], T.bj[:, a:b], 2.0, None, ALU.mult, None, ["bj" + qq],
+               ["bB%d_%d" % (q, u) for q in range(q0, q1)])
+            names(q0, q1, cells, TBC, u)
+            plus[0] = 0
+            if q0 % 2 == 0:
+                key_start("pK" + hh, "I2")
+                key_start("pR" + hh, "I1")
+            if q1 % 2 == 0:
+                sums(h, hf(T.xr, h, t, XW), rxs[2 * h:2 * h + 2])
+            if q1 == 4:
+                mm(group(pu[:, 16:32], [(wr_(T.Wu, r), sl(T.xr, t, XW)[:, r:K:16]) for r in range(16)]), rxs + ["Wu"], ["pU1"], 512)
                 cp(T.bi[:, 16:32], pu[:, 16:32], ["pU1"], ["biA"])
                 ts(T.bj[:, 16:32], T.bi[:, 16:32], CELLS - 1, None, ALU.bitwise_and, None, ["biA"], ["bjA"])
                 ts(sl(T.bA, u, 16), T.bj[:, 16:32], 2.0, None, ALU.mult, None, ["bjA"], ["bA%d" % u])
                 ts(full("bC"), T.bj[:, 16:32], 2.0, 1.0, ALU.mult, ALU.add, ["bjA"], ["bC"])
+                if LIST:
+                    ts(full("ckl"), T.bj[:, 16:32], -2.0, -2048.0, ALU.mult, ALU.add, ["bjA"], ["ckl"])
                 act(full("Lf"), cells.indirect(sl(T.bA, u, 16)), TBC + ["bA%d" % u], ["Lf"], bias=-2048.0, c=gat(K))
                 act(full("ck"), cells.indirect(full("bC")), TBC + ["bC"], ["ck"], c=gat(K))
-            big(1, h, T.TB[:, 0:W], ptok, "pR" + hh, "W4", "W8", "DA")
-            act(hf(T.A3, h), T["pR" + hh][:, 0:HN], ["pR" + hh], ["A3" + hh])
+            for q in range(q0, q1):
+                spread(1, q, xq, rxs[q])
+                big(1, q, q % 2, T.TB[:, 0:W], ptok, "pR" + hh, "W4", "W8", "DA")
+            if q1 % 2 == 0:
+                act(hf(T.A3, h), T["pR" + hh][:, 0:HN], ["pR" + hh], ["A3" + hh])
         for h in range(2):
             hh = "%d" % h
-            rx, pu, pk = "rx%d_%d" % (h, t), T["pU" + hh], T["pK" + hh]
-            x, yw, live = hf(T.xr, h, t), Y[h][:, 0:YW], hf(T.live, h)
+            rx, pu, pk = rxs[2 * h:2 * h + 2], T["pU" + hh], T["pK" + hh]
+            x, yw, live, MS = hf(T.xr, h, t, XW), Y[h][:, 0:YW], hf(T.live, h), hf(T.MS, h)
+            sj, sm, cj, cm = K + HN * h, K + HN * h + HN, 24 * h, 8 + 8 * h
+            plus[0] = BON["f"]
             tt(hf(T.nk, h), pk[:, 0:HN], hf(T.A3, h), ALU.subtract, ["pK" + hh, "A3" + hh], ["nk" + hh], HN)
-            best(h, hf(T.nk, h), ["nk" + hh])
+            best(h, hf(T.nk, h), ["nk" + hh], sj)
             act(hf(T.sg, h), hf(T.nk, h), ["nk" + hh], ["sg" + hh], f=AF.Sign, bias=1.0 - 4096.0 * (4080 - TH1 + 1))
             scan(hf(T.cs, h), full("m0"), hf(T.sg, h), ALU.mult, ALU.add, ["m0", "sg" + hh], ["cs" + hh], 64)
-            zc = "zc%d_%d" % (h, u)
+            zc = "zc%d_%d" % (h, t)
             tt(hl(ntx, h), dg(T.cs, h), hl(T.thr, h), ALU.is_lt, ["cs" + hh, "thr"], [zc])
             cp(hl(T.nu, h), hl(ntx, h), [zc], ["nu" + hh])
             act(live, T.NP[:, 0:16].indirect(hl(T.nu, h)), ["NP", "nu" + hh], ["live" + hh], c=gat(HN))
-            tt(hf(T.ne, h), hf(T.SC, h).indirect(full("c15")), hf(T.nk, h), ALU.not_equal, ["SC%d_0" % h, "c15", "nk" + hh],
-               ["ne" + hh], gat(HN))
+            tt(hf(T.ne, h), hf(T.SC, 2 + 2 * h).indirect(full("c15")), hf(T.nk, h), ALU.not_equal,
+               ["SC%d_%d" % (h, sj), "c15", "nk" + hh], ["ne" + hh], gat(HN))
             tt(hf(T.ks, h), hf(T.ne, h), pk[:, 0:HN], ALU.mult, ["ne" + hh, "pK" + hh], ["ks" + hh], HN)
-            best(h, hf(T.ks, h), ["ks" + hh], K)
-            cp(hl(T.oi, h), dg(T.SC, h), ["SC%d_0" % h], ["oi" + hh])
-            offsets(hl(T.off, h), HA * h, HA, hh)
-            ts(hl(T.oi, h, 1), dg(T.SC, h, K), 0.5, None, ALU.mult, None, ["SC%d_%d" % (h, K)], ["oim" + hh])
-            offsets(hl(T.ofm, h), 16 + HA * h, HA, "m" + hh)
-            offj = hl(T.off, h)
-            tt(hf(T.fs, h, t), yw.indirect(hl(T.ofm, h)), x, ALU.max, ytoks(h) + ["offm" + hh, rx], ["fs" + hh], gat(HN))
+            best(h, hf(T.ks, h), ["ks" + hh], sm)
+            offj, offm = T.of2[:, cj:cj + HA], T.of2[:, cm:cm + HA]
+            if h == 0 and JOIN:
+                tt(T.oi[:, 16:32], T.SC[:, K + 15:2 * K:16], full("hc"), ALU.mult,
+                   ["SC0_%d" % sj, "SC0_%d" % sm, "hca", "hcb"], ["oij0"])
+                offsets(T.of2[:, 0:16], 16, 16, "j0", [], ["offm0"])
+            else:
+                cp(T.oi[:, 16 + cj:24 + cj], dg(T.SC, h, sj), ["SC%d_%d" % (h, sj)], ["oij" + hh])
+                offsets(offj, 16 + cj, HA, "j" + hh)
+                ts(T.oi[:, 16 + cm:24 + cm], dg(T.SC, h, sm), 0.5, None, ALU.mult, None, ["SC%d_%d" % (h, sm)], ["oim" + hh])
+                offsets(offm, 16 + cm, HA, "m" + hh)
+            tt(hf(T.fs, h, t), yw.indirect(offm), x, ALU.max, ytoks(h) + ["offm" + hh] + rx, ["fs" + hh], gat(HN))
             send("f" + hh, t, hf(T.fs, h, t), hf(T.fr, h, t), ["fs" + hh])
-            tt(hf(T.MS, h), ohw.indirect(offj), hf(T.Lf, h), ALU.mult, ["OH", "OHz", "off" + hh, "Lf"], ["MS" + hh], gat(HN))
-            act(hf(T.oh, h), ohw.indirect(offj), ["OH", "OHz", "off" + hh], ["oh" + hh], c=gat(HN))
-            act(hf(T.yj, h), yw.indirect(offj), ytoks(h) + ["off" + hh], ["yj" + hh], c=gat(HN))
-            mm(group(pu[:, 0:128], [(full("I8k"), live), (full("GO"), hf(T.MS, h))]), ["I8k", "GO", "live" + hh, "MS" + hh],
-               ["pU" + hh])
-            tt(hf(T.kr, h), pu[:, 0:128], hf(T.ck, h), ALU.min, ["pU" + hh, "ck"], ["kr" + hh], HN)
+            plus[0] = BON["t0"] * (1 - h)
+            tt(MS, ohw.indirect(offj), hf(T.Lf, h), ALU.mult, ["OH", "OHz", "offj" + hh, "Lf"], ["MS" + hh], gat(HN))
+            act(hf(T.oh, h), ohw.indirect(offj), ["OH", "OHz", "offj" + hh], ["oh" + hh], scale=8192.0, c=gat(HN))
+            act(hf(T.yj, h), yw.indirect(offj), ytoks(h) + ["offj" + hh], ["yj" + hh], c=gat(HN))
             pr = T["pR" + hh][:, 256:384]
-            mm(group(pr, [(full("I1"), full("NM"))], stop=False), ["NM"], ["pR" + hh])
-            mm(group(pr, [(full("I1n"), hf(T.kr, h))], start=False), ["I1n", "kr" + hh], ["pR" + hh])
-            scan(hf(T.s1, h), hf(T.RR, h), pr, ALU.min, ALU.max, ["RR", "pR" + hh], ["s1" + hh])
+            mm(group(pr, [(I1, NM1)], stop=False), ["NM"], ["pR" + hh])
+            mm(group(pu[:, 0:128], [(I1, live), (GO, MS)]), ["GO", "live" + hh, "MS" + hh], ["pU" + hh])
+            if LIST:
+                mm(group(pr, [(I1n, live), (GOn, MS)], start=False), ["GOn", "live" + hh, "MS" + hh], ["pR" + hh])
+                scan(hf(T.s1, h), hf(T.RR, h), pr, ALU.min, ALU.max, ["RR", "pR" + hh], ["sa" + hh, "s1" + hh])
+                tt(hf(T.kr, h), pu[:, 0:128], hf(T.ck, h), ALU.min, ["pU" + hh, "ck"], ["kr" + hh], HN)
+                tt(hl(T.kl, h), dg(T.s1, h), hl(T.ckl, h), ALU.max, ["sa" + hh, "ckl"], ["s1" + hh])
+            else:
+                tt(hf(T.kr, h), pu[:, 0:128], hf(T.ck, h), ALU.min, ["pU" + hh, "ck"], ["kr" + hh], HN)
+                mm(group(pr, [(I1n, hf(T.kr, h))], start=False), ["I1n", "kr" + hh], ["pR" + hh])
+                scan(hf(T.s1, h), hf(T.RR, h), pr, ALU.min, ALU.max, ["RR", "pR" + hh], ["s1" + hh])
             if h == 1:
-                tt(sl(T.ms, t, MW, 0, K), ohw.indirect(full("ofm")), full("Lf"), ALU.mult,
+                tt(sl(T.ms, t, MW, 0, K), ohw.indirect(T.of2[:, 8:24]), full("Lf"), ALU.mult,
                    ["OH", "OHz", "offm0", "offm1", "Lf"], ["ms"], gat(K))
-                cp(sl(T.ms, t, MW, K, MW), ntx, ["zc0_%d" % u, zc], ["ml"])
-                send("m", t, sl(T.ms, t, MW), sl(T.mr, t, MW), ["ms", "ml"])
-            z0 = hf(T.zr, h, t, ZW)
-            mm(group(pk[:, 256:384], [(full("I1"), z0), (full("I8n"), live)])
-               + group(pk[:, 384:512], [(full("I1"), hf(T.yj, h)), (full("I8n"), live)]),
-               [rz, "live" + hh, "yj" + hh, "I8n"], ["pK" + hh])
+                send("m", t, sl(T.ms, t, MW), sl(T.mr, t, MW), ["ms", "za%d" % t, "zb%d" % t, "zc0_%d" % t, zc])
+            z0 = sl(T.xr, t, XW, K + HN * h, K + HN * h + HN)
+            mm(group(pk[:, 256:384], [(I1, z0), (I1n, live)]) + group(pk[:, 384:512], [(I1, hf(T.yj, h)), (I1n, live)]),
+               [rz, "live" + hh, "yj" + hh], ["pK" + hh])
             act(T.E12[:, K * h:K * h + K], pk[:, 256:512], ["pK" + hh], ["E12" + hh], f=AF.Relu, c=K)
-            write(h, x, hf(T.yj, h), [rx, "yj" + hh], hf(T.Lf, h), "Lf", 2048.0 - 8192.0, hf(T.nr, h, t), "rn_%d" % t,
-                  live, "live" + hh)
+            write(h, x, hf(T.yj, h), rx + ["yj" + hh], hf(T.Lf, h), "Lf", 2048.0 - 8192.0, hf(T.nr, h, t), "rn_%d" % t,
+                  live, "live" + hh, 128, key_list if LIST else key_scan, 1)
         rm = "rm_%d" % t
         for h in range(2):
-            hh, c0 = "%d" % h, t * K + HN * h
+            hh = "%d" % h
             rf, f = "rf%d_%d" % (h, t), hf(T.fr, h, t)
             pu, pk, pr = T["pU" + hh], T["pK" + hh], T["pR" + hh]
+            plus[0] = BON["p"]
             mm(group(pu[:, 256:384], [const(0, 2), (full("KB"), f)]) + group(pk[:, 128:256], [const(0)], stop=False)
-               + reorder(pk[:, 128:256], full("KB"), T.fr, c0, False, False), [rf, "KB", "one", "CK"], ["pU" + hh, "pK" + hh], 448)
+               + reorder2(pk[:, 128:256], full("KB"), f, False), [rf, "KB", "one", "CK"], ["pU" + hh, "pK" + hh], 448)
+            behind("fs1")
             if HV[h]:
                 ts(hf(T.hi, h), pu[:, 256:384], M4096, M4096, ALU.add, ALU.subtract, ["pU" + hh], ["hi" + hh], HN)
             else:
                 act(hf(T.a2, h), pu[:, 256:384], ["pU" + hh], ["a2" + hh], bias=M4096)
                 act(hf(T.hi, h), hf(T.a2, h), ["a2" + hh], ["hi" + hh], bias=-M4096)
-            mm(reorder(pk[:, 128:256], full("I1n"), T.hi, HN * h, False, True), ["hi" + hh, "I1n"], ["pK" + hh], 256)
-            ts(hf(T.Lu, h), pk[:, 128:256], 2048.0, None, ALU.add, None, ["pK" + hh], ["Lu" + hh], HN)
-            spread(h, T.fr, c0, rf)
-            sums(h, T.fr, c0, rf)
+            mm(reorder2(pk[:, 128:256], I1n, hf(T.hi, h), True), ["hi" + hh, "I1n"], ["pK" + hh], 256)
+            ts(hf(T.Lu, h), pk[:, 128:256], 2048.0, None, ALU.add, None, ["pK" + hh], ["Lu%d" % (2 * h), "Lu%d" % (2 * h + 1)], HN)
+            plus[0] = 0
+            sums(h, f, [rf])
             key_start("pK" + hh, "I1")
             mm(group(pu[:, 384:512], [const(1, 2), (full("KB"), f)]), [rf, "KB"], ["pU" + hh])
-            act(hf(T.a3, h), pu[:, 384:512], ["pU" + hh], ["a3" + hh], bias=M1024)
-            act(hf(T.md, h), hf(T.a3, h), ["a3" + hh], ["md" + hh], bias=-M1024)
+            act(hf(T.sel, h), pu[:, 384:512], ["pU" + hh], ["sel" + hh], bias=M1024)
+            act(hf(T.md, h), hf(T.sel, h), ["sel" + hh], ["md" + hh], bias=-M1024)
             mm(group(pr[:, 256:384], [(full("KB2"), f), (full("J32"), hf(T.md, h))]), [rf, "KB2", "J32", "md" + hh], ["pR" + hh], 320)
             act(hf(T.Lcc, h), pr[:, 256:384], ["pR" + hh], ["Lcc" + hh], bias=2048.0)
-            big(2, h, T.TB[:, 0:W], ["TB"], "pK" + hh, "W4n", "W8", "DAn")
-        ts(full("dk"), sl(T.mr, t, MW, K, MW), -TOP, TOP, ALU.mult, ALU.add, [rm], ["dk"])
+            for q in (2 * h, 2 * h + 1):
+                spread(2, q, f, rf)
+                big(2, q, q % 2, T.TB[:, 0:W], ["TB"], "pK" + hh, "W4n", "W8", "DAn")
+        ts(full("dk"), counts(T.mr, t)[2], -TOP, TOP, ALU.mult, ALU.add, [rm], ["dk"])
         for h in range(2):
             hh = "%d" % h
             rf, f = "rf%d_%d" % (h, t), hf(T.fr, h, t)
             pu, pk = T["pU" + hh], T["pK" + hh]
-            offj, npb, oh, w_ = hl(T.off, h), hf(T.np3, h), hf(T.oh, h), hf(T.ws, h, t)
+            offj, npb, oh, w_, MS = hl(T.off, h), hf(T.np3, h), hf(T.oh, h), hf(T.ws, h, t), hf(T.MS, h)
+            otok = ["offq%d" % q0 for q0, q1 in XPARTS if q0 // 2 == h]
+            plus[0] = BON["w"]
             best(h, pk[:, 0:HN], ["pK" + hh])
             ts(hl(T.nu, h), dg(T.SC, h), 4096.0 * (4080 - TH2 + 1), None, ALU.is_lt, None, ["SC%d_0" % h], ["nu" + hh])
             tt(hl(T.oi, h), dg(T.SC, h), hl(T.dk, h), ALU.max, ["SC%d_0" % h, "dk"], ["oi" + hh])
-            offsets(offj, HA * h, HA, hh)
+            offsets(offj, HA * h, HA, hh, [], otok)
             act(npb, T.NP[:, 0:16].indirect(hl(T.nu, h)), ["NP", "nu" + hh], ["np" + hh], c=gat(HN))
             act(w_, Y[h][:, 0:YW].indirect(offj), ytoks(h) + ["off" + hh], ["ws" + hh], c=gat(HN))
             send("w" + hh, t, w_, hf(T.wr, h, t), ["ws" + hh])
-            act(oh, ohw.indirect(offj), ["OH", "OHz", "off" + hh], ["oh" + hh], c=gat(HN))
-            mm(group(pu[:, 0:128], [const(0), (full("KB"), f), (full("I1n"), hf(T.hi, h))], stop=False), [rf, "hi" + hh], ["pU" + hh])
-            mm(group(pu[:, 0:128], [(full("I8k"), npb)], start=False), ["np" + hh], ["pU" + hh])
+            plus[0] = BON["t0"] * (1 - h)
+            act(oh, ohw.indirect(offj), ["OH", "OHz", "off" + hh], ["oh" + hh], scale=8192.0, c=gat(HN))
+            mm(group(pu[:, 0:128], [const(0), (full("KB"), f), (I1n, hf(T.hi, h))], stop=False), [rf, "hi" + hh], ["pU" + hh])
+            mm(group(pu[:, 0:128], [(I1, npb)], start=False), ["np" + hh], ["pU" + hh])
             tt(hf(T.sel, h), pu[:, 0:128], hf(T.Lcc, h), ALU.min, ["pU" + hh, "Lcc" + hh], ["sel" + hh], HN)
-            tt(hf(T.MS, h), ohw.indirect(offj), hf(T.sel, h), ALU.mult, ["OH", "OHz", "off" + hh, "sel" + hh], ["MS" + hh], gat(HN))
+            tt(MS, ohw.indirect(offj), hf(T.sel, h), ALU.mult, ["OH", "OHz", "off" + hh, "sel" + hh], ["MS" + hh], gat(HN))
             pr = T["pR" + hh][:, 0:128]
-            mm(group(pr, [(full("I1"), full("NM")), const(3), (full("G8k"), oh)], stop=False), ["oh" + hh, "G8k", "NM"], ["pR" + hh])
-            mm(group(pu[:, 128:256], [(full("G8n"), oh)], stop=False), ["oh" + hh, "G8n"], ["pU" + hh])
-            mm(group(pu[:, 128:256], [(full("GO"), hf(T.MS, h))], start=False), ["MS" + hh], ["pU" + hh])
-            mm(group(pr, [(full("GOn"), hf(T.MS, h))], start=False), ["MS" + hh, "GOn"], ["pR" + hh])
+            mm(group(pr, [(I1, NM1), const(3), (GO, oh)], stop=False), ["oh" + hh, "NM"], ["pR" + hh])
+            mm(group(pu[:, 128:256], [(GOn, oh)], stop=False), ["oh" + hh, "GOn"], ["pU" + hh])
+            mm(group(pu[:, 128:256], [(GO, MS)], start=False), ["MS" + hh], ["pU" + hh])
+            mm(group(pr, [(GOn, MS)], start=False), ["MS" + hh, "GOn"], ["pR" + hh])
             ts(hf(T.kr, h), pu[:, 128:256], 8192.0, None, ALU.add, None, ["pU" + hh], ["kr" + hh], HN)
             scan(hf(T.s1, h), hf(T.RR, h), pr, ALU.min, ALU.max, ["RR", "pR" + hh], ["s1" + hh])
             ts(hl(T.ku, h), dg(T.s1, h), -1.0, 2048.0, ALU.mult, ALU.add, ["s1" + hh], ["ku" + hh])
             act(hf(T.OLD, h), T.TB[:, 0:TBW].indirect(hl(T.ku, h)), ["TB", "TBc", "TBo", "TBd", "ku" + hh], ["OLD" + hh], c=gat(HN))
-            write(h, f, w_, [rf, "ws" + hh], hf(T.OLD, h), "OLD" + hh, -8192.0, hf(T.mr, h, t, MW), rm, npb, "np" + hh)
+            write(h, f, w_, [rf, "ws" + hh], hf(T.OLD, h), "OLD" + hh, -8192.0, hf(T.mr, h, t, MW), rm, npb, "np" + hh, 0, key_scan, 2)
+            plus[0] = 0
             e = T.E12[:, K * h:K * h + HN], T.E12[:, K * h + HN:K * h + K]
-            mm(group(pk[:, 128:256], [(full("I1"), hf(T.zr, h, t, ZW)), (full("I1"), e[0]), (full("I2n"), e[1])], stop=False),
+            mm(group(pk[:, 128:256], [(I1, sl(T.xr, t, XW, K + HN * h, K + HN * h + HN)), (I1, e[0]), (full("I2n"), e[1])], stop=False),
                [rz, "E12" + hh, "I2n"], ["pK" + hh])
-            mm(group(pk[:, 128:256], [(full("I1"), hf(T.wr, h, t))], start=False), ["rw%d_%d" % (h, t)], ["pK" + hh])
+            mm(group(pk[:, 128:256], [(I1, hf(T.wr, h, t))], start=False), ["rw%d_%d" % (h, t)], ["pK" + hh])
+            late.append(len(ops) - 1)
+            if h == 1 and GUARD:
+                ops[late[-2]]["line"] = [wrote["ws1"]]
             act(hf(T.a2, h), pk[:, 128:256], ["pK" + hh], ["a2" + hh], bias=M1, scale=HALF)
-            act(hf(T.zs, h, u, ZW), hf(T.a2, h), ["a2" + hh], ["z%d_%d" % (h, u)], f=AF.Abs, bias=-M1)
-        if u < RO:
-            send("z", u, sl(T.zs, u, ZW), sl(T.zr, u, ZW),
-                 ["z0_%d" % u, "z1_%d" % u, "za%d" % u, "zb%d" % u, "zc0_%d" % u, "zc1_%d" % u])
+            act(sl(T.xs, u, XW, K + HN * h, K + HN * h + HN), hf(T.a2, h), ["a2" + hh], ["z%d_%d" % (h, u)], f=AF.Abs, bias=-M1)
 
-    store("G", T.yx[:, :], T.TB[:, 0:W], ["TB"])
-    record("A", lambda: A.activation(full("YC"), T.TB[:, W:SP:2], AF.Identity), ["TBc"], ["YC"], CELLS)
-    store("S", T.yc[:, :], full("YC"), ["YC"])
+    store("G", T.yx[:, :], T.TB[:, 0:W], ["TB"], 6000)
+    for i, fn in enumerate((cp, act)):
+        fn(T.YC[:, 512 * i:512 * i + 512], T.TB[:, W + 1024 * i:W + 1024 * i + 1024:2], ["TBc"], ["YC%d" % i], c=512)
+    store("S", T.yc[:, :], full("YC"), ["YC0", "YC1"], 4000)
     cp(full("yvf"), T.bj[:, 16:32], ["bjA"], ["yvf"])
-    tt(full("t1"), na, ntx, ALU.add, ["za%d" % RO, "zc0_%d" % RO, "zc1_%d" % RO], ["t1"])
+    tt(full("t1"), na, ntx, ALU.add, ["za%d" % t, "zc0_%d" % t, "zc1_%d" % t], ["t1"])
     ts(full("au"), full("t1"), -1.0, float(RO), ALU.mult, ALU.add, ["t1"], ["au"])
     cp(full("ar"), full("ioc").indirect(full("au")), ["au", "ioc"], ["ar"], gat(K))
-    store("S", T.yz[:, :], sl(T.zs, RO, ZW, 0, K), ["z0_%d" % RO, "z1_%d" % RO])
+    store("S", T.yz[:, :], sl(T.xs, RO, XW, K, XW), ["z0_%d" % RO, "z1_%d" % RO])
     store("S", T.yv[:, :], full("yvf"), ["yvf"])
     for q in range(8):
         store("S", T.ya[q:q + 1, :], T.ar[16 * q:16 * q + 1, :], ["ar"])
@@ -540,16 +677,20 @@ def rank_program(g, core, T, topo):
     for i in range(n - 1, -1, -1):
         rest[i] = ops[i]["cost"] + max([hop + rest[j] for j, hop in after[i]] + [0.0])
 
-    def plan(after, before, rest):
+    def plan(after, before, rest, look, sign=1):
         missing = [len(b) for b in before]
         ready, ends, free, order = [0.0] * n, [0.0] * n, {e: 0.0 for e in Q}, []
         pool = [i for i in range(n) if not missing[i]]
+
+        def begin(i):
+            return max(ready[i], free.get(ops[i]["e"], 0.0))
+
+        def rank_(i):
+            return rest[i] + ops[i]["plus"] * sign
         while pool:
-            def begin(i):
-                return max(ready[i], free.get(ops[i]["e"], 0.0))
-            i = min(pool, key=lambda j: (begin(j), -rest[j]))
-            soon = begin(i) + ops[i]["cost"] * LOOK
-            i = max([j for j in pool if ops[j]["e"] == ops[i]["e"] and begin(j) <= soon], key=lambda j: rest[j])
+            i = min(pool, key=lambda j: (begin(j), -rank_(j)))
+            soon = begin(i) + ops[i]["cost"] * look
+            i = max([j for j in pool if ops[j]["e"] == ops[i]["e"] and begin(j) <= soon], key=rank_)
             ends[i] = begin(i) + ops[i]["cost"]
             if ops[i]["e"] is not None:
                 free[ops[i]["e"]] = ends[i]
@@ -562,9 +703,11 @@ def rank_program(g, core, T, topo):
                     pool.append(j)
         return max(ends), order, ends
 
-    plans = [plan(after, before, rest)]
-    for _ in range(PASSES):
-        plans.append(plan(after, before, plan(before, after, plans[-1][2])[2]))
+    plans = []
+    for look in LOOKS:
+        plans.append(plan(after, before, rest, look))
+        for _ in range(PASSES):
+            plans.append(plan(after, before, plan(before, after, plans[-1][2], look, -1)[2], look))
     order = min(plans, key=lambda p: p[0])[1]
 
     cnt = {"cV": 0, "cA": 0, "cP": 0, "cG": 0, "sent": 0, "outs": 0, "outg": 0}

@@ -15,11 +15,14 @@ XW, MW = 512, 304
 TOP = 2.0 ** 24 - 1
 XPARTS = ((0, 2), (2, 4))
 VSHARE = ((1, 0, 1, 0), (1, 0, 1, 0), (1, 1, 1, 0))
-WIDE = ((1, 3), (1, 3), (1,))
-JOIN, MG, XV, HV, ZJOIN, LIST, GUARD, WV = 1, 4, (0, 0), (0, 0), 0, 0, 1, 2
-MERGE = ()
-RELAYED, HAND = ("z", "n"), 3500
-BON = {"x": 1000, "b": 0, "f": 0, "p": 0, "w": 0, "t0": 0, "lf": 0, "z": -3000}
+WIDE = ((1, 3), (1, 3), (1, 3))
+JOIN, MG, XV, HV, ZJOIN, LIST, GUARD, WV = 1, 2, (0, 0), (0, 0), 0, 1, 1, 1
+PV = (0, 0)
+PSEL, NA, CA, AFTER = 1, (0, 0), 0, {(0, 3, 1): "xsq0"}
+CUTS = (0, 4, 8)
+RELAYED, HAND = ("z", "n", "m"), 3500
+BON = {"x": 1000, "b": 0, "f": 0, "p": 0, "w": 500, "t0": 0, "lf": 0, "z": -3000, "k": -500, "z0": 30000, "m": 0}
+INLINE, SOON = (), {}
 LOOKS, PASSES = (0.25,), 3
 HOP, FLIGHT, ISSUE = 230, 5000, 800
 LOADS = (2200, 4000, 2400, 6000, 3500)
@@ -38,28 +41,28 @@ SCRATCH = {
     "pi": _s(16, I32), "pj": _s(16, I32), "col": _s(16, F32), "ioc": _s(256, F32), "ioa": _s(128, F32), "iok": _s(128, F32),
     "ioe": _s(128, F32), "GE": _s(128, BF), "RS": _s(8, BF), "rep": _s(8, U16),
     "W1": _s(144, BF), "W4": _s(144, BF), "W8": _s(144, BF), "W4n": _s(144, BF), "Wu": _s(144, BF),
-    "GO": _s(128, BF), "GOn": _s(128, BF), "G8n": _s(128, BF), "TRI": _s(128, BF),
+    "GO": _s(128, BF), "GOn": _s(128, BF), "G8n": _s(128, BF), "G8k": _s(128, BF), "I8k": _s(128, BF), "I8n": _s(128, BF), "TRI": _s(128, BF),
     "I1": _s(128, BF), "I2": _s(128, BF), "I2n": _s(128, BF), "I1n": _s(128, BF),
-    "I32": _s(128, F32), "J32": _s(128, F32), "one": _s(128, BF), "CK": _s(512, BF),
+    "I32": _s(128, F32), "J32": _s(128, F32), "one": _s(128, BF), "CK": _s(768, BF), "Wu2": _s(144, BF),
     "NM": _s(256, BF), "m0": _s(128, BF), "JH": _s(128, BF), "JL": _s(128, BF), "RR": _s(256, F32),
-    "DA": _s(128, F32), "DAn": _s(128, F32), "c15": _s(8, U16), "hc": _s(16, F32),
+    "DA": _s(128, F32), "DAn": _s(128, F32), "c15": _s(8, U16), "bf": _s(16, F32),
     "bB": _s(16 * (RO + 1), U16), "bA": _s(16 * (RO + 1), U16), "bC": _s(16, U16),
     "bi": _s(32, I32), "bj": _s(32, I32), "yvf": _s(16, F32), "thr": _s(16, F32), "dk": _s(16, F32),
     "Lu": _s(256, U16), "Lf": _s(256, F32), "ck": _s(256, F32), "SX": _s(256, F32), "A3": _s(256, F32), "nk": _s(256, F32),
-    "SC": _s(768, F32), "ne": _s(256, BF), "ks": _s(256, F32), "sg": _s(256, BF), "cs": _s(256, BF),
+    "SC": _s(768, I32), "ne": _s(256, BF), "ks": _s(256, F32), "sg": _s(256, BF), "cs": _s(256, BF),
     "oi": _s(48, I32), "oj": _s(48, I32), "off": _s(16, U16), "of2": _s(32, U16), "nu": _s(16, U16),
     "MS": _s(256, F16), "kr": _s(256, F16), "s1": _s(256, F32), "s2": _s(256, F32), "ku": _s(16, U16), "fo": _s(16, U16),
     "oh": _s(256, BF), "live": _s(256, BF), "yj": _s(256, BF), "np3": _s(256, BF), "OLD": _s(256, F32), "sel": _s(256, F32),
     "a1": _s(256, F32), "a2": _s(256, F32), "Hs": _s(256, F32), "Cs": _s(256, F32), "Q": _s(256, F32),
     "hi": _s(256, BF), "md": _s(256, F32), "Lcc": _s(256, F32), "E12": _s(512, BF),
     "t1": _s(16, F32), "au": _s(16, U16), "ar": _s(256, F32), "ckl": _s(16, F32), "kl": _s(16, F32),
-    "xs": _s(XW * (RO + 1), BF), "ns": _s(K * RO, F16), "fs": _s(K * RO, BF), "ms": _s(MW * RO, F16), "ws": _s(K * RO, BF),
-    "xr": _s(XW * RO, BF), "nr": _s(K * RO, F16), "fr": _s(K * RO, BF), "mr": _s(MW * (RO + 1), F16), "wr": _s(K * RO, BF),
+    "xs": _s(XW * (RO + 1), BF), "ns": _s(K * RO, F16), "fs": _s(MW * RO, BF), "ms": _s(K * RO, F16), "ws": _s(K * RO, BF),
+    "xr": _s(XW * RO, BF), "nr": _s(K * RO, F16), "fr": _s(MW * (RO + 1), BF), "mr": _s(K * RO, F16), "wr": _s(K * RO, BF),
 }
 for _b in ("pX0", "pX1", "pK0", "pK1", "pU0", "pU1", "pR0", "pR1"):
     SCRATCH[_b] = ("psum", [128, 512], F32)
 MSGS = ("z", "x0", "x1", "x2", "x3", "n", "f0", "f1", "m", "w0", "w1")
-SEMAPHORES = (["cV", "cA", "cP", "cG", "sent", "dv0", "dce", "dz", "dpx", "dw", "outs", "outg"]
+SEMAPHORES = (["cV", "cA", "cP", "cG", "sent", "dv0", "dce", "dz", "dpx", "dw", "outs", "outg", "ry_0"]
               + ["r%s_%d" % (m, t) for m in MSGS for t in range(RO)] + ["h%s_%d" % (m, t) for m in "znm" for t in range(RO)])
 
 
@@ -80,7 +83,7 @@ def rank_program(g, core, T, topo):
                 rid, pid = topo.addr(to)[0:2]
                 for t in range(RO):
                     for m in RELAYED:
-                        ap = {"z": T.xr[:, XW * t + K:XW * t + XW], "n": T.nr[:, K * t:K * t + K], "m": T.mr[:, MW * t:MW * t + MW]}[m]
+                        ap = {"z": T.xr[:, XW * t + K:XW * t + (XW if t else K + HN)], "n": T.nr[:, K * t:K * t + K], "m": T.mr[:, K * t:K * t + K]}[m]
                         g.wait_ge(T.sem["h%s_%d" % (m, t)], len(inner(r)))
                         g.remote_dma(ap, ap, T.sem["r%s_%d" % (m, t)], T.sem.sent, pid, rid, topo.mask(core, to))
                 g.wait_ge(T.sem.sent, RO * len(RELAYED) * len(topo.engines(core, to)))
@@ -113,7 +116,7 @@ def rank_program(g, core, T, topo):
 
     def in_line(name):
         if name in lines:
-            ops[-1]["line"] = [lines[name]]
+            ops[-1]["line"] = ops[-1].get("line", []) + [lines[name]]
         lines[name] = len(ops) - 1
 
     def behind(tok):
@@ -157,6 +160,8 @@ def rank_program(g, core, T, topo):
 
     def iota(out, pattern, base, tok, n):
         record("G", lambda: g.iota(out, pattern, base, 0, allow_small_or_imprecise_dtypes=True), [], [tok], 160 + 2 * n)
+        if tok in ("ioc", "ioe", "JH", "ioa", "iok", "JL", "SEL"):
+            in_line("first")
 
     def send(m, t, src, dst, R):
         name = "r%s_%d" % (m, t)
@@ -170,7 +175,9 @@ def rank_program(g, core, T, topo):
                    ISSUE, "send", len(engines))
         if m in RELAYED:
             in_line("relayed")
-        record(None, None, [], [name], FLIGHT + HAND * (m in RELAYED), "land", (name, len(topo.engines(last, core))))
+        if t == 0 and m in "yz":
+            in_line("first")
+        record(None, None, [], [name], FLIGHT - SOON.get(m, 0) + HAND * (m in RELAYED), "land", (name, len(topo.engines(last, core))))
         ops[-1]["pre"] = [i]
 
     def load(e, dst, src, sem, total, tok, cost, **kw):
@@ -207,13 +214,15 @@ def rank_program(g, core, T, topo):
     Y = (T.Y0, T.Y1)
     ohw = T.OH[:, 0:YW]
 
-    load("S", T.vi[:, :], T.v0[:, :], "dv0", 16, "vi", LOADS[0])
+    load("S", hl(T.vi, 0), hl(T.v0, 1), "dv0", 32, None, 0)
+    load("S", hl(T.vi, 1), hl(T.v0, 0), "dv0", 32, "vi", LOADS[0])
     load("S", T.CE[:, :], T.ce[:, :], "dce", 16, "CE", LOADS[1])
-    load("A", T.xs[:, K:XW], T.z0[:, :], "dz", 16, "z0", LOADS[2])
+    load("A", T.kp[:, :], T.kap[:, :], "dz", 48, None, 0)
+    load("A", hf(T.xs, 2), hf(T.z0, 1), "dz", 48, None, 0)
+    load("A", hf(T.xs, 3), hf(T.z0, 0), "dz", 48, "z0", LOADS[2])
     load("A", T.PXB[:, 0:W // 2], T.px[:, 0:W // 2], "dpx", 32, None, 0)
     load("S", T.PXB[:, W // 2:W], T.px[:, W // 2:W], "dpx", 32, "PXB", LOADS[3])
-    load("G", T.kp[:, :], T.kap[:, :], "dw", 32, None, 0)
-    load("G", T.wv[:, 0:1], T.wu[:, :], "dw", 32, "kw", LOADS[4], allow_slow_non_contiguous=True)
+    load("G", T.wv[:, 0:1], T.wu[:, :], "dw", 16, "kw", LOADS[4], allow_slow_non_contiguous=True)
     wrote["z0_0"] = wrote["z1_0"] = wrote["z0"]
 
     record("G", lambda: g.iota(T.pi[:, :], [[0, 16]], 0, 1), [], ["pi"], 200)
@@ -227,7 +236,7 @@ def rank_program(g, core, T, topo):
     iota(T.TB[:, SP:TBW], [[0, K]], 0, "TBd", K)
     iota(T.SEL[:, :], [[1, 8], [16, 8], [0, 16]], 8, "SEL", 1024)
     pc, rc, gc_, ec, sc_, qc, wc, jc, uc, nc = [T.col[:, i:i + 1] for i in range(10)]
-    for i, (ap, c) in enumerate(zip(counts(T.mr, RO), (-1.0, 0.0, 1.0))):
+    for i, (ap, c) in enumerate(zip(counts(T.fr, RO), (-1.0, 0.0, 1.0))):
         fill(ap, c, "first%d" % i)
     pi = T.pi[:, 0:1]
     cp(T.pj[:, 0:1], pi, ["pi"], ["pj0"])
@@ -264,8 +273,6 @@ def rank_program(g, core, T, topo):
     ts(T.Wu[:, :], T.W1[:, :], T.wv[:, 0:1], None, ALU.mult, None, ["W1", "kw"], ["Wu"])
     ts(T.DA[0:32, :], T.ioa[0:32, :], T.col[0:32, 0:1], 4096.0, ALU.is_equal, ALU.mult, ["ioa", "col"], ["DA"], 128)
     ts(T.SEL[:, :], T.SEL[:, :], pc, None, ALU.is_equal, None, ["SEL", "col"], ["SEL"], 512)
-    fill(T.hc[:, 0:HA], 1.0, "hca")
-    fill(T.hc[:, HA:16], 0.5, "hcb")
     ts(T.TRI[:, :], T.ioc[:, 0:128], pc, -8192.0, ALU.is_gt, ALU.mult, ["ioc", "col"], ["TRI"], 128)
     tt(T.TRI[:, :], T.TRI[:, :], T.GO[:, :], ALU.mult, ["TRI", "GO"], ["TRI"], 256)
     ts(T.c15[:, :], T.ioc[:, 0:HA], 16.0, 15.0, ALU.mult, ALU.add, ["ioc"], ["c15"])
@@ -274,22 +281,25 @@ def rank_program(g, core, T, topo):
     ts(T.RR[:, 0:K:16], T.ioc[:, 0:16], -16.0, nc, ALU.mult, ALU.add, ["ioc", "nc"], ["RR"])
     fill(T.one[0:2, :], 1.0, "one")
     fill(T.CK[0:2, 0:256], 0.5, "CK")
-    for i, c in enumerate((-2048.0, -512.0, 2048.0 - 16384.0, -8192.0)):
+    fill(T.CK[0:2, 512:768], 0.25, "CK")
+    for i, c in enumerate((-2048.0, -512.0, 2048.0 - 16384.0, -8192.0, 2048.0, 4096.0)):
         fill(T.CK[0:1, 128 * i:128 * i + 128], c, "CK")
 
     def blocks():
         for q in range(8):
             i = V.tensor_tensor(T.KB[:, 16 * q:16 * q + 16], T.kp[:, :], T.GO[:, 16 * q:16 * q + 16], ALU.mult)
         return i
-    record("V", blocks, ["kw", "GO"], ["KB"], 512)
-    for name, src, c in (("I2", "I1", 2.0), ("W8", "W4", 2.0), ("G8n", "GO", -8192.0), ("GOn", "GO", -1.0), ("I2n", "I1", -2.0),
-                         ("I1n", "I1", -1.0), ("W4n", "W4", -1.0), ("I32", "I1", 1.0), ("J32", "I1", -2.0), ("KB2", "KB", 2.0)):
+    record("V", blocks, ["z0", "GO"], ["KB"], 512)
+    for name, src, c in (("I2", "I1", 2.0), ("I8k", "I1", 8192.0), ("I8n", "I1", -8192.0), ("G8k", "GO", 8192.0),
+                         ("W8", "W4", 2.0), ("G8n", "GO", -8192.0), ("GOn", "GO", -1.0), ("I2n", "I1", -2.0),
+                         ("I1n", "I1", -1.0), ("W4n", "W4", -1.0), ("I32", "I1", 1.0), ("J32", "I1", -2.0), ("KB2", "KB", 2.0),
+                         ("Wu2", "Wu", 2.0)):
         act(T[name][:, :], T[src][:, :], [src], [name], scale=c)
     act(T.DAn[0:32, :], T.DA[0:32, :], ["DA"], ["DAn"], scale=-1.0)
     I1, I1n, GO, GOn = full("I1"), full("I1n"), full("GO"), full("GOn")
 
-    def const(i, rows=1):
-        return (T.one[0:rows, :], T.CK[0:rows, 128 * i:128 * i + 128])
+    def const(i, rows=1, w=128):
+        return (T.one[0:rows, :], T.CK[0:rows, 128 * i:128 * i + w])
 
     def wr_(buf, r):
         return buf[:, 15 - r:143 - r]
@@ -319,7 +329,12 @@ def rank_program(g, core, T, topo):
         mm(group(T[bank][:, a:b], [(full(one), T.JH[:, a:b]), (full(one), T.JL[:, a:b])], stop=False), [one, "JH", "JL"], [bank],
            b - a)
 
-    def names(q0, q1, win, wtok, t):
+    def names(q0, q1, win, wtok, t, by_scalar=False):
+        if by_scalar:
+            h = q0 // 2
+            act(hf(T.sel, h), win.indirect(hl(T.bB, 2 * t + h)), wtok + ["bB%d_%d" % (q0, t)], ["sel%d" % h], c=gat(HN))
+            cp(hf(T.Lu, h), hf(T.sel, h), ["sel%d" % h], ["Lu%d" % q for q in range(q0, q1)], HN)
+            return
         cp(T.Lu[:, 64 * q0:64 * q1], win.indirect(T.bB[:, 16 * t + 4 * q0:16 * t + 4 * q1]),
            wtok + ["bB%d_%d" % (q, t) for q in range(q0, q1)], ["Lu%d" % q for q in range(q0, q1)], gat(64 * (q1 - q0)))
 
@@ -334,9 +349,13 @@ def rank_program(g, core, T, topo):
             o, src = Y[h][:, y0 + 512 * i:y0 + 512 * i + 512], win.indirect(T.Lu[:, 64 * q + 32 * i:64 * q + 32 * i + 32])
             if i < VSHARE[step][q]:
                 cp(o, src, wtok + ["Lu%d" % q], [yt[i]], gat(512))
+                if step in INLINE:
+                    in_line("mins")
             else:
                 act(o, src, wtok + ["Lu%d" % q], [yt[i]], c=gat(512))
                 in_line("gathers")
+                if (step, q, i) in AFTER:
+                    behind(AFTER[step, q, i])
         if ybank is not None:
             if c == 1:
                 mm([(T[ybank][:, 0:HN], T.SX[0:HA, HN * h:HN * h + HN], T[sw][0:HA, :], False, False)], ["SX%d" % h, sw], [ybank], 256)
@@ -367,73 +386,41 @@ def rank_program(g, core, T, topo):
     def best(h, src, R, a=0):
         scan(T.SC[:, a + HN * h:a + HN * h + HN], full("m0"), src, ALU.mult, ALU.max, R + ["m0"], ["SC%d_%d" % (h, a)])
 
-    def offsets(out, c0, n, tok, w1=[], w2=[]):
-        ts(T.oj[:, c0:c0 + n], T.oi[:, c0:c0 + n], 4095, None, ALU.bitwise_and, None, ["oi" + tok], ["oj" + tok] + w1)
+    def offsets(out, c0, n, tok, keys, ktok, w1=[], w2=[], shift=0):
+        ts(T.oj[:, c0:c0 + n], keys, 4095 << shift, shift, ALU.bitwise_and, ALU.arith_shift_right, [ktok], ["oj" + tok] + w1)
         ts(out, T.oj[:, c0:c0 + n], -1.0, 4095.0, ALU.mult, ALU.add, ["oj" + tok], ["off" + tok] + w2)
 
-    def settle(key):
-        r_ = T.pR1[:, 128:128 + K]
-        mm(group(r_, [(I1, full("NM")), (I1n, full("kr"))], stop=False), ["NM", "I1n", "kr0", "kr1"], ["pR1"], 256)
-        for j in range(4):
-            cols = range(4 * j, 4 * j + 4)
-
-            def fn(cols=cols):
-                for a in cols:
-                    i = V.tensor_scalar(T.E[:, a, 0:K - 16 * a], T.kr[:, 16 * a:K], key(a), 0.0, ALU.add, ALU.is_equal)
-                return i
-            etok = ["E0_%d" % j, "E1_%d" % j]
-            record("V", fn, ["kr0", "kr1", "s1%d" % (j // 2)], etok, sum(max(64, 128 - 8 * a) for a in cols))
-            mm([(r_[:, 16 * a + 16:K], full("G8n"), T.E[:, a, 16:K - 16 * a], False, False) for a in cols if a < 15]
-               + [(r_[:, 64 * j:64 * j + 64], full("TRI"), T.E[:, 4 * j:4 * j + 4, 0:16], False, j == 3)],
-               etok + ["G8n", "TRI"], ["pR1"], 32 + sum(max(32, 120 - 8 * a) for a in cols))
-        scan(full("s2"), full("RR"), r_, ALU.min, ALU.max, ["RR", "pR1"], ["s20", "s21"], K)
-        ts(full("fo"), T.s2[:, 15:K:16], -1.0, 2048.0, ALU.mult, ALU.add, ["s20", "s21"], ["fo0", "fo1"])
-        tt(T.TB[:, 0:TBW].indirect(full("fo")), full("Cs"), full("Q"), ALU.max, ["fo0", "Cs0", "Cs1", "Q0", "Q1"],
-           ["TB", "TBc", "TBo", "TBd"], 60 + 3.5 * K)
-
-    def write(h, rec, old, rtok, oldf, oftok, obias, newname, ntok, npb, nptok, c0, key, step):
+    def write(h, rec, old, rtok, oldf, oftok, obias, newname, ntok, npb, nptok, c0, key):
         r_, hh = T["pR%d" % h], "%d" % h
         xb, cb = ("pU0", "pU0") if h == 0 else ("pX0", "pX1")
         x_, u_, oh = T[xb], T[cb][:, 256:384], hf(T.oh, h)
         mm(group(x_[:, c0:c0 + 128], [(I1, rec), (I1, old), (I1n, npb)])
-           + group(x_[:, 384:512], [const(2), (GO, newname), (I1, oh), (I1, npb)]),
-           rtok + [nptok, ntok, "oh" + hh, "I1n", "GO", "one", "CK"], [xb], 448)
+           + group(x_[:, 384:512], [const(2), (GO, newname), (full("I8k"), oh), (I1, npb)]),
+           rtok + [nptok, ntok, "oh" + hh, "I1n", "I8k", "GO", "one", "CK"], [xb], 448)
         act(hf(T.a1, h), x_[:, c0:c0 + 128], [xb], ["a1" + hh], bias=M1, scale=HALF)
         act(hf(T.Hs, h), hf(T.a1, h), ["a1" + hh], ["Hs" + hh], bias=-M1)
         tt(hf(T.Q, h), hf(T.Hs, h), x_[:, 384:512], ALU.max, ["Hs" + hh, xb], ["Q" + hh], HN)
-        mm(group(u_, [(I1n, oh), (I1, npb)], stop=False), [nptok, "oh" + hh], [cb])
+        mm(group(u_, [(full("I8n"), oh), (I1, npb)], stop=False), [nptok, "oh" + hh, "I8n"], [cb])
         mm(group(u_, [(full("I32"), oldf)], start=False), [oftok, "I32"], [cb], 256)
         act(hf(T.Cs, h), u_, [cb], ["Cs" + hh], bias=obias)
-        if step in MERGE:
-            if h == 1:
-                settle(key)
-            return
         mm(group(r_[:, 128:256], [(I1, NM1), (I1n, hf(T.kr, h))], stop=False), ["NM", "I1n", "kr" + hh], ["pR" + hh], 128)
-        top = HN * h + HN
-        cuts = (0, 4, 8) if h == 0 else (0, 4, 8, 12, 16)
-        for j in range(len(cuts) - 1):
-            cols = range(cuts[j], cuts[j + 1])
-            own = cols[0] >= HA * h
-            e0, etok = 128 * (not own), "E%d_%d" % (h, j)
+        for j in range(len(CUTS) - 1):
+            cols, etok = range(CUTS[j], CUTS[j + 1]), "E%d_%d" % (h, j)
 
-            def fn(cols=cols, e0=e0):
+            def fn(cols=cols):
                 for a in cols:
-                    lo = max(16 * a, HN * h)
-                    i = V.tensor_scalar(T.E[:, a, e0:e0 + top - lo], T.kr[:, lo:top], key(a), 0.0, ALU.add, ALU.is_equal)
+                    i = V.tensor_scalar(T.E[:, HA * h + a, 0:HN - 16 * a], hf(T.kr, h)[:, 16 * a:HN], key(HA * h + a), 0.0,
+                                        ALU.add, ALU.is_equal)
                 return i
-            record("V", fn, ["kr" + hh, "s1%d" % (cols[0] // HA)], [etok], 256)
-            lst = []
-            for a in cols:
-                lo = max(16 * a + 16, HN * h)
-                if lo < top:
-                    lst.append((r_[:, 128 + lo - HN * h:256], full("G8n"), T.E[:, a, e0 + 16 * own:e0 + 16 * own + top - lo], False, False))
-            a = cols[0]
-            if own:
-                lst.append((r_[:, 128 + 16 * a - HN * h:192 + 16 * a - HN * h], full("TRI"), T.E[:, a:a + 4, 0:16],
-                            False, j == len(cuts) - 2))
-            mm(lst, [etok, "G8n", "TRI"], ["pR" + hh], 200)
+            record("V", fn, ["kr" + hh, "s1" + hh], [etok], 64 * len(cols))
+            mm([(r_[:, 144 + 16 * a:256], full("G8n"), T.E[:, HA * h + a, 16:HN - 16 * a], False, False) for a in cols if a < HA - 1]
+               + [(r_[:, 128 + 16 * CUTS[j]:128 + 16 * CUTS[j + 1]], full("TRI"), T.E[:, HA * h + CUTS[j]:HA * h + CUTS[j + 1], 0:16],
+                   False, j == len(CUTS) - 2)], [etok, "G8n", "TRI"], ["pR" + hh], 40 * len(cols) + 32)
         scan(hf(T.s2, h), hf(T.RR, h), r_[:, 128:256], ALU.min, ALU.max, ["RR", "pR" + hh], ["s2" + hh])
         ts(hl(T.fo, h), dg(T.s2, h), -1.0, 2048.0, ALU.mult, ALU.add, ["s2" + hh], ["fo" + hh])
+
+    def scatter(h):
+        hh = "%d" % h
         tt(T.TB[:, 0:TBW].indirect(hl(T.fo, h)), hf(T.Cs, h), hf(T.Q, h), ALU.max, ["fo" + hh, "Cs" + hh, "Q" + hh],
            ["TB", "TBc", "TBo", "TBd"], 60 + 3.5 * HN)
 
@@ -450,22 +437,24 @@ def rank_program(g, core, T, topo):
         cwin, ctok = (T.CE[:, :], ["CE"]) if t == 0 else (cells, TBC)
         pwin, ptok = (T.PXB[:, 0:W], ["PXB"]) if t == 0 else (T.TB[:, 0:W], ["TB"])
         zt = ["z0_%d" % t, "z1_%d" % t]
-        if not ZJOIN:
-            plus[0] = BON["z"]
+        plus[0] = BON["z"] if t else BON["z0"]
+        if t == 0:
+            send("y", t, hf(T.xs, 3), hf(T.xr, 3), zt)
+            send("z", t, hf(T.xs, 2), hf(T.xr, 2), zt)
+        else:
             send("z", t, sl(T.xs, t, XW, K, XW), sl(T.xr, t, XW, K, XW), zt)
-            plus[0] = 0
+        plus[0] = 0
         for q0, q1 in XPARTS:
             h, qq, a, b = q0 // 2, "q%d" % q0, 64 * q0, 64 * q1
             kb, c0, c1 = "pK%d" % h, a - HN * h, b - HN * h
             key_start(kb, "I1", c0, c1)
-            names(q0, q1, cwin, ctok, t)
+            names(q0, q1, cwin, ctok, t, NA[0] and t and h)
             for q in range(q0, q1):
                 spread(0, q, sl(T.xs, t, XW, K + a, K + b), zt[h])
                 big(0, q, q == q1 - 1, pwin, ptok, None, None, "W4")
             plus[0] = BON["x"]
             scan(T.SC[:, a:b], T.m0[:, 0:b - a], T[kb][:, c0:c1], ALU.mult, ALU.max, [kb, "m0"], ["SC%d_0" % h], b - a)
-            cp(T.oi[:, 4 * q0:4 * q1], T.SC[:, a + 15:b:16], ["SC%d_0" % h], ["oi" + qq, "oi%d" % h])
-            offsets(T.off[:, 4 * q0:4 * q1], 4 * q0, 4 * (q1 - q0), qq, ["oj%d" % h], ["off%d" % h])
+            offsets(T.off[:, 4 * q0:4 * q1], 4 * q0, 4 * (q1 - q0), qq, T.SC[:, a + 15:b:16], "SC%d_0" % h, ["oj%d" % h], ["off%d" % h])
             (cp if XV[h] else act)(sl(T.xs, t, XW, a, b), Y[h][:, 0:PAD + 16 * c1].indirect(T.off[:, 4 * q0:4 * q1]),
                                    ytoks(h, q1 - 2 * h) + ["off" + qq], ["xs" + qq], c=gat(b - a))
             if ZJOIN and q1 == 4:
@@ -487,13 +476,20 @@ def rank_program(g, core, T, topo):
                 o, i = T.TB[:, 512 * q:512 * q + 512], T.PXB[:, 512 * q:512 * q + 512]
                 (cp if q < WV else act)(o, i, ["PXB"], ["TB%d" % q], c=512)
         ptok = ["TB"] + (["TB%d" % q for q in range(8)] if t == 0 else [])
-        rz = "rz_%d" % t
-        na, par, ntx = counts(T.ms, t)
-        na0, par0, ntx0 = counts(T.mr, t - 1 if t else RO)
-        was = ["rm_%d" % (t - 1)] if t else ["first0", "first1", "first2"]
-        tt(na, na0, ntx0, ALU.add, was, ["za%d" % t])
-        tt(par, par0, ntx0, ALU.is_equal, was, ["zb%d" % t])
-        ts(full("thr"), par, 2.0, -12.0, ALU.mult, ALU.add, ["zb%d" % t], ["thr"])
+        rz = ("rz_%d" % t, "rz_%d" % t if t else "ry_0")
+        na, par, ntx = counts(T.fs, t)
+        na0, par0, ntx0 = counts(T.fr, t - 1 if t else RO)
+        was = ["rf1_%d" % (t - 1)] if t else ["first0", "first1", "first2"]
+        if CA:
+            mm(group(T.pR1[:, 384:400], [(I1, na0), (I1, ntx0)]) + group(T.pR1[:, 400:416], [(I1, par0), (I1, ntx0)]),
+               was + ["I1"], ["pR1"])
+            act(na, T.pR1[:, 384:400], ["pR1"], ["za%d" % t], c=64)
+            act(par, T.pR1[:, 400:416], ["pR1"], ["zb%d" % t], f=AF.Abs, bias=-1.0, c=64)
+            act(full("thr"), par, ["zb%d" % t], ["thr"], scale=2.0, bias=-12.0, c=64)
+        else:
+            tt(na, na0, ntx0, ALU.add, was, ["za%d" % t])
+            tt(par, par0, ntx0, ALU.is_equal, was, ["zb%d" % t])
+            ts(full("thr"), par, 2.0, -12.0, ALU.mult, ALU.add, ["zb%d" % t], ["thr"])
         rxs = ["rx%d_%d" % (q, t) for q in range(4)]
         for q0, q1 in XPARTS:
             h, qq, a, b = q0 // 2, "q%d" % q0, 4 * q0, 4 * q1
@@ -501,14 +497,14 @@ def rank_program(g, core, T, topo):
             pu = T["pU" + hh]
             plus[0] = BON["b"]
             xq = hf(T.xr, h, t, XW)
-            mm(group(pu[:, a:b], [(wr_(T.Wu, i), xq[:, 16 * (i % 8) + i // 8:16 * (i % 8) + 16:2]) for i in range(16)]),
-               [rxs[q0], "Wu"], ["pU" + hh], 512)
+            mm(group(pu[:, a:b], [const(4, 2, HA)]
+                     + [(wr_(T.Wu2, i), xq[:, 16 * (i % 8) + i // 8:16 * (i % 8) + 16:2]) for i in range(16)]),
+               [rxs[q0], "Wu2", "one", "CK"], ["pU" + hh], 544)
             behind("offq%d" % XPARTS[-1][0])
-            cp(T.bi[:, a:b], pu[:, a:b], ["pU" + hh], ["bi" + qq])
-            ts(T.bj[:, a:b], T.bi[:, a:b], CELLS - 1, None, ALU.bitwise_and, None, ["bi" + qq], ["bj" + qq])
-            ts(T.bB[:, 16 * u + a:16 * u + b], T.bj[:, a:b], 2.0, None, ALU.mult, None, ["bj" + qq],
+            ts(T.bf[:, a:b], pu[:, a:b], 2.0 ** 34 - 1024, 2.0 ** 34, ALU.add, ALU.subtract, ["pU" + hh], ["bf" + qq])
+            tt(T.bB[:, 16 * u + a:16 * u + b], pu[:, a:b], T.bf[:, a:b], ALU.subtract, ["pU" + hh, "bf" + qq],
                ["bB%d_%d" % (q, u) for q in range(q0, q1)])
-            names(q0, q1, cells, TBC, u)
+            names(q0, q1, cells, TBC, u, NA[1] and h)
             plus[0] = 0
             if q0 % 2 == 0:
                 key_start("pK" + hh, "I2")
@@ -542,27 +538,23 @@ def rank_program(g, core, T, topo):
             scan(hf(T.cs, h), full("m0"), hf(T.sg, h), ALU.mult, ALU.add, ["m0", "sg" + hh], ["cs" + hh], 64)
             zc = "zc%d_%d" % (h, t)
             tt(hl(ntx, h), dg(T.cs, h), hl(T.thr, h), ALU.is_lt, ["cs" + hh, "thr"], [zc])
-            cp(hl(T.nu, h), hl(ntx, h), [zc], ["nu" + hh])
+            tt(hl(T.nu, h), dg(T.cs, h), hl(T.thr, h), ALU.is_lt, ["cs" + hh, "thr"], ["nu" + hh])
             act(live, T.NP[:, 0:16].indirect(hl(T.nu, h)), ["NP", "nu" + hh], ["live" + hh], c=gat(HN))
             tt(hf(T.ne, h), hf(T.SC, 2 + 2 * h).indirect(full("c15")), hf(T.nk, h), ALU.not_equal,
                ["SC%d_%d" % (h, sj), "c15", "nk" + hh], ["ne" + hh], gat(HN))
             tt(hf(T.ks, h), hf(T.ne, h), pk[:, 0:HN], ALU.mult, ["ne" + hh, "pK" + hh], ["ks" + hh], HN)
             best(h, hf(T.ks, h), ["ks" + hh], sm)
             offj, offm = T.of2[:, cj:cj + HA], T.of2[:, cm:cm + HA]
-            if h == 0 and JOIN:
-                tt(T.oi[:, 16:32], T.SC[:, K + 15:2 * K:16], full("hc"), ALU.mult,
-                   ["SC0_%d" % sj, "SC0_%d" % sm, "hca", "hcb"], ["oij0"])
-                offsets(T.of2[:, 0:16], 16, 16, "j0", [], ["offm0"])
+            offsets(offj, 16 + cj, HA, "j" + hh, dg(T.SC, h, sj), "SC%d_%d" % (h, sj))
+            offsets(offm, 16 + cm, HA, "m" + hh, dg(T.SC, h, sm), "SC%d_%d" % (h, sm), shift=1)
+            tt(hf(T.fs, h, t, MW), yw.indirect(offm), x, ALU.max, ytoks(h) + ["offm" + hh] + rx, ["fs" + hh], gat(HN))
+            if h == 0:
+                send("f0", t, hf(T.fs, 0, t, MW), hf(T.fr, 0, t, MW), ["fs0"])
             else:
-                cp(T.oi[:, 16 + cj:24 + cj], dg(T.SC, h, sj), ["SC%d_%d" % (h, sj)], ["oij" + hh])
-                offsets(offj, 16 + cj, HA, "j" + hh)
-                ts(T.oi[:, 16 + cm:24 + cm], dg(T.SC, h, sm), 0.5, None, ALU.mult, None, ["SC%d_%d" % (h, sm)], ["oim" + hh])
-                offsets(offm, 16 + cm, HA, "m" + hh)
-            tt(hf(T.fs, h, t), yw.indirect(offm), x, ALU.max, ytoks(h) + ["offm" + hh] + rx, ["fs" + hh], gat(HN))
-            send("f" + hh, t, hf(T.fs, h, t), hf(T.fr, h, t), ["fs" + hh])
+                send("f1", t, sl(T.fs, t, MW, HN, MW), sl(T.fr, t, MW, HN, MW), ["fs1", "za%d" % t, "zb%d" % t, "zc0_%d" % t, zc])
             plus[0] = BON["t0"] * (1 - h)
             tt(MS, ohw.indirect(offj), hf(T.Lf, h), ALU.mult, ["OH", "OHz", "offj" + hh, "Lf"], ["MS" + hh], gat(HN))
-            act(hf(T.oh, h), ohw.indirect(offj), ["OH", "OHz", "offj" + hh], ["oh" + hh], scale=8192.0, c=gat(HN))
+            act(hf(T.oh, h), ohw.indirect(offj), ["OH", "OHz", "offj" + hh], ["oh" + hh], c=gat(HN))
             act(hf(T.yj, h), yw.indirect(offj), ytoks(h) + ["offj" + hh], ["yj" + hh], c=gat(HN))
             pr = T["pR" + hh][:, 256:384]
             mm(group(pr, [(I1, NM1)], stop=False), ["NM"], ["pR" + hh])
@@ -577,31 +569,46 @@ def rank_program(g, core, T, topo):
                 mm(group(pr, [(I1n, hf(T.kr, h))], start=False), ["I1n", "kr" + hh], ["pR" + hh])
                 scan(hf(T.s1, h), hf(T.RR, h), pr, ALU.min, ALU.max, ["RR", "pR" + hh], ["s1" + hh])
             if h == 1:
-                tt(sl(T.ms, t, MW, 0, K), ohw.indirect(T.of2[:, 8:24]), full("Lf"), ALU.mult,
+                plus[0] = BON["m"]
+                tt(sl(T.ms, t), ohw.indirect(T.of2[:, 8:24]), full("Lf"), ALU.mult,
                    ["OH", "OHz", "offm0", "offm1", "Lf"], ["ms"], gat(K))
-                send("m", t, sl(T.ms, t, MW), sl(T.mr, t, MW), ["ms", "za%d" % t, "zb%d" % t, "zc0_%d" % t, zc])
+                send("m", t, sl(T.ms, t), sl(T.mr, t), ["ms"])
+                plus[0] = 0
             z0 = sl(T.xr, t, XW, K + HN * h, K + HN * h + HN)
             mm(group(pk[:, 256:384], [(I1, z0), (I1n, live)]) + group(pk[:, 384:512], [(I1, hf(T.yj, h)), (I1n, live)]),
-               [rz, "live" + hh, "yj" + hh], ["pK" + hh])
+               [rz[h], "live" + hh, "yj" + hh], ["pK" + hh])
             act(T.E12[:, K * h:K * h + K], pk[:, 256:512], ["pK" + hh], ["E12" + hh], f=AF.Relu, c=K)
             write(h, x, hf(T.yj, h), rx + ["yj" + hh], hf(T.Lf, h), "Lf", 2048.0 - 8192.0, hf(T.nr, h, t), "rn_%d" % t,
-                  live, "live" + hh, 128, key_list if LIST else key_scan, 1)
+                  live, "live" + hh, 128, key_list if LIST else key_scan)
+            scatter(h)
         rm = "rm_%d" % t
         for h in range(2):
             hh = "%d" % h
-            rf, f = "rf%d_%d" % (h, t), hf(T.fr, h, t)
+            rf, f = "rf%d_%d" % (h, t), hf(T.fr, h, t, MW)
             pu, pk, pr = T["pU" + hh], T["pK" + hh], T["pR" + hh]
             plus[0] = BON["p"]
-            mm(group(pu[:, 256:384], [const(0, 2), (full("KB"), f)]) + group(pk[:, 128:256], [const(0)], stop=False)
-               + reorder2(pk[:, 128:256], full("KB"), f, False), [rf, "KB", "one", "CK"], ["pU" + hh, "pK" + hh], 448)
-            behind("fs1")
+            if PV[h]:
+                mm(group(pk[:, 128:256], [const(5, 2)], stop=False) + reorder2(pk[:, 128:256], full("KB"), f, True),
+                   [rf, "KB", "one", "CK"], ["pK" + hh], 320)
+                behind("fs1")
+                ts(hf(T.md, h), pk[:, 128:256], 2.0 ** 35 - 2048, 2.0 ** 35, ALU.add, ALU.subtract, ["pK" + hh], ["md" + hh], HN)
+                tt(hf(T.Lu, h), pk[:, 128:256], hf(T.md, h), ALU.subtract, ["pK" + hh, "md" + hh],
+                   ["Lu%d" % (2 * h), "Lu%d" % (2 * h + 1)], HN)
+                plus[0] = 0
+                mm(group(pu[:, 256:384], [const(0, 2), (full("KB"), f)]), [rf, "KB", "one", "CK"], ["pU" + hh])
+                behind("fs1")
+            else:
+                mm(group(pu[:, 256:384], [const(0, 2), (full("KB"), f)]) + group(pk[:, 128:256], [const(0)], stop=False)
+                   + reorder2(pk[:, 128:256], full("KB"), f, False), [rf, "KB", "one", "CK"], ["pU" + hh, "pK" + hh], 448)
+                behind("fs1")
             if HV[h]:
                 ts(hf(T.hi, h), pu[:, 256:384], M4096, M4096, ALU.add, ALU.subtract, ["pU" + hh], ["hi" + hh], HN)
             else:
                 act(hf(T.a2, h), pu[:, 256:384], ["pU" + hh], ["a2" + hh], bias=M4096)
                 act(hf(T.hi, h), hf(T.a2, h), ["a2" + hh], ["hi" + hh], bias=-M4096)
-            mm(reorder2(pk[:, 128:256], I1n, hf(T.hi, h), True), ["hi" + hh, "I1n"], ["pK" + hh], 256)
-            ts(hf(T.Lu, h), pk[:, 128:256], 2048.0, None, ALU.add, None, ["pK" + hh], ["Lu%d" % (2 * h), "Lu%d" % (2 * h + 1)], HN)
+            if not PV[h]:
+                mm(reorder2(pk[:, 128:256], I1n, hf(T.hi, h), True), ["hi" + hh, "I1n"], ["pK" + hh], 256)
+                ts(hf(T.Lu, h), pk[:, 128:256], 2048.0, None, ALU.add, None, ["pK" + hh], ["Lu%d" % (2 * h), "Lu%d" % (2 * h + 1)], HN)
             plus[0] = 0
             sums(h, f, [rf])
             key_start("pK" + hh, "I1")
@@ -613,10 +620,13 @@ def rank_program(g, core, T, topo):
             for q in (2 * h, 2 * h + 1):
                 spread(2, q, f, rf)
                 big(2, q, q % 2, T.TB[:, 0:W], ["TB"], "pK" + hh, "W4n", "W8", "DAn")
-        ts(full("dk"), counts(T.mr, t)[2], -TOP, TOP, ALU.mult, ALU.add, [rm], ["dk"])
+        if CA:
+            act(full("dk"), counts(T.fr, t)[2], ["rf1_%d" % t], ["dk"], scale=-TOP, bias=TOP, c=64)
+        else:
+            ts(full("dk"), counts(T.fr, t)[2], -TOP, TOP, ALU.mult, ALU.add, ["rf1_%d" % t], ["dk"])
         for h in range(2):
             hh = "%d" % h
-            rf, f = "rf%d_%d" % (h, t), hf(T.fr, h, t)
+            rf, f = "rf%d_%d" % (h, t), hf(T.fr, h, t, MW)
             pu, pk = T["pU" + hh], T["pK" + hh]
             offj, npb, oh, w_, MS = hl(T.off, h), hf(T.np3, h), hf(T.oh, h), hf(T.ws, h, t), hf(T.MS, h)
             otok = ["offq%d" % q0 for q0, q1 in XPARTS if q0 // 2 == h]
@@ -624,30 +634,39 @@ def rank_program(g, core, T, topo):
             best(h, pk[:, 0:HN], ["pK" + hh])
             ts(hl(T.nu, h), dg(T.SC, h), 4096.0 * (4080 - TH2 + 1), None, ALU.is_lt, None, ["SC%d_0" % h], ["nu" + hh])
             tt(hl(T.oi, h), dg(T.SC, h), hl(T.dk, h), ALU.max, ["SC%d_0" % h, "dk"], ["oi" + hh])
-            offsets(offj, HA * h, HA, hh, [], otok)
+            offsets(offj, HA * h, HA, hh, hl(T.oi, h), "oi" + hh, [], otok)
             act(npb, T.NP[:, 0:16].indirect(hl(T.nu, h)), ["NP", "nu" + hh], ["np" + hh], c=gat(HN))
             act(w_, Y[h][:, 0:YW].indirect(offj), ytoks(h) + ["off" + hh], ["ws" + hh], c=gat(HN))
             send("w" + hh, t, w_, hf(T.wr, h, t), ["ws" + hh])
             plus[0] = BON["t0"] * (1 - h)
-            act(oh, ohw.indirect(offj), ["OH", "OHz", "off" + hh], ["oh" + hh], scale=8192.0, c=gat(HN))
+            act(oh, ohw.indirect(offj), ["OH", "OHz", "off" + hh], ["oh" + hh], c=gat(HN))
             mm(group(pu[:, 0:128], [const(0), (full("KB"), f), (I1n, hf(T.hi, h))], stop=False), [rf, "hi" + hh], ["pU" + hh])
             mm(group(pu[:, 0:128], [(I1, npb)], start=False), ["np" + hh], ["pU" + hh])
-            tt(hf(T.sel, h), pu[:, 0:128], hf(T.Lcc, h), ALU.min, ["pU" + hh, "Lcc" + hh], ["sel" + hh], HN)
-            tt(MS, ohw.indirect(offj), hf(T.sel, h), ALU.mult, ["OH", "OHz", "off" + hh, "sel" + hh], ["MS" + hh], gat(HN))
+            if h < PSEL:
+                tt(pu[:, 0:128], pu[:, 0:128], hf(T.Lcc, h), ALU.min, ["Lcc" + hh], ["pU" + hh], HN)
+                tt(MS, oh, pu[:, 0:128], ALU.mult, ["oh" + hh, "pU" + hh], ["MS" + hh], HN)
+            else:
+                tt(hf(T.sel, h), pu[:, 0:128], hf(T.Lcc, h), ALU.min, ["pU" + hh, "Lcc" + hh], ["sel" + hh], HN)
+                tt(MS, ohw.indirect(offj), hf(T.sel, h), ALU.mult, ["OH", "OHz", "off" + hh, "sel" + hh], ["MS" + hh], gat(HN))
             pr = T["pR" + hh][:, 0:128]
-            mm(group(pr, [(I1, NM1), const(3), (GO, oh)], stop=False), ["oh" + hh, "NM"], ["pR" + hh])
-            mm(group(pu[:, 128:256], [(GOn, oh)], stop=False), ["oh" + hh, "GOn"], ["pU" + hh])
+            mm(group(pr, [(I1, NM1), const(3), (full("G8k"), oh)], stop=False), ["oh" + hh, "NM", "G8k"], ["pR" + hh])
+            mm(group(pu[:, 128:256], [(full("G8n"), oh)], stop=False), ["oh" + hh, "G8n"], ["pU" + hh])
             mm(group(pu[:, 128:256], [(GO, MS)], start=False), ["MS" + hh], ["pU" + hh])
             mm(group(pr, [(GOn, MS)], start=False), ["MS" + hh, "GOn"], ["pR" + hh])
             ts(hf(T.kr, h), pu[:, 128:256], 8192.0, None, ALU.add, None, ["pU" + hh], ["kr" + hh], HN)
             scan(hf(T.s1, h), hf(T.RR, h), pr, ALU.min, ALU.max, ["RR", "pR" + hh], ["s1" + hh])
+            plus[0] += BON["k"]
             ts(hl(T.ku, h), dg(T.s1, h), -1.0, 2048.0, ALU.mult, ALU.add, ["s1" + hh], ["ku" + hh])
+            plus[0] -= BON["k"]
             act(hf(T.OLD, h), T.TB[:, 0:TBW].indirect(hl(T.ku, h)), ["TB", "TBc", "TBo", "TBd", "ku" + hh], ["OLD" + hh], c=gat(HN))
-            write(h, f, w_, [rf, "ws" + hh], hf(T.OLD, h), "OLD" + hh, -8192.0, hf(T.mr, h, t, MW), rm, npb, "np" + hh, 0, key_scan, 2)
+            write(h, f, w_, [rf, "ws" + hh], hf(T.OLD, h), "OLD" + hh, -8192.0, hf(T.mr, h, t), rm, npb, "np" + hh, 0, key_scan)
+            if h == 1:
+                scatter(0)
+                scatter(1)
             plus[0] = 0
             e = T.E12[:, K * h:K * h + HN], T.E12[:, K * h + HN:K * h + K]
             mm(group(pk[:, 128:256], [(I1, sl(T.xr, t, XW, K + HN * h, K + HN * h + HN)), (I1, e[0]), (full("I2n"), e[1])], stop=False),
-               [rz, "E12" + hh, "I2n"], ["pK" + hh])
+               [rz[h], "E12" + hh, "I2n"], ["pK" + hh])
             mm(group(pk[:, 128:256], [(I1, hf(T.wr, h, t))], start=False), ["rw%d_%d" % (h, t)], ["pK" + hh])
             late.append(len(ops) - 1)
             if h == 1 and GUARD:
@@ -659,12 +678,13 @@ def rank_program(g, core, T, topo):
     for i, fn in enumerate((cp, act)):
         fn(T.YC[:, 512 * i:512 * i + 512], T.TB[:, W + 1024 * i:W + 1024 * i + 1024:2], ["TBc"], ["YC%d" % i], c=512)
     store("S", T.yc[:, :], full("YC"), ["YC0", "YC1"], 4000)
-    cp(full("yvf"), T.bj[:, 16:32], ["bjA"], ["yvf"])
     tt(full("t1"), na, ntx, ALU.add, ["za%d" % t, "zc0_%d" % t, "zc1_%d" % t], ["t1"])
-    ts(full("au"), full("t1"), -1.0, float(RO), ALU.mult, ALU.add, ["t1"], ["au"])
-    cp(full("ar"), full("ioc").indirect(full("au")), ["au", "ioc"], ["ar"], gat(K))
-    store("S", T.yz[:, :], sl(T.xs, RO, XW, K, XW), ["z0_%d" % RO, "z1_%d" % RO])
-    store("S", T.yv[:, :], full("yvf"), ["yvf"])
+    for h in range(2):
+        cp(hl(T.yvf, 1 - h), hl(T.bj, 2 + h), ["bjA"], ["yvf%d" % h])
+        ts(hl(T.au, 1 - h), hl(T.t1, h), -1.0, float(RO), ALU.mult, ALU.add, ["t1"], ["au%d" % h])
+        store("S", hf(T.yz, 1 - h), hf(T.xs, 2 + h, RO, XW), ["z%d_%d" % (h, RO)])
+    cp(full("ar"), full("ioc").indirect(full("au")), ["au0", "au1", "ioc"], ["ar"], gat(K))
+    store("S", T.yv[:, :], full("yvf"), ["yvf0", "yvf1"])
     for q in range(8):
         store("S", T.ya[q:q + 1, :], T.ar[16 * q:16 * q + 1, :], ["ar"])
 

from concourse.mybir import AluOpType, ActivationFunctionType
ALU = AluOpType
AF = ActivationFunctionType

N, W, CELLS, K, RO, TH1, TH2 = 4, 4096, 1024, 256, 4, 256, 600
HN, HA, PAD = 128, 8, 16
SP = W + 2 * CELLS
TBW = SP + K
YW = PAD + 16 * HN
M1 = 1.5 * 2.0 ** 23
M1024 = 1.5 * 2.0 ** 33
M4096 = 1.5 * 2.0 ** 35
HALF = 0.5 - 2.0 ** -12
XW, MW = 512, 304
TOP = 2.0 ** 24 - 1
XPARTS = ((0, 2), (2, 4))
VSHARE = ((1, 0, 1, 0), (1, 0, 1, 0), (1, 1, 1, 0))
WIDE = ((1, 3), (1, 3), (1, 3))
JOIN, MG, XV, HV, ZJOIN, LIST, GUARD, WV = 1, 2, (0, 0), (0, 0), 0, 1, 1, 1
PV = (0, 0)
PSEL, NA, CA, AFTER = 1, (0, 0), 0, {(0, 3, 1): "xsq0"}
CUTS = (0, 4, 8)
RELAYED, HAND = ("z", "n", "m"), 3500
BON = {"x": 1000, "b": 0, "f": 0, "p": 0, "w": 500, "t0": 0, "lf": 0, "z": -3000, "k": -500, "z0": 30000, "m": 0}
INLINE, SOON = (), {}
LOOKS, PASSES = (0.25,), 3
HOP, FLIGHT, ISSUE = 230, 5000, 800
LOADS = (2200, 4000, 2400, 6000, 3500)


def _s(cols, dtype):
    return ("sbuf", [128, cols], dtype)


BF, F32, I32, U16, F16 = "bfloat16", "float32", "int32", "uint16", "float16"
SCRATCH = {
    "TB": _s(TBW, F32), "PXB": _s(W, BF), "CE": _s(CELLS, I32), "NP": _s(16, BF), "OH": _s(YW, BF),
    "Y0": _s(YW, BF), "Y1": _s(YW, BF), "MN": _s(W, BF), "E": ("sbuf", [128, 16, 256], BF),
    "YC": _s(CELLS, F32), "xT": _s(128, BF), "SEL": _s(1024, BF),
    "vi": _s(16, I32), "VX": _s(512, F16), "kp": _s(16, BF), "wv": _s(8, BF), "KB": _s(128, BF), "KB2": _s(128, BF),
    "pi": _s(16, I32), "pj": _s(16, I32), "col": _s(16, F32), "ioc": _s(256, F32), "ioa": _s(128, F32), "iok": _s(128, F32),
    "ioe": _s(128, F32), "GE": _s(128, BF), "RS": _s(8, BF), "rep": _s(8, U16),
    "W1": _s(144, BF), "W4": _s(144, BF), "W8": _s(144, BF), "W4n": _s(144, BF), "Wu": _s(144, BF),
    "GO": _s(128, BF), "GOn": _s(128, BF), "G8n": _s(128, BF), "G8k": _s(128, BF), "I8k": _s(128, BF), "I8n": _s(128, BF), "TRI": _s(128, BF),
    "I1": _s(128, BF), "I2": _s(128, BF), "I2n": _s(128, BF), "I1n": _s(128, BF),
    "I32": _s(128, F32), "J32": _s(128, F32), "one": _s(128, BF), "CK": _s(768, BF), "Wu2": _s(144, BF),
    "NM": _s(256, BF), "m0": _s(128, BF), "JH": _s(128, BF), "JL": _s(128, BF), "RR": _s(256, F32),
    "DA": _s(128, F32), "DAn": _s(128, F32), "c15": _s(8, U16), "bf": _s(16, F32),
    "bB": _s(16 * (RO + 1), U16), "bA": _s(16 * (RO + 1), U16), "bC": _s(16, U16),
    "bi": _s(32, I32), "bj": _s(32, I32), "yvf": _s(16, F32), "thr": _s(16, F32), "dk": _s(16, F32),
    "Lu": _s(256, U16), "Lf": _s(256, F32), "ck": _s(256, F32), "SX": _s(256, F32), "A3": _s(256, F32), "nk": _s(256, F32),
    "SC": _s(768, I32), "ne": _s(256, BF), "ks": _s(256, F32), "sg": _s(256, BF), "cs": _s(256, BF),
    "oi": _s(48, I32), "oj": _s(48, I32), "off": _s(16, U16), "of2": _s(32, U16), "nu": _s(16, U16),
    "MS": _s(256, F16), "kr": _s(256, F16), "s1": _s(256, F32), "s2": _s(256, F32), "ku": _s(16, U16), "fo": _s(16, U16),
    "oh": _s(256, BF), "live": _s(256, BF), "yj": _s(256, BF), "np3": _s(256, BF), "OLD": _s(256, F32), "sel": _s(256, F32),
    "a1": _s(256, F32), "a2": _s(256, F32), "Hs": _s(256, F32), "Cs": _s(256, F32), "Q": _s(256, F32),
    "hi": _s(256, BF), "md": _s(256, F32), "Lcc": _s(256, F32), "E12": _s(512, BF),
    "t1": _s(16, F32), "au": _s(16, U16), "ar": _s(256, F32), "ckl": _s(16, F32), "kl": _s(16, F32),
    "xs": _s(XW * (RO + 1), BF), "ns": _s(K * RO, F16), "fs": _s(MW * RO, BF), "ms": _s(K * RO, F16), "ws": _s(K * RO, BF),
    "xr": _s(XW * RO, BF), "nr": _s(K * RO, F16), "fr": _s(MW * (RO + 1), BF), "mr": _s(K * RO, F16), "wr": _s(K * RO, BF),
}
for _b in ("pX0", "pX1", "pK0", "pK1", "pU0", "pU1", "pR0", "pR1"):
    SCRATCH[_b] = ("psum", [128, 512], F32)
MSGS = ("z", "x0", "x1", "x2", "x3", "n", "f0", "f1", "m", "w0", "w1")
SEMAPHORES = (["cV", "cA", "cP", "cG", "sent", "dv0", "dce", "dz", "dpx", "dw", "outs", "outg", "ry_0"]
              + ["r%s_%d" % (m, t) for m in MSGS for t in range(RO)] + ["h%s_%d" % (m, t) for m in "znm" for t in range(RO)])


def rank_program(g, core, T, topo):
    def relay(r):
        own, to = T.cores[r], T.cores[(r + 1) % N]
        return [c for c in topo.cores_of(own) if c not in T.cores and topo.die(c) != topo.die(own) and topo.may_write(c, to)][0]

    def inner(r):
        own = T.cores[r]
        return [e for e in topo.engines(own, relay(r)) if e not in topo.engines(own, T.cores[(r + 1) % N])]

    rank = T.rank_of(core)
    if rank is None:
        for r in range(N):
            if RELAYED and core == relay(r):
                to = T.cores[(r + 1) % N]
                rid, pid = topo.addr(to)[0:2]
                for t in range(RO):
                    for m in RELAYED:
                        ap = {"z": T.xr[:, XW * t + K:XW * t + (XW if t else K + HN)], "n": T.nr[:, K * t:K * t + K], "m": T.mr[:, K * t:K * t + K]}[m]
                        g.wait_ge(T.sem["h%s_%d" % (m, t)], len(inner(r)))
                        g.remote_dma(ap, ap, T.sem["r%s_%d" % (m, t)], T.sem.sent, pid, rid, topo.mask(core, to))
                g.wait_ge(T.sem.sent, RO * len(RELAYED) * len(topo.engines(core, to)))
        return
    nxt, prv = T.cores[(rank + 1) % N], T.cores[(rank - 1) % N]
    assert topo.may_write(core, nxt) and topo.may_write(core, prv)
    V, A, P, S = g.vector, g.scalar, g.tensor, g.sync
    Q = {"V": V, "A": A, "P": P, "G": g, "S": S}

    ops, wrote, readers, lines, plus = [], {}, {}, {}, [0]

    def record(e, fn, R, Wr, cost, kind="op", sem=None):
        pre = set()
        for t in R:
            if t in wrote:
                pre.add(wrote[t])
            if t[0] == "p" and t[1].isupper():
                pre.update(d for d in readers.get(t, []) if ops[d]["e"] != e)
        for t in Wr:
            pre.update(([wrote[t]] if t in wrote else []) + readers.get(t, []))
        me = len(ops)
        ops.append({"e": e, "fn": fn, "pre": sorted(pre), "cost": cost, "kind": kind, "sem": sem, "plus": plus[0],
                    "tag": (Wr or R or ["-"])[0]})
        for t in (R if kind == "op" else []):
            readers.setdefault(t, []).append(me)
        for t in Wr:
            wrote[t] = me
            readers[t] = []
        return me

    def in_line(name):
        if name in lines:
            ops[-1]["line"] = ops[-1].get("line", []) + [lines[name]]
        lines[name] = len(ops) - 1

    def behind(tok):
        if GUARD:
            ops[-1]["line"] = ops[-1].get("line", []) + [wrote[tok]]

    def gat(n):
        return 70 + 1.5 * n

    def tt(out, a, b, alu, R, Wr, c=64):
        record("V", lambda: V.tensor_tensor(out, a, b, alu), R, Wr, c)

    def ts(out, a, s1, s2, o0, o1, R, Wr, c=64):
        if o1 is None:
            record("V", lambda: V.tensor_scalar(out, a, s1, None, o0), R, Wr, c)
        else:
            record("V", lambda: V.tensor_scalar(out, a, s1, s2, o0, o1), R, Wr, c)

    def cp(out, a, R, Wr, c=64):
        record("V", lambda: V.tensor_copy(out, a), R, Wr, c)

    def fill(ap, c, tok, cost=64):
        record("V", lambda: V.memset(ap, c), [], [tok], cost)

    def scan(out, d0, d1, o0, o1, R, Wr, c=HN):
        record("V", lambda: V.tensor_tensor_scan(out, d0, d1, 0.0, o0, o1), R, Wr, c)

    def act(out, a, R, Wr, f=AF.Identity, c=HN, **kw):
        record("A", lambda: A.activation(out, a, f, **kw), R, Wr, c)

    def mm(lst, R, Wr, c=None):
        def fn():
            for m in lst:
                i = P.matmul(m[0], m[1], m[2], bool(m[3]), bool(m[4]))
            return i
        record("P", fn, R, Wr, 64 * len(lst) if c is None else c)

    def group(out, terms, start=True, stop=True):
        n = len(terms)
        return [(out, l, r, start and i == 0, stop and i == n - 1) for i, (l, r) in enumerate(terms)]

    def iota(out, pattern, base, tok, n):
        record("G", lambda: g.iota(out, pattern, base, 0, allow_small_or_imprecise_dtypes=True), [], [tok], 160 + 2 * n)
        if tok in ("ioc", "ioe", "JH", "ioa", "iok", "JL", "SEL"):
            in_line("first")

    def send(m, t, src, dst, R):
        name = "r%s_%d" % (m, t)
        if m in RELAYED:
            to, first, engines, last = relay(rank), "h%s_%d" % (m, t), inner(rank), relay((rank - 1) % N)
        else:
            to, first, last = (prv, name, nxt) if m[0] == "w" else (nxt, name, prv)
            engines = topo.engines(core, to)
        rid, pid = topo.addr(to)[0:2]
        i = record("G", lambda: g.remote_dma(dst, src, T.sem[first], T.sem.sent, pid, rid, sum(1 << e for e in engines)), R, [],
                   ISSUE, "send", len(engines))
        if m in RELAYED:
            in_line("relayed")
        if t == 0 and m in "yz":
            in_line("first")
        record(None, None, [], [name], FLIGHT - SOON.get(m, 0) + HAND * (m in RELAYED), "land", (name, len(topo.engines(last, core))))
        ops[-1]["pre"] = [i]

    def load(e, dst, src, sem, total, tok, cost, **kw):
        i = record(e, lambda: Q[e].dma_start(dst, src, **kw).then_inc(T.sem[sem], 16), [], [], 60, "dma")
        in_line("loads" + e)
        if tok is not None:
            record(None, None, [], [tok], cost, "land", (sem, total))
            ops[-1]["pre"] = list(range(i + 1 - total // 16, i + 1))

    def store(e, dst, src, R, cost=2000):
        i = record(e, lambda: Q[e].dma_start(dst, src).then_inc(T.sem["outg" if e == "G" else "outs"], 16), R, [], 60, "out")
        record(None, None, [], [], cost, "land")
        ops[-1]["pre"] = [i]

    def sl(buf, t, w=K, a=0, b=None):
        return buf[:, t * w + a: t * w + (w if b is None else b)]

    def hf(buf, h, t=0, w=K):
        return buf[:, t * w + HN * h:t * w + HN * h + HN]

    def hl(buf, h):
        return buf[:, HA * h:HA * h + HA]

    def dg(buf, h, a=0):
        return buf[:, a + HN * h + 15:a + HN * h + HN:16]

    def full(name):
        return T[name][:, :]

    def counts(buf, t):
        return [sl(buf, t, MW, K + 16 * i, K + 16 * i + 16) for i in range(3)]

    cells = T.TB[:, W:SP]
    Y = (T.Y0, T.Y1)
    ohw = T.OH[:, 0:YW]

    load("S", hl(T.vi, 0), hl(T.v0, 1), "dv0", 32, None, 0)
    load("S", hl(T.vi, 1), hl(T.v0, 0), "dv0", 32, "vi", LOADS[0])
    load("S", T.CE[:, :], T.ce[:, :], "dce", 16, "CE", LOADS[1])
    load("A", T.kp[:, :], T.kap[:, :], "dz", 48, None, 0)
    load("A", hf(T.xs, 2), hf(T.z0, 1), "dz", 48, None, 0)
    load("A", hf(T.xs, 3), hf(T.z0, 0), "dz", 48, "z0", LOADS[2])
    load("A", T.PXB[:, 0:W // 2], T.px[:, 0:W // 2], "dpx", 32, None, 0)
    load("S", T.PXB[:, W // 2:W], T.px[:, W // 2:W], "dpx", 32, "PXB", LOADS[3])
    load("G", T.wv[:, 0:1], T.wu[:, :], "dw", 16, "kw", LOADS[4], allow_slow_non_contiguous=True)
    wrote["z0_0"] = wrote["z1_0"] = wrote["z0"]

    record("G", lambda: g.iota(T.pi[:, :], [[0, 16]], 0, 1), [], ["pi"], 200)
    iota(T.ioc[:, :], [[1, 256]], 0, "ioc", 256)
    iota(T.ioe[:, :], [[1, 16], [0, 8]], 0, "ioe", 128)
    iota(T.JH[:, :], [[-16, 8], [0, 16]], 0, "JH", 128)
    iota(T.ioa[:, :], [[1, 8], [0, 16]], 0, "ioa", 128)
    iota(T.iok[:, :], [[0, 8], [1, 16]], 0, "iok", 128)
    iota(T.JL[:, :], [[0, 8], [-1, 16]], 15, "JL", 128)
    iota(T.TB[:, W + 1:SP:2], [[2, CELLS]], 2048, "TBo", CELLS)
    iota(T.TB[:, SP:TBW], [[0, K]], 0, "TBd", K)
    iota(T.SEL[:, :], [[1, 8], [16, 8], [0, 16]], 8, "SEL", 1024)
    pc, rc, gc_, ec, sc_, qc, wc, jc, uc, nc = [T.col[:, i:i + 1] for i in range(10)]
    for i, (ap, c) in enumerate(zip(counts(T.fr, RO), (-1.0, 0.0, 1.0))):
        fill(ap, c, "first%d" % i)
    pi = T.pi[:, 0:1]
    cp(T.pj[:, 0:1], pi, ["pi"], ["pj0"])
    for i, (mask, shift) in enumerate(((15, 0), (127, 4), (1, 0), (15, 1), (7, 0))):
        ts(T.pj[:, i + 1:i + 2], pi, mask, shift, ALU.bitwise_and, ALU.arith_shift_right, ["pi"], ["pj%d" % (i + 1)])
    cp(T.col[:, 0:6], T.pj[:, 0:6], ["pj%d" % i for i in range(6)], ["col"])
    ts(wc, gc_, 16.0, 15.0, ALU.mult, ALU.add, ["col"], ["wc"])
    ts(jc, rc, -128.0, 4080.0 - PAD, ALU.mult, ALU.add, ["col"], ["jc"])
    ts(uc, gc_, 2.0, ec, ALU.mult, ALU.add, ["col"], ["uc"])
    ts(nc, rc, -1.0, -4096.0, ALU.mult, ALU.add, ["col"], ["nc"])
    ts(T.GE[:, :], T.ioe[:, :], uc, None, ALU.is_equal, None, ["ioe", "uc"], ["GE"], 128)
    ts(T.RS[:, :], T.ioc[:, 0:8], sc_, None, ALU.is_equal, None, ["ioc", "col"], ["RS"])
    ts(T.rep[:, 0:8], T.ioe[:, 0:8], qc, None, ALU.add, None, ["ioe", "col"], ["rep"])
    for h in range(2):
        bank = "pU%d" % h
        tt(hf(T.VX, h), hl(T.vi, h).indirect(T.rep[:, 0:8]), T.GE[:, :], ALU.mult, ["vi", "rep", "GE"], ["VX%d" % h], gat(HN))
        mm(group(T[bank][:, 0:HA], [(hf(T.VX, h), T.RS[:, :])]), ["VX%d" % h, "RS"], [bank], 32)
        cp(hl(T.bB, h), T[bank][:, 0:HA], [bank], ["bB%d_0" % (2 * h), "bB%d_0" % (2 * h + 1)])
    ts(T.bA[:, 0:16], T.vi[:, :], 2.0, None, ALU.mult, None, ["vi"], ["bA0"])
    cp(T.TB[:, W:SP:2], T.CE[:, :], ["CE"], ["TBc"], 1024)
    ts(T.I1[:, :], T.ioc[:, 0:128], pc, None, ALU.is_equal, None, ["ioc", "col"], ["I1"], 128)
    ts(T.W4[:, :], T.ioc[:, 0:144], wc, 4096.0, ALU.is_equal, ALU.mult, ["ioc", "wc"], ["W4"], 144)
    ts(T.JH[:, :], T.JH[:, :], jc, None, ALU.add, None, ["JH", "jc"], ["JH"])
    ts(T.m0[:, :], T.iok[:, :], 0.0, None, ALU.is_gt, None, ["iok"], ["m0"], 128)
    ts(T.OH[:, PAD:PAD + 128], T.iok[:, :], rc, None, ALU.is_equal, None, ["iok", "col"], ["OH"], 128)
    for w in (128, 256, 512, 1024):
        cp(T.OH[:, PAD + w:PAD + 2 * w], T.OH[:, PAD:PAD + w], ["OH"], ["OH"], w // 2)
    ts(T.NM[:, :], T.OH[:, PAD:PAD + K], -1.0, 2.0 ** 22, ALU.add, ALU.mult, ["OH"], ["NM"], 128)
    NM1 = T.NM[:, 0:HN]
    for buf, tok in ((T.OH, "OHz"), (T.Y0, "Yz0"), (T.Y1, "Yz1")):
        fill(buf[:, 0:PAD], 0.0, tok)
    ts(T.GO[:, :], T.ioa[:, :], gc_, None, ALU.is_equal, None, ["ioa", "col"], ["GO"], 128)
    ts(T.W1[:, :], T.W4[:, :], 2.0 ** -12, None, ALU.mult, None, ["W4"], ["W1"])
    ts(T.Wu[:, :], T.W1[:, :], T.wv[:, 0:1], None, ALU.mult, None, ["W1", "kw"], ["Wu"])
    ts(T.DA[0:32, :], T.ioa[0:32, :], T.col[0:32, 0:1], 4096.0, ALU.is_equal, ALU.mult, ["ioa", "col"], ["DA"], 128)
    ts(T.SEL[:, :], T.SEL[:, :], pc, None, ALU.is_equal, None, ["SEL", "col"], ["SEL"], 512)
    ts(T.TRI[:, :], T.ioc[:, 0:128], pc, -8192.0, ALU.is_gt, ALU.mult, ["ioc", "col"], ["TRI"], 128)
    tt(T.TRI[:, :], T.TRI[:, :], T.GO[:, :], ALU.mult, ["TRI", "GO"], ["TRI"], 256)
    ts(T.c15[:, :], T.ioc[:, 0:HA], 16.0, 15.0, ALU.mult, ALU.add, ["ioc"], ["c15"])
    ts(T.NP[:, :], T.ioc[:, 0:16], 8192.0, None, ALU.mult, None, ["ioc"], ["NP"])
    fill(T.RR[:, :], 2.0 ** 26, "RR", 256)
    ts(T.RR[:, 0:K:16], T.ioc[:, 0:16], -16.0, nc, ALU.mult, ALU.add, ["ioc", "nc"], ["RR"])
    fill(T.one[0:2, :], 1.0, "one")
    fill(T.CK[0:2, 0:256], 0.5, "CK")
    fill(T.CK[0:2, 512:768], 0.25, "CK")
    for i, c in enumerate((-2048.0, -512.0, 2048.0 - 16384.0, -8192.0, 2048.0, 4096.0)):
        fill(T.CK[0:1, 128 * i:128 * i + 128], c, "CK")

    def blocks():
        for q in range(8):
            i = V.tensor_tensor(T.KB[:, 16 * q:16 * q + 16], T.kp[:, :], T.GO[:, 16 * q:16 * q + 16], ALU.mult)
        return i
    record("V", blocks, ["z0", "GO"], ["KB"], 512)
    for name, src, c in (("I2", "I1", 2.0), ("I8k", "I1", 8192.0), ("I8n", "I1", -8192.0), ("G8k", "GO", 8192.0),
                         ("W8", "W4", 2.0), ("G8n", "GO", -8192.0), ("GOn", "GO", -1.0), ("I2n", "I1", -2.0),
                         ("I1n", "I1", -1.0), ("W4n", "W4", -1.0), ("I32", "I1", 1.0), ("J32", "I1", -2.0), ("KB2", "KB", 2.0),
                         ("Wu2", "Wu", 2.0)):
        act(T[name][:, :], T[src][:, :], [src], [name], scale=c)
    act(T.DAn[0:32, :], T.DA[0:32, :], ["DA"], ["DAn"], scale=-1.0)
    I1, I1n, GO, GOn = full("I1"), full("I1n"), full("GO"), full("GOn")

    def const(i, rows=1, w=128):
        return (T.one[0:rows, :], T.CK[0:rows, 128 * i:128 * i + w])

    def wr_(buf, r):
        return buf[:, 15 - r:143 - r]

    def reorder2(out, lhs, src, stop):
        return [(out[:, a:HN:HA], lhs, src[:, 16 * a:16 * a + 16], False, stop and a == HA - 1) for a in range(HA)]

    def spread(step, q, src, tok):
        c = q % 2
        bank = "pX%d" % c
        if q in WIDE[step]:
            mm([(T[bank][:, 0:128], src, I1, True, True)], [tok, "I1"], [bank])
            act(full("xT"), T[bank][:, 0:128], [bank], ["xT"])
            for i, bk in enumerate(("pU%d" % (q // 2), bank)):
                mm([(T[bk][:, :], full("xT"), T.SEL[:, 512 * i:512 * i + 512], True, True)], ["xT", "SEL"], [bk], 256)
        else:
            mm([(T[bank][:, a:64:HA], I1, src[:, 16 * a + 8 * c:16 * a + 8 * c + 8], True, True) for a in range(HA)],
               [tok, "I1"], [bank], 256)

    def sums(h, src, toks):
        u = T["pU%d" % h]
        mm([(u[0:HA, 128 + r:256:16], src[:, r:HN:16], T.GO[:, 0:128:16], True, True) for r in range(16)],
           toks + ["GO"], ["pU%d" % h], 128)
        act(T.SX[0:HA, HN * h:HN * h + HN], u[0:HA, 128:256], ["pU%d" % h], ["SX%d" % h], bias=-4080.0)

    def key_start(bank, one, a=0, b=HN):
        mm(group(T[bank][:, a:b], [(full(one), T.JH[:, a:b]), (full(one), T.JL[:, a:b])], stop=False), [one, "JH", "JL"], [bank],
           b - a)

    def names(q0, q1, win, wtok, t, by_scalar=False):
        if by_scalar:
            h = q0 // 2
            act(hf(T.sel, h), win.indirect(hl(T.bB, 2 * t + h)), wtok + ["bB%d_%d" % (q0, t)], ["sel%d" % h], c=gat(HN))
            cp(hf(T.Lu, h), hf(T.sel, h), ["sel%d" % h], ["Lu%d" % q for q in range(q0, q1)], HN)
            return
        cp(T.Lu[:, 64 * q0:64 * q1], win.indirect(T.bB[:, 16 * t + 4 * q0:16 * t + 4 * q1]),
           wtok + ["bB%d_%d" % (q, t) for q in range(q0, q1)], ["Lu%d" % q for q in range(q0, q1)], gat(64 * (q1 - q0)))

    def ytoks(h, q1=2):
        return ["Y%d_%d" % (h, i) for i in range(2 * q1)] + ["Yz%d" % h]

    def big(step, q, last, win, wtok, ybank, yw, mw, sw=None):
        h, c = q // 2, q % 2
        px_, kb, y0, m0_ = "pX%d" % c, "pK%d" % h, PAD + 1024 * c, 1024 * q
        yt = ["Y%d_%d" % (h, 2 * c + i) for i in range(2)]
        for i in range(2):
            o, src = Y[h][:, y0 + 512 * i:y0 + 512 * i + 512], win.indirect(T.Lu[:, 64 * q + 32 * i:64 * q + 32 * i + 32])
            if i < VSHARE[step][q]:
                cp(o, src, wtok + ["Lu%d" % q], [yt[i]], gat(512))
                if step in INLINE:
                    in_line("mins")
            else:
                act(o, src, wtok + ["Lu%d" % q], [yt[i]], c=gat(512))
                in_line("gathers")
                if (step, q, i) in AFTER:
                    behind(AFTER[step, q, i])
        if ybank is not None:
            if c == 1:
                mm([(T[ybank][:, 0:HN], T.SX[0:HA, HN * h:HN * h + HN], T[sw][0:HA, :], False, False)], ["SX%d" % h, sw], [ybank], 256)
            for i in range(2):
                mm([(T[ybank][:, 0:HN], wr_(T[yw], r), Y[h][:, PAD + 128 * r:PAD + 128 * r + 128], False, ybank != kb and r == 15)
                    for r in range(8 * c + 4 * i, 8 * c + 4 * i + 4)], [yt[i], yw], [ybank], 256)

        def add(r0, r1, toks):
            mm([(T[kb][:, 0:HN], wr_(T[mw], r), T.MN[:, 2048 * h + 128 * r:2048 * h + 128 * r + 128], False, r == 15)
                for r in range(8 * c + r0, 8 * c + r1)], toks + [mw], [kb], 64 * (r1 - r0))
        if q in WIDE[step]:
            for j in range(4):
                bk, a = ("pU%d" % h, px_)[j // 2], 256 * j
                tt(T.MN[:, m0_ + a:m0_ + a + 256], Y[h][:, y0 + a:y0 + a + 256], T[bk][:, a % 512:a % 512 + 256], ALU.min,
                   [yt[j // 2], bk], ["M%d_%d" % (q, j)], 256)
                in_line("mins")
                add(2 * j, 2 * j + 2, ["M%d_%d" % (q, j)])
            return
        for j in range(16 // MG):
            def fn(j=j):
                for k in range(MG * j, MG * j + MG):
                    i = V.tensor_tensor(T.MN[:, m0_ + k:m0_ + 1024:16], Y[h][:, y0 + k:y0 + 1024:16], T[px_][:, 0:64], ALU.min)
                return i
            record("V", fn, yt + [px_], ["M%d_%d" % (q, j)], 64 * MG)
            in_line("mins")
        add(0, 8, ["M%d_%d" % (q, j) for j in range(16 // MG)])

    def best(h, src, R, a=0):
        scan(T.SC[:, a + HN * h:a + HN * h + HN], full("m0"), src, ALU.mult, ALU.max, R + ["m0"], ["SC%d_%d" % (h, a)])

    def offsets(out, c0, n, tok, keys, ktok, w1=[], w2=[], shift=0):
        ts(T.oj[:, c0:c0 + n], keys, 4095 << shift, shift, ALU.bitwise_and, ALU.arith_shift_right, [ktok], ["oj" + tok] + w1)
        ts(out, T.oj[:, c0:c0 + n], -1.0, 4095.0, ALU.mult, ALU.add, ["oj" + tok], ["off" + tok] + w2)

    def write(h, rec, old, rtok, oldf, oftok, obias, newname, ntok, npb, nptok, c0, key):
        r_, hh = T["pR%d" % h], "%d" % h
        xb, cb = ("pU0", "pU0") if h == 0 else ("pX0", "pX1")
        x_, u_, oh = T[xb], T[cb][:, 256:384], hf(T.oh, h)
        mm(group(x_[:, c0:c0 + 128], [(I1, rec), (I1, old), (I1n, npb)])
           + group(x_[:, 384:512], [const(2), (GO, newname), (full("I8k"), oh), (I1, npb)]),
           rtok + [nptok, ntok, "oh" + hh, "I1n", "I8k", "GO", "one", "CK"], [xb], 448)
        act(hf(T.a1, h), x_[:, c0:c0 + 128], [xb], ["a1" + hh], bias=M1, scale=HALF)
        act(hf(T.Hs, h), hf(T.a1, h), ["a1" + hh], ["Hs" + hh], bias=-M1)
        tt(hf(T.Q, h), hf(T.Hs, h), x_[:, 384:512], ALU.max, ["Hs" + hh, xb], ["Q" + hh], HN)
        mm(group(u_, [(full("I8n"), oh), (I1, npb)], stop=False), [nptok, "oh" + hh, "I8n"], [cb])
        mm(group(u_, [(full("I32"), oldf)], start=False), [oftok, "I32"], [cb], 256)
        act(hf(T.Cs, h), u_, [cb], ["Cs" + hh], bias=obias)
        mm(group(r_[:, 128:256], [(I1, NM1), (I1n, hf(T.kr, h))], stop=False), ["NM", "I1n", "kr" + hh], ["pR" + hh], 128)
        for j in range(len(CUTS) - 1):
            cols, etok = range(CUTS[j], CUTS[j + 1]), "E%d_%d" % (h, j)

            def fn(cols=cols):
                for a in cols:
                    i = V.tensor_scalar(T.E[:, HA * h + a, 0:HN - 16 * a], hf(T.kr, h)[:, 16 * a:HN], key(HA * h + a), 0.0,
                                        ALU.add, ALU.is_equal)
                return i
            record("V", fn, ["kr" + hh, "s1" + hh], [etok], 64 * len(cols))
            mm([(r_[:, 144 + 16 * a:256], full("G8n"), T.E[:, HA * h + a, 16:HN - 16 * a], False, False) for a in cols if a < HA - 1]
               + [(r_[:, 128 + 16 * CUTS[j]:128 + 16 * CUTS[j + 1]], full("TRI"), T.E[:, HA * h + CUTS[j]:HA * h + CUTS[j + 1], 0:16],
                   False, j == len(CUTS) - 2)], [etok, "G8n", "TRI"], ["pR" + hh], 40 * len(cols) + 32)
        scan(hf(T.s2, h), hf(T.RR, h), r_[:, 128:256], ALU.min, ALU.max, ["RR", "pR" + hh], ["s2" + hh])
        ts(hl(T.fo, h), dg(T.s2, h), -1.0, 2048.0, ALU.mult, ALU.add, ["s2" + hh], ["fo" + hh])

    def scatter(h):
        hh = "%d" % h
        tt(T.TB[:, 0:TBW].indirect(hl(T.fo, h)), hf(T.Cs, h), hf(T.Q, h), ALU.max, ["fo" + hh, "Cs" + hh, "Q" + hh],
           ["TB", "TBc", "TBo", "TBd"], 60 + 3.5 * HN)

    def key_scan(a):
        return T.s1[:, 16 * a + 15:16 * a + 16]

    def key_list(a):
        return T.kl[:, a:a + 1]

    TBC, late = ["TBc", "TBo"], []

    for t in range(RO):
        u = t + 1
        cwin, ctok = (T.CE[:, :], ["CE"]) if t == 0 else (cells, TBC)
        pwin, ptok = (T.PXB[:, 0:W], ["PXB"]) if t == 0 else (T.TB[:, 0:W], ["TB"])
        zt = ["z0_%d" % t, "z1_%d" % t]
        plus[0] = BON["z"] if t else BON["z0"]
        if t == 0:
            send("y", t, hf(T.xs, 3), hf(T.xr, 3), zt)
            send("z", t, hf(T.xs, 2), hf(T.xr, 2), zt)
        else:
            send("z", t, sl(T.xs, t, XW, K, XW), sl(T.xr, t, XW, K, XW), zt)
        plus[0] = 0
        for q0, q1 in XPARTS:
            h, qq, a, b = q0 // 2, "q%d" % q0, 64 * q0, 64 * q1
            kb, c0, c1 = "pK%d" % h, a - HN * h, b - HN * h
            key_start(kb, "I1", c0, c1)
            names(q0, q1, cwin, ctok, t, NA[0] and t and h)
            for q in range(q0, q1):
                spread(0, q, sl(T.xs, t, XW, K + a, K + b), zt[h])
                big(0, q, q == q1 - 1, pwin, ptok, None, None, "W4")
            plus[0] = BON["x"]
            scan(T.SC[:, a:b], T.m0[:, 0:b - a], T[kb][:, c0:c1], ALU.mult, ALU.max, [kb, "m0"], ["SC%d_0" % h], b - a)
            offsets(T.off[:, 4 * q0:4 * q1], 4 * q0, 4 * (q1 - q0), qq, T.SC[:, a + 15:b:16], "SC%d_0" % h, ["oj%d" % h], ["off%d" % h])
            (cp if XV[h] else act)(sl(T.xs, t, XW, a, b), Y[h][:, 0:PAD + 16 * c1].indirect(T.off[:, 4 * q0:4 * q1]),
                                   ytoks(h, q1 - 2 * h) + ["off" + qq], ["xs" + qq], c=gat(b - a))
            if ZJOIN and q1 == 4:
                send("x%d" % q0, t, sl(T.xs, t, XW, a, XW), sl(T.xr, t, XW, a, XW), ["xs" + qq] + zt)
                wrote["rz_%d" % t] = wrote["rx%d_%d" % (q0, t)]
            else:
                send("x%d" % q0, t, sl(T.xs, t, XW, a, b), sl(T.xr, t, XW, a, b), ["xs" + qq])
            plus[0] = 0
            for q in range(q0, q1):
                wrote["rx%d_%d" % (q, t)] = wrote["rx%d_%d" % (q0, t)]
        plus[0] = BON["lf"]
        act(full("Lf"), cells.indirect(sl(T.bA, t, 16)), TBC + ["bA%d" % t], ["Lf"], bias=-2048.0, c=gat(K))
        plus[0] = 0
        tt(sl(T.ns, t), ohw.indirect(full("off")), full("Lf"), ALU.mult,
           ["OH", "OHz", "Lf"] + ["offq%d" % q0 for q0, q1 in XPARTS] + ["off0", "off1"], ["ns"], gat(K))
        send("n", t, sl(T.ns, t), sl(T.nr, t), ["ns"])
        if t == 0:
            for q in range(8):
                o, i = T.TB[:, 512 * q:512 * q + 512], T.PXB[:, 512 * q:512 * q + 512]
                (cp if q < WV else act)(o, i, ["PXB"], ["TB%d" % q], c=512)
        ptok = ["TB"] + (["TB%d" % q for q in range(8)] if t == 0 else [])
        rz = ("rz_%d" % t, "rz_%d" % t if t else "ry_0")
        na, par, ntx = counts(T.fs, t)
        na0, par0, ntx0 = counts(T.fr, t - 1 if t else RO)
        was = ["rf1_%d" % (t - 1)] if t else ["first0", "first1", "first2"]
        if CA:
            mm(group(T.pR1[:, 384:400], [(I1, na0), (I1, ntx0)]) + group(T.pR1[:, 400:416], [(I1, par0), (I1, ntx0)]),
               was + ["I1"], ["pR1"])
            act(na, T.pR1[:, 384:400], ["pR1"], ["za%d" % t], c=64)
            act(par, T.pR1[:, 400:416], ["pR1"], ["zb%d" % t], f=AF.Abs, bias=-1.0, c=64)
            act(full("thr"), par, ["zb%d" % t], ["thr"], scale=2.0, bias=-12.0, c=64)
        else:
            tt(na, na0, ntx0, ALU.add, was, ["za%d" % t])
            tt(par, par0, ntx0, ALU.is_equal, was, ["zb%d" % t])
            ts(full("thr"), par, 2.0, -12.0, ALU.mult, ALU.add, ["zb%d" % t], ["thr"])
        rxs = ["rx%d_%d" % (q, t) for q in range(4)]
        for q0, q1 in XPARTS:
            h, qq, a, b = q0 // 2, "q%d" % q0, 4 * q0, 4 * q1
            hh = "%d" % h
            pu = T["pU" + hh]
            plus[0] = BON["b"]
            xq = hf(T.xr, h, t, XW)
            mm(group(pu[:, a:b], [const(4, 2, HA)]
                     + [(wr_(T.Wu2, i), xq[:, 16 * (i % 8) + i // 8:16 * (i % 8) + 16:2]) for i in range(16)]),
               [rxs[q0], "Wu2", "one", "CK"], ["pU" + hh], 544)
            behind("offq%d" % XPARTS[-1][0])
            ts(T.bf[:, a:b], pu[:, a:b], 2.0 ** 34 - 1024, 2.0 ** 34, ALU.add, ALU.subtract, ["pU" + hh], ["bf" + qq])
            tt(T.bB[:, 16 * u + a:16 * u + b], pu[:, a:b], T.bf[:, a:b], ALU.subtract, ["pU" + hh, "bf" + qq],
               ["bB%d_%d" % (q, u) for q in range(q0, q1)])
            names(q0, q1, cells, TBC, u, NA[1] and h)
            plus[0] = 0
            if q0 % 2 == 0:
                key_start("pK" + hh, "I2")
                key_start("pR" + hh, "I1")
            if q1 % 2 == 0:
                sums(h, hf(T.xr, h, t, XW), rxs[2 * h:2 * h + 2])
            if q1 == 4:
                mm(group(pu[:, 16:32], [(wr_(T.Wu, r), sl(T.xr, t, XW)[:, r:K:16]) for r in range(16)]), rxs + ["Wu"], ["pU1"], 512)
                cp(T.bi[:, 16:32], pu[:, 16:32], ["pU1"], ["biA"])
                ts(T.bj[:, 16:32], T.bi[:, 16:32], CELLS - 1, None, ALU.bitwise_and, None, ["biA"], ["bjA"])
                ts(sl(T.bA, u, 16), T.bj[:, 16:32], 2.0, None, ALU.mult, None, ["bjA"], ["bA%d" % u])
                ts(full("bC"), T.bj[:, 16:32], 2.0, 1.0, ALU.mult, ALU.add, ["bjA"], ["bC"])
                if LIST:
                    ts(full("ckl"), T.bj[:, 16:32], -2.0, -2048.0, ALU.mult, ALU.add, ["bjA"], ["ckl"])
                act(full("Lf"), cells.indirect(sl(T.bA, u, 16)), TBC + ["bA%d" % u], ["Lf"], bias=-2048.0, c=gat(K))
                act(full("ck"), cells.indirect(full("bC")), TBC + ["bC"], ["ck"], c=gat(K))
            for q in range(q0, q1):
                spread(1, q, xq, rxs[q])
                big(1, q, q % 2, T.TB[:, 0:W], ptok, "pR" + hh, "W4", "W8", "DA")
            if q1 % 2 == 0:
                act(hf(T.A3, h), T["pR" + hh][:, 0:HN], ["pR" + hh], ["A3" + hh])
        for h in range(2):
            hh = "%d" % h
            rx, pu, pk = rxs[2 * h:2 * h + 2], T["pU" + hh], T["pK" + hh]
            x, yw, live, MS = hf(T.xr, h, t, XW), Y[h][:, 0:YW], hf(T.live, h), hf(T.MS, h)
            sj, sm, cj, cm = K + HN * h, K + HN * h + HN, 24 * h, 8 + 8 * h
            plus[0] = BON["f"]
            tt(hf(T.nk, h), pk[:, 0:HN], hf(T.A3, h), ALU.subtract, ["pK" + hh, "A3" + hh], ["nk" + hh], HN)
            best(h, hf(T.nk, h), ["nk" + hh], sj)
            act(hf(T.sg, h), hf(T.nk, h), ["nk" + hh], ["sg" + hh], f=AF.Sign, bias=1.0 - 4096.0 * (4080 - TH1 + 1))
            scan(hf(T.cs, h), full("m0"), hf(T.sg, h), ALU.mult, ALU.add, ["m0", "sg" + hh], ["cs" + hh], 64)
            zc = "zc%d_%d" % (h, t)
            tt(hl(ntx, h), dg(T.cs, h), hl(T.thr, h), ALU.is_lt, ["cs" + hh, "thr"], [zc])
            tt(hl(T.nu, h), dg(T.cs, h), hl(T.thr, h), ALU.is_lt, ["cs" + hh, "thr"], ["nu" + hh])
            act(live, T.NP[:, 0:16].indirect(hl(T.nu, h)), ["NP", "nu" + hh], ["live" + hh], c=gat(HN))
            tt(hf(T.ne, h), hf(T.SC, 2 + 2 * h).indirect(full("c15")), hf(T.nk, h), ALU.not_equal,
               ["SC%d_%d" % (h, sj), "c15", "nk" + hh], ["ne" + hh], gat(HN))
            tt(hf(T.ks, h), hf(T.ne, h), pk[:, 0:HN], ALU.mult, ["ne" + hh, "pK" + hh], ["ks" + hh], HN)
            best(h, hf(T.ks, h), ["ks" + hh], sm)
            offj, offm = T.of2[:, cj:cj + HA], T.of2[:, cm:cm + HA]
            offsets(offj, 16 + cj, HA, "j" + hh, dg(T.SC, h, sj), "SC%d_%d" % (h, sj))
            offsets(offm, 16 + cm, HA, "m" + hh, dg(T.SC, h, sm), "SC%d_%d" % (h, sm), shift=1)
            tt(hf(T.fs, h, t, MW), yw.indirect(offm), x, ALU.max, ytoks(h) + ["offm" + hh] + rx, ["fs" + hh], gat(HN))
            if h == 0:
                send("f0", t, hf(T.fs, 0, t, MW), hf(T.fr, 0, t, MW), ["fs0"])
            else:
                send("f1", t, sl(T.fs, t, MW, HN, MW), sl(T.fr, t, MW, HN, MW), ["fs1", "za%d" % t, "zb%d" % t, "zc0_%d" % t, zc])
            plus[0] = BON["t0"] * (1 - h)
            tt(MS, ohw.indirect(offj), hf(T.Lf, h), ALU.mult, ["OH", "OHz", "offj" + hh, "Lf"], ["MS" + hh], gat(HN))
            act(hf(T.oh, h), ohw.indirect(offj), ["OH", "OHz", "offj" + hh], ["oh" + hh], c=gat(HN))
            act(hf(T.yj, h), yw.indirect(offj), ytoks(h) + ["offj" + hh], ["yj" + hh], c=gat(HN))
            pr = T["pR" + hh][:, 256:384]
            mm(group(pr, [(I1, NM1)], stop=False), ["NM"], ["pR" + hh])
            mm(group(pu[:, 0:128], [(I1, live), (GO, MS)]), ["GO", "live" + hh, "MS" + hh], ["pU" + hh])
            if LIST:
                mm(group(pr, [(I1n, live), (GOn, MS)], start=False), ["GOn", "live" + hh, "MS" + hh], ["pR" + hh])
                scan(hf(T.s1, h), hf(T.RR, h), pr, ALU.min, ALU.max, ["RR", "pR" + hh], ["sa" + hh, "s1" + hh])
                tt(hf(T.kr, h), pu[:, 0:128], hf(T.ck, h), ALU.min, ["pU" + hh, "ck"], ["kr" + hh], HN)
                tt(hl(T.kl, h), dg(T.s1, h), hl(T.ckl, h), ALU.max, ["sa" + hh, "ckl"], ["s1" + hh])
            else:
                tt(hf(T.kr, h), pu[:, 0:128], hf(T.ck, h), ALU.min, ["pU" + hh, "ck"], ["kr" + hh], HN)
                mm(group(pr, [(I1n, hf(T.kr, h))], start=False), ["I1n", "kr" + hh], ["pR" + hh])
                scan(hf(T.s1, h), hf(T.RR, h), pr, ALU.min, ALU.max, ["RR", "pR" + hh], ["s1" + hh])
            if h == 1:
                plus[0] = BON["m"]
                tt(sl(T.ms, t), ohw.indirect(T.of2[:, 8:24]), full("Lf"), ALU.mult,
                   ["OH", "OHz", "offm0", "offm1", "Lf"], ["ms"], gat(K))
                send("m", t, sl(T.ms, t), sl(T.mr, t), ["ms"])
                plus[0] = 0
            z0 = sl(T.xr, t, XW, K + HN * h, K + HN * h + HN)
            mm(group(pk[:, 256:384], [(I1, z0), (I1n, live)]) + group(pk[:, 384:512], [(I1, hf(T.yj, h)), (I1n, live)]),
               [rz[h], "live" + hh, "yj" + hh], ["pK" + hh])
            act(T.E12[:, K * h:K * h + K], pk[:, 256:512], ["pK" + hh], ["E12" + hh], f=AF.Relu, c=K)
            write(h, x, hf(T.yj, h), rx + ["yj" + hh], hf(T.Lf, h), "Lf", 2048.0 - 8192.0, hf(T.nr, h, t), "rn_%d" % t,
                  live, "live" + hh, 128, key_list if LIST else key_scan)
            scatter(h)
        rm = "rm_%d" % t
        for h in range(2):
            hh = "%d" % h
            rf, f = "rf%d_%d" % (h, t), hf(T.fr, h, t, MW)
            pu, pk, pr = T["pU" + hh], T["pK" + hh], T["pR" + hh]
            plus[0] = BON["p"]
            if PV[h]:
                mm(group(pk[:, 128:256], [const(5, 2)], stop=False) + reorder2(pk[:, 128:256], full("KB"), f, True),
                   [rf, "KB", "one", "CK"], ["pK" + hh], 320)
                behind("fs1")
                ts(hf(T.md, h), pk[:, 128:256], 2.0 ** 35 - 2048, 2.0 ** 35, ALU.add, ALU.subtract, ["pK" + hh], ["md" + hh], HN)
                tt(hf(T.Lu, h), pk[:, 128:256], hf(T.md, h), ALU.subtract, ["pK" + hh, "md" + hh],
                   ["Lu%d" % (2 * h), "Lu%d" % (2 * h + 1)], HN)
                plus[0] = 0
                mm(group(pu[:, 256:384], [const(0, 2), (full("KB"), f)]), [rf, "KB", "one", "CK"], ["pU" + hh])
                behind("fs1")
            else:
                mm(group(pu[:, 256:384], [const(0, 2), (full("KB"), f)]) + group(pk[:, 128:256], [const(0)], stop=False)
                   + reorder2(pk[:, 128:256], full("KB"), f, False), [rf, "KB", "one", "CK"], ["pU" + hh, "pK" + hh], 448)
                behind("fs1")
            if HV[h]:
                ts(hf(T.hi, h), pu[:, 256:384], M4096, M4096, ALU.add, ALU.subtract, ["pU" + hh], ["hi" + hh], HN)
            else:
                act(hf(T.a2, h), pu[:, 256:384], ["pU" + hh], ["a2" + hh], bias=M4096)
                act(hf(T.hi, h), hf(T.a2, h), ["a2" + hh], ["hi" + hh], bias=-M4096)
            if not PV[h]:
                mm(reorder2(pk[:, 128:256], I1n, hf(T.hi, h), True), ["hi" + hh, "I1n"], ["pK" + hh], 256)
                ts(hf(T.Lu, h), pk[:, 128:256], 2048.0, None, ALU.add, None, ["pK" + hh], ["Lu%d" % (2 * h), "Lu%d" % (2 * h + 1)], HN)
            plus[0] = 0
            sums(h, f, [rf])
            key_start("pK" + hh, "I1")
            mm(group(pu[:, 384:512], [const(1, 2), (full("KB"), f)]), [rf, "KB"], ["pU" + hh])
            act(hf(T.sel, h), pu[:, 384:512], ["pU" + hh], ["sel" + hh], bias=M1024)
            act(hf(T.md, h), hf(T.sel, h), ["sel" + hh], ["md" + hh], bias=-M1024)
            mm(group(pr[:, 256:384], [(full("KB2"), f), (full("J32"), hf(T.md, h))]), [rf, "KB2", "J32", "md" + hh], ["pR" + hh], 320)
            act(hf(T.Lcc, h), pr[:, 256:384], ["pR" + hh], ["Lcc" + hh], bias=2048.0)
            for q in (2 * h, 2 * h + 1):
                spread(2, q, f, rf)
                big(2, q, q % 2, T.TB[:, 0:W], ["TB"], "pK" + hh, "W4n", "W8", "DAn")
        if CA:
            act(full("dk"), counts(T.fr, t)[2], ["rf1_%d" % t], ["dk"], scale=-TOP, bias=TOP, c=64)
        else:
            ts(full("dk"), counts(T.fr, t)[2], -TOP, TOP, ALU.mult, ALU.add, ["rf1_%d" % t], ["dk"])
        for h in range(2):
            hh = "%d" % h
            rf, f = "rf%d_%d" % (h, t), hf(T.fr, h, t, MW)
            pu, pk = T["pU" + hh], T["pK" + hh]
            offj, npb, oh, w_, MS = hl(T.off, h), hf(T.np3, h), hf(T.oh, h), hf(T.ws, h, t), hf(T.MS, h)
            otok = ["offq%d" % q0 for q0, q1 in XPARTS if q0 // 2 == h]
            plus[0] = BON["w"]
            best(h, pk[:, 0:HN], ["pK" + hh])
            ts(hl(T.nu, h), dg(T.SC, h), 4096.0 * (4080 - TH2 + 1), None, ALU.is_lt, None, ["SC%d_0" % h], ["nu" + hh])
            tt(hl(T.oi, h), dg(T.SC, h), hl(T.dk, h), ALU.max, ["SC%d_0" % h, "dk"], ["oi" + hh])
            offsets(offj, HA * h, HA, hh, hl(T.oi, h), "oi" + hh, [], otok)
            act(npb, T.NP[:, 0:16].indirect(hl(T.nu, h)), ["NP", "nu" + hh], ["np" + hh], c=gat(HN))
            act(w_, Y[h][:, 0:YW].indirect(offj), ytoks(h) + ["off" + hh], ["ws" + hh], c=gat(HN))
            send("w" + hh, t, w_, hf(T.wr, h, t), ["ws" + hh])
            plus[0] = BON["t0"] * (1 - h)
            act(oh, ohw.indirect(offj), ["OH", "OHz", "off" + hh], ["oh" + hh], c=gat(HN))
            mm(group(pu[:, 0:128], [const(0), (full("KB"), f), (I1n, hf(T.hi, h))], stop=False), [rf, "hi" + hh], ["pU" + hh])
            mm(group(pu[:, 0:128], [(I1, npb)], start=False), ["np" + hh], ["pU" + hh])
            if h < PSEL:
                tt(pu[:, 0:128], pu[:, 0:128], hf(T.Lcc, h), ALU.min, ["Lcc" + hh], ["pU" + hh], HN)
                tt(MS, oh, pu[:, 0:128], ALU.mult, ["oh" + hh, "pU" + hh], ["MS" + hh], HN)
            else:
                tt(hf(T.sel, h), pu[:, 0:128], hf(T.Lcc, h), ALU.min, ["pU" + hh, "Lcc" + hh], ["sel" + hh], HN)
                tt(MS, ohw.indirect(offj), hf(T.sel, h), ALU.mult, ["OH", "OHz", "off" + hh, "sel" + hh], ["MS" + hh], gat(HN))
            pr = T["pR" + hh][:, 0:128]
            mm(group(pr, [(I1, NM1), const(3), (full("G8k"), oh)], stop=False), ["oh" + hh, "NM", "G8k"], ["pR" + hh])
            mm(group(pu[:, 128:256], [(full("G8n"), oh)], stop=False), ["oh" + hh, "G8n"], ["pU" + hh])
            mm(group(pu[:, 128:256], [(GO, MS)], start=False), ["MS" + hh], ["pU" + hh])
            mm(group(pr, [(GOn, MS)], start=False), ["MS" + hh, "GOn"], ["pR" + hh])
            ts(hf(T.kr, h), pu[:, 128:256], 8192.0, None, ALU.add, None, ["pU" + hh], ["kr" + hh], HN)
            scan(hf(T.s1, h), hf(T.RR, h), pr, ALU.min, ALU.max, ["RR", "pR" + hh], ["s1" + hh])
            plus[0] += BON["k"]
            ts(hl(T.ku, h), dg(T.s1, h), -1.0, 2048.0, ALU.mult, ALU.add, ["s1" + hh], ["ku" + hh])
            plus[0] -= BON["k"]
            act(hf(T.OLD, h), T.TB[:, 0:TBW].indirect(hl(T.ku, h)), ["TB", "TBc", "TBo", "TBd", "ku" + hh], ["OLD" + hh], c=gat(HN))
            write(h, f, w_, [rf, "ws" + hh], hf(T.OLD, h), "OLD" + hh, -8192.0, hf(T.mr, h, t), rm, npb, "np" + hh, 0, key_scan)
            if h == 1:
                scatter(0)
                scatter(1)
            plus[0] = 0
            e = T.E12[:, K * h:K * h + HN], T.E12[:, K * h + HN:K * h + K]
            mm(group(pk[:, 128:256], [(I1, sl(T.xr, t, XW, K + HN * h, K + HN * h + HN)), (I1, e[0]), (full("I2n"), e[1])], stop=False),
               [rz[h], "E12" + hh, "I2n"], ["pK" + hh])
            mm(group(pk[:, 128:256], [(I1, hf(T.wr, h, t))], start=False), ["rw%d_%d" % (h, t)], ["pK" + hh])
            late.append(len(ops) - 1)
            if h == 1 and GUARD:
                ops[late[-2]]["line"] = [wrote["ws1"]]
            act(hf(T.a2, h), pk[:, 128:256], ["pK" + hh], ["a2" + hh], bias=M1, scale=HALF)
            act(sl(T.xs, u, XW, K + HN * h, K + HN * h + HN), hf(T.a2, h), ["a2" + hh], ["z%d_%d" % (h, u)], f=AF.Abs, bias=-M1)

    store("G", T.yx[:, :], T.TB[:, 0:W], ["TB"], 6000)
    for i, fn in enumerate((cp, act)):
        fn(T.YC[:, 512 * i:512 * i + 512], T.TB[:, W + 1024 * i:W + 1024 * i + 1024:2], ["TBc"], ["YC%d" % i], c=512)
    store("S", T.yc[:, :], full("YC"), ["YC0", "YC1"], 4000)
    tt(full("t1"), na, ntx, ALU.add, ["za%d" % t, "zc0_%d" % t, "zc1_%d" % t], ["t1"])
    for h in range(2):
        cp(hl(T.yvf, 1 - h), hl(T.bj, 2 + h), ["bjA"], ["yvf%d" % h])
        ts(hl(T.au, 1 - h), hl(T.t1, h), -1.0, float(RO), ALU.mult, ALU.add, ["t1"], ["au%d" % h])
        store("S", hf(T.yz, 1 - h), hf(T.xs, 2 + h, RO, XW), ["z%d_%d" % (h, RO)])
    cp(full("ar"), full("ioc").indirect(full("au")), ["au0", "au1", "ioc"], ["ar"], gat(K))
    store("S", T.yv[:, :], full("yvf"), ["yvf0", "yvf1"])
    for q in range(8):
        store("S", T.ya[q:q + 1, :], T.ar[16 * q:16 * q + 1, :], ["ar"])

    n = len(ops)
    after, before, rest = [[] for _ in ops], [[] for _ in ops], [0.0] * n
    for i, o in enumerate(ops):
        for d, hop in [(d, 0 if o["e"] == ops[d]["e"] == "P" else HOP) for d in o["pre"]] + [(d, 0) for d in o.get("line", [])]:
            after[d].append((i, hop))
            before[i].append((d, hop))
    for i in range(n - 1, -1, -1):
        rest[i] = ops[i]["cost"] + max([hop + rest[j] for j, hop in after[i]] + [0.0])

    def plan(after, before, rest, look, sign=1):
        missing = [len(b) for b in before]
        ready, ends, free, order = [0.0] * n, [0.0] * n, {e: 0.0 for e in Q}, []
        pool = [i for i in range(n) if not missing[i]]

        def begin(i):
            return max(ready[i], free.get(ops[i]["e"], 0.0))

        def rank_(i):
            return rest[i] + ops[i]["plus"] * sign
        while pool:
            i = min(pool, key=lambda j: (begin(j), -rank_(j)))
            soon = begin(i) + ops[i]["cost"] * look
            i = max([j for j in pool if ops[j]["e"] == ops[i]["e"] and begin(j) <= soon], key=rank_)
            ends[i] = begin(i) + ops[i]["cost"]
            if ops[i]["e"] is not None:
                free[ops[i]["e"]] = ends[i]
            pool.remove(i)
            order.append(i)
            for j, hop in after[i]:
                ready[j] = max(ready[j], ends[i] + hop)
                missing[j] -= 1
                if not missing[j]:
                    pool.append(j)
        return max(ends), order, ends

    plans = []
    for look in LOOKS:
        plans.append(plan(after, before, rest, look))
        for _ in range(PASSES):
            plans.append(plan(after, before, plan(before, after, plans[-1][2], look, -1)[2], look))
    order = min(plans, key=lambda p: p[0])[1]

    cnt = {"cV": 0, "cA": 0, "cP": 0, "cG": 0, "sent": 0, "outs": 0, "outg": 0}
    seen = {e: {} for e in Q}

    def need(e, dep):
        if seen[e].get(dep[0], 0) < dep[1]:
            Q[e].wait_ge(T.sem[dep[0]], dep[1])
            seen[e][dep[0]] = dep[1]

    for i in order:
        o = ops[i]
        e = o["e"]
        if e is None:
            continue
        ds = {}
        for d in o["pre"]:
            s, v = ops[d]["sem"]
            ds[s] = max(ds.get(s, 0), v)
        for s in sorted(ds):
            if not (e == "P" and s == "cP"):
                need(e, (s, ds[s]))
        if o["kind"] == "op":
            o["fn"]().then_inc(T.sem["c" + e], 1)
            cnt["c" + e] += 1
            o["sem"] = ("c" + e, cnt["c" + e])
        else:
            o["fn"]()
            if o["kind"] == "send":
                cnt["sent"] += o["sem"]
            elif o["kind"] == "out":
                cnt["outg" if e == "G" else "outs"] += 16
    for s in ("cV", "cA", "cP", "cG", "sent", "outs", "outg"):
        need("G", (s, cnt[s]))
